import numpy as np, ml_dtypes
CORES = [9,25,41,57]
N = 4
BF = ml_dtypes.bfloat16
V, A, M, RO, BN = 4096, 2048, 256, 4, 3
HOPS = [1, 2, 3, 1]
def parts(rng):
    x = rng.integers(0, 256, (N, 8, 16, V)); sb = rng.integers(0, V, (N, 8, 16, A)); la = rng.integers(0, A, (N, 8, 16, M)); lw = rng.integers(0, A, (N, 8, 16, M))
    z = rng.integers(0, 256, (N, 8, 16, M)); b = rng.integers(0, 16, (N, 8, M)); th = rng.integers(1420, 1680, (N, 8, 1)) - 60 * (BN - 3)
    return x, sb, la, lw, z, b, th
def pack(x, sb, la, lw, z, b, th):
    return {"xs": x.reshape(N, 128, V).astype(np.float32).astype(BF), "sb": np.ascontiguousarray(sb.reshape(N, 128, A)).astype(np.int32),
            "la": np.ascontiguousarray(la.reshape(N, 128, M)).astype(np.int32), "lw": np.ascontiguousarray(lw.reshape(N, 128, M)).astype(np.int32),
            "z0": z.reshape(N, 128, M).astype(np.float32).astype(BF), "b0": b.astype(np.int32), "th": th.astype(np.int32)}
def setup_inputs(rng):
    return pack(*parts(rng))
def setup_inputs_spread(rng):
    x, sb, la, lw, z, b, th = parts(rng)
    x = (np.exp2(8 * rng.random((N, 8, 1, V))) * rng.random((N, 8, 16, V))).astype(np.int64)
    z = (np.exp2(8 * rng.random((N, 8, 1, M))) * rng.random((N, 8, 16, M))).astype(np.int64)
    th = np.minimum(np.exp2(4 + 8 * rng.random((N, 8, 1))).astype(np.int64), 4080)
    sb = (V * rng.random((N, 8, 16, A)) ** 2).astype(np.int64); la = (A * rng.random((N, 8, 16, M)) ** 2).astype(np.int64)
    lw = A - 1 - (A * rng.random((N, 8, 16, M)) ** 3).astype(np.int64)
    return pack(np.minimum(x, 255), np.minimum(sb, V - 1), np.minimum(la, A - 1), np.maximum(lw, 0), np.minimum(z, 255), b, th)
def edge(rng, hi, shape):
    return np.where(rng.random(shape) < 0.7, hi * rng.integers(0, 2, shape), rng.integers(0, hi + 1, shape))
def setup_inputs_ends(rng):
    kind = rng.integers(0, 4, (N, 8, 1, V)); x = 255 * np.where(kind == 0, 0, np.where(kind < 3, 1, rng.integers(0, 2, (N, 8, 16, V))))
    kind = rng.integers(0, 4, (N, 8, 1, M)); z = 255 * np.where(kind == 0, 0, np.where(kind == 1, 1, rng.integers(0, 2, (N, 8, 16, M))))
    sb = edge(rng, V - 1, (N, 8, 16, A)); la = edge(rng, A - 1, (N, 8, 16, M)); lw = edge(rng, A - 1, (N, 8, 16, M)); b = 15 * rng.integers(0, 2, (N, 8, M))
    m = rng.random((N, 8, 1, M)); la = np.where(m < 0.1, 0, np.where(m < 0.2, A - 1, la)); m = rng.random((N, 8, 1, M)); lw = np.where(m < 0.1, 0, np.where(m < 0.2, A - 1, lw))
    th = np.zeros((N, 8, 1), np.int64); th[:, :6, 0] = np.where(np.argsort(rng.random((N, 6)), axis=1) < 3, 1, 4080); th[:, 6] = 1; th[:, 7] = 4080
    x[:, 6:, :, 0] = 0; x[:, 6:, :, V - 1] = 255; x[:, 6:, :, A - 1] = 255; sb[:, 6:, :, A - 1] = V - 1
    for c in (0, 1, M - 2, M - 1):
        la[:, 6:, :, c] = A - 1; lw[:, 6:, :, c] = (A - 1) * (c % 2); z[:, 6, :, c] = 255; z[:, 7, :, c] = 0
    return pack(x, sb, la, lw, z, b, th)
def setup_inputs_corners(rng):
    x, sb, la, lw, z, b, th = parts(rng); odd = np.arange(V) & 1
    th[:, 0] = 1; b[:, 0] = 0
    th[:, 1] = 4080; b[:, 1] = 15
    x[:, 2] = 85 * rng.integers(0, 4, (N, 1, V)); z[:, 2] = 85 * rng.integers(0, 4, (N, 1, M)); th[:, 2] = rng.choice(np.array([1360, 1361, 2720]), (N, 1)); th[0, 2] = 1360; th[N - 1, 2] = 2720
    sb[:, 3] = sb[:, 3, :1]
    la[:, 4] = la[:, 4, :1]; lw[:, 4] = la[:, 4]; z[:, 4] = 255 * rng.integers(0, 2, (N, 1, M))
    x[:, 5] = np.where(odd == 0, 255, 0); th[:, 5, 0] = 3072 + (np.arange(N) & 1)
    n = rng.choice(np.array([0, BN - 1, BN, BN + 1, 16]), (N, 1, A))
    sb[:, 5] = 2 * rng.integers(0, V // 2, (N, 16, A)) + (np.argsort(rng.random((N, 16, A)), axis=1) >= n)
    la[:, 5] = 2 * rng.integers(0, A // 2, (N, 16, M)) + (rng.random((N, 16, M)) < 0.125)
    x[:, 6] = np.where(odd == 0, rng.integers(0, 8, (N, 16, V)), rng.integers(248, 256, (N, 16, V))); th[:, 6] = 40
    sb[:, 6] = 2 * rng.integers(0, V // 2, (N, 16, A)); la[:, 6] = 2 * rng.integers(0, A // 2, (N, 16, M)) + 1
    la[:, 7] = rng.choice(np.array([0, A - 1, A // 2]), (N, 16, M)); lw[:, 7] = rng.choice(np.array([0, A - 1, A // 2 + 1, 1]), (N, 16, M))
    sb[:, 7] = rng.choice(np.array([0, V - 1, 1, V // 2]), (N, 16, A)); sb[:, 7, :8] = np.arange(A)
    return pack(x, sb, la, lw, z, b, th)
def setup_inputs_crowd(rng):
    x, sb, la, lw, z, b, th = parts(rng); q = np.arange(V - 20, V - 4)
    o = np.arange(V) & 3; turn = ((np.arange(16)[None, :] + np.arange(N)[:, None]) & 15) < BN
    x[:, 3] = np.where(o == 0, x[:, 3], np.where(o == 1, rng.integers(110, 128, (N, 16, V)), np.where(o == 2, rng.integers(0, 41, (N, 16, V)), rng.integers(250, 256, (N, 16, V)))))
    sb[:, 3] = np.where(turn[:, :, None] & (o[:A] == 1), 4 * rng.integers(0, A // 4 - 5, (N, 16, A)) + 3, 4 * rng.integers(0, V // 4 - 5, (N, 16, A)) + 2)
    x[..., 0] = 0; x[..., A - 1] = 255; x[..., q] = 255; sb[..., A - 1] = q
    hot = np.zeros((8, M), bool); hot[1, M - 1] = True; hot[2] = True; hot[3] = True; hot[5] = rng.random(M) < 0.5; hot[6, M - 1] = True; hot[7, :M - 1] = True
    for e in (2, 4, 6):
        la[:, e] = la[:, e, :, :1]; lw[:, e] = lw[:, e, :, :1]; z[:, e] = z[:, e, :, :1]; b[:, e] = b[:, e, :1]
    la[:, 5] = rng.choice(np.array([1, 3, A // 2, A - 2]), (N, 16, M)); lw[:, 5] = rng.choice(np.array([0, 2, A // 2 + 1, A - 3]), (N, 16, M))
    la = np.where(np.arange(16)[None, None, :, None] == b[:, :, None, :], np.where(hot[None, :, None, :], A - 1, 0), la)
    kinds = rng.permutation(N) & 3
    for r in range(N):
        n, k = ((1, 2), (3, 1), (0, 3), (2, 2))[int(kinds[r])]; p = rng.permutation(M)
        for c, i in ((p[:n], 0), (p[n:n + k], 1)):
            la[r, 3][:, c] = 4 * rng.integers(0, A // 4 - 5, (16, c.size)) + i; lw[r, 3][:, c] = 4 * rng.integers(0, A // 4 - 5, (16, c.size)) + i
    return pack(x, sb, la, lw, z, b, th)
def setup_inputs_full(rng):
    x, sb, la, lw, z, b, th = parts(rng); n = np.arange(V) & 3; c = np.arange(M); v = np.arange(2, V, 4)
    for r in range(N):
        for e in (0, 7):
            x[r, e] = np.where(n == 3, rng.integers(250, 256, (16, V)), np.where(n == 1, rng.integers(228, 250, (16, V)), rng.integers(208, 256, (16, V))))
            x[r, e, (v >> 2) & 15, v] = rng.integers(208, 228, v.size)
            p = 4 * rng.permutation(A // 4)[:M] + 1
            sb[r, e] = 4 * rng.integers(0, V // 4, (16, A)) + 2
            sb[r, e, rng.integers(0, 16, M), p] = 4 * rng.permutation(V // 4)[:M] + 3
            la[r, e, b[r, e], c] = p; th[r, e, 0] = rng.integers(3300, 3329)
        for e in (1, 4):
            x[r, e] = np.where(n == 0, rng.integers(0, 64, (16, V)), np.where(n == 3, rng.integers(240, 256, (16, V)), rng.integers(128, 240, (16, V))))
            u = 4 * rng.permutation(A // 4)[:M] + 1; k = rng.integers(0, 16, M)
            sb[r, e] = 4 * rng.integers(0, V // 4, (16, A)) + np.where(n[:A] == 0, 0, 2)
            sb[r, e, k, u] = 4 * rng.permutation(V // 4)[:M] + 3
            la[r, e] = 4 * rng.integers(0, A // 4, (16, M)) + 2; lw[r, e] = 4 * rng.integers(0, A // 4, (16, M)) + 2
            la[r, e, b[r, e], c] = 4 * rng.integers(0, A // 4, M); la[r, e, (b[r, e] + rng.integers(1, 16, M)) & 15, c] = u
            lw[r, e, k, c] = 4 * rng.integers(0, A // 4, M)
            z[r, e] = x[r, e][:, u]; th[r, e, 0] = rng.integers(1800, 2049)
    for e in (2, 5):
        x[:, e] = rng.integers(208, 256, (N, 16, V)); z[:, e] = rng.integers(208, 256, (N, 16, M)); th[:, e] = rng.integers(3560, 3640, (N, 1))
    side = rng.integers(0, 2, (N, 1, M)); side[:, 0, 0] = 0; side[:, 0, M - 1] = 1
    x[:, 6] = 255 * (np.arange(V) & 1); z[:, 6] = 255 * side; b[:, 6] = 0
    la[:, 6] = 2 * rng.integers(0, A // 2, (N, 16, M)) + np.where(np.arange(16)[None, :, None] == 0, side, 1 - side)
    return pack(x, sb, la, lw, z, b, th)
def check_inputs(d):
    bad = []
    for k, lo, hi in (("xs", 0, 255), ("sb", 0, V - 1), ("la", 0, A - 1), ("lw", 0, A - 1), ("z0", 0, 255), ("b0", 0, 15), ("th", 1, 4080)):
        a = np.asarray(d[k]).astype(np.float64)
        if not np.all((a >= lo) & (a <= hi)): bad.append("range of " + k)
        elif not np.all(a == np.floor(a)): bad.append("whole numbers of " + k)
    return bad
def pick(x, ix):
    return np.stack([np.stack([np.take(x[r, e], ix[r, e].reshape(-1), axis=1).reshape(16, 16, M) for e in range(8)]) for r in range(N)])
def slot_of(a, k):
    return np.take_along_axis(a, k[:, :, None, :], 2)[:, :, 0]
def first(p, m):
    c = np.flatnonzero(m)
    return c[np.unique(p[c], return_index=True)[1]]
def reference(xs, sb, la, lw, z0, b0, th):
    x = xs.astype(np.float32).astype(np.int32).reshape(N, 8, 16, V); t = sb.astype(np.int64).reshape(N, 8, 16, A)
    l = la.astype(np.int64).reshape(N, 8, 16, M); w = lw.astype(np.int64).reshape(N, 8, 16, M)
    z = z0.astype(np.float32).astype(np.int32).reshape(N, 8, 16, M); b = b0.astype(np.int64).reshape(N, 8, M); h = th.astype(np.int64).reshape(N, 8, 1, 1)
    al = np.zeros((N, 8), np.int64); slot = np.arange(16)[None, None, :, None]
    for rnd in range(RO):
        hop = HOPS[rnd]
        y = pick(x, l); d = np.add.reduce(np.abs(y - z[:, :, :, None, :]), axis=2)
        j = np.argmin(np.where(slot == b[:, :, None], 9999, d), axis=2)
        yj = np.take_along_axis(y, j[:, :, None, None, :], 3)[:, :, :, 0]
        yb = np.take_along_axis(y, b[:, :, None, None, :], 3)[:, :, :, 0]
        lb = slot_of(l, b); lj = slot_of(l, j)
        s = np.take_along_axis(t, lb[:, :, None, :], 3)
        xc = np.roll(x, -hop, axis=0); hc = np.roll(h, -hop, axis=0); need = (BN + (al & 1))[:, :, None]
        g = np.add.reduce(np.minimum(pick(xc, s), yb[:, :, :, None, :]), axis=2)
        occ = np.add.reduce((g >= hc).astype(np.int64), axis=2) >= need
        place = slot_of(s, np.argmax(g, axis=2))
        new = np.maximum(np.take_along_axis(xc, place[:, :, None, :], 3) - (yb >> 2), 0)
        for r in range(N):
            for e in range(8):
                c = first(place[r, e], occ[r, e]); xc[r, e][:, place[r, e, c]] = new[r, e][:, c]
        q = pick(xc, s); g = np.add.reduce(np.minimum(q, yb[:, :, :, None, :]), axis=2)
        keep = occ & (np.add.reduce((g >= hc).astype(np.int64), axis=2) >= need); out = ~keep
        f = np.maximum.reduce(q, axis=3); xk = np.take_along_axis(xc, place[:, :, None, :], 3)
        x = np.roll(xc, hop, axis=0)
        u = np.argmin(np.add.reduce(np.abs(pick(x, w) - f[:, :, :, None, :]), axis=2), axis=2)
        wu = slot_of(w, u); su = slot_of(s, u)
        l = np.where((slot == b[:, :, None]) & out[:, :, None], wu[:, :, None], l)
        w = np.where((slot == u[:, :, None]) & out[:, :, None], lb[:, :, None], w)
        if rnd < RO - 1:
            for r in range(N):
                for e in range(8):
                    c = first(lj[r, e], out[r, e]); t[r, e][u[r, e, c], lj[r, e, c]] = su[r, e, c]
        z = np.where(keep[:, :, None], (z + xk) >> 1, (z + yj) >> 1)
        b = np.where(out, j, b); al = np.add.reduce(out.astype(np.int64), axis=2)
    return {"yx": x.reshape(N, 128, V).astype(np.float32).astype(BF), "yl": l.reshape(N, 128, M).astype(np.float32), "yw": w.reshape(N, 128, M).astype(np.float32),
            "yz": z.reshape(N, 128, M).astype(np.float32).astype(BF), "yb": b.astype(np.float32)}

@@ -1,0 +1,666 @@
+import numpy as np
+from concourse.mybir import AluOpType, ActivationFunctionType
+
+F32, BF, I32, U16 = "float32", "bfloat16", "int32", "uint16"
+V, A, M, RO = 4096, 2048, 256, 4
+HOPS = [1, 2, 3, 1]
+E = M + 16
+CFG = {"sameq": True, "gap": 0.1, "abs1": (0, 16), "abs5": (0, 8), "v2": 64, "v4": 64, "ch": 32, "chq": 64, "dwv": False,
+       "cyc": 1.04e-3, "pe": 0.8e-3, "g": 1.56, "sc": 3.8, "hop": 0.08, "fix": 0.03, "lat": 4.7, "iters": 1, "v1": 0,
+       "abs2": (0, 0), "abs4": (0, 0), "w1": 0, "w2": 0, "w4": 8, "w5": 8, "dnv": True}
+PR = {"rawy": 10, "s2": 20, "cx": 30, "s1": 40, "cj": 45, "f": 60, "s4": 62, "raww": 64, "fill": 66, "s5": 70, "ex": 72, "tile": 74, "patch": 75,
+      "z": 76, "pre": 77, "L": 78, "W": 125}
+PR.update({'rawy': -10, 's2': 24, 'cx': 38, 's1': 60, 'cj': 51, 'f': 48, 's4': 59, 'raww': 89, 'fill': 89, 's5': 158, 'ex': 55, 'tile': 76, 'patch': 84, 'z': 48, 'pre': 63, 'L': 60, 'W': 165})
+CFG.update({'iters': 2, 'abs1': (0, 16), 'abs5': (0, 4), 'v1': 64, 'v2': 64, 'v4': 64, 'dwv': False, 'chq': 64, 'abs2': (0, 4), 'abs4': (0, 0), 'w1': 8, 'w2': 0, 'w4': 12, 'w5': 12, 'dnv': True, 'ch': 32})
+PR.update({'rawy': -8, 's2': 51, 'cx': 29, 's1': 42, 'cj': 60, 'f': 38, 's4': 58, 'raww': 102, 'fill': 59, 's5': 151, 'ex': 68, 'tile': 92, 'patch': 116, 'z': 48, 'pre': 61, 'L': 65, 'W': 142})
+CFG.update({'abs1': (16, 4), 'abs5': (0, 4), 'v1': 0, 'v2': 64, 'v4': 64, 'dwv': False, 'chq': 64, 'abs2': (0, 4), 'abs4': (0, 0), 'w1': 0, 'w2': 0, 'w4': 12, 'w5': 4, 'dnv': True, 'ch': 32, 'gap': 0.1})
+
+
+def sb_(w, d):
+    return ("sbuf", [128, w], d)
+
+
+SCRATCH = {
+    "x": sb_(V + 16, BF), "xo0": sb_(A, BF), "xo1": sb_(A, BF), "sbi": sb_(A, I32), "tile": sb_(A + 16, F32),
+    "lai": sb_(M, I32), "lwi": sb_(M, I32), "b0i": sb_(M, I32), "thi": sb_(8, I32),
+    "L": sb_(M, F32), "W": sb_(M, F32), "L16": sb_(M, U16), "W16": sb_(M, U16), "z": sb_(M, BF),
+    "rawy": sb_(V, BF), "raww": sb_(V, BF), "rawg": sb_(V, BF), "miny": sb_(2 * V, BF), "minw": sb_(2 * V, BF), "ming": sb_(2 * V, BF), "So": sb_(M, F32), "fsc": sb_(V, BF),
+    "ci2": sb_(16, I32), "ci3": sb_(16, I32), "kc": sb_(8, F32), "kio": sb_(M, BF), "ones": sb_(M, BF), "ones32": sb_(128, F32),
+    "zero": sb_(M, BF), "e15": sb_(128, BF), "idb": sb_(128, BF), "nidb": sb_(128, BF), "hidb": sb_(128, BF),
+    "penb": sb_(128, BF), "nbig": sb_(128, BF), "bigb": sb_(128, BF), "id32": sb_(128, F32), "nid32": sb_(128, F32), "blk": sb_(128, F32), "nblk": sb_(128, F32),
+    "b8": sb_(8, F32), "b8s": sb_(8, F32), "b8b": sb_(8, BF), "bo16": sb_(8, BF), "bm32": sb_(8, BF), "bm16": sb_(8, BF), "kb8": sb_(8, BF), "two": sb_(128, BF),
+    "b8t": sb_(128, BF), "quart": sb_(M, BF), "tmpa": sb_(128, F32), "tmpb": sb_(128, F32), "tmpc": sb_(M, F32), "tmpd": sb_(M, BF), "thf": sb_(8, F32), "throw": sb_(M, F32),
+    "diag": sb_(M, F32), "diage": sb_(M, BF), "trix": sb_(M, F32), "trio": sb_(M, F32), "rown": sb_(M, BF), "rbig": sb_(M, F32), "r01": sb_(1024, BF),
+    "last": sb_(16, U16), "exps": sb_(16, U16), "exp": sb_(16, U16), "ncon": sb_(16, BF),
+    "wd": sb_(144, BF), "tmpe": sb_(144, BF), "id16": sb_(128, BF),
+    "ohw": sb_(M, BF), "vw": sb_(M, BF), "offb": sb_(16, U16), "offw": sb_(16, U16),
+    "selo": sb_(M, F32), "selg": sb_(M, F32), "Xm": sb_(M, F32), "Xf": sb_(M, F32), "XmB": sb_(M, F32), "XfB": sb_(M, F32),
+    "XmJ": sb_(M, F32), "XfJ": sb_(M, F32), "XN": sb_(M, BF), "XE": sb_(M, BF), "sg": sb_(M, BF), "cn": sb_(M, BF), "noc": sb_(16, BF), "lt": sb_(16, BF),
+    "S32": sb_(M, F32), "q0": sb_(M, BF), "q": sb_(M, BF), "nq": sb_(M, BF), "mx": sb_(M, BF), "Z": sb_(M, BF), "Zs": sb_(M, BF), "Ze": sb_(M, BF), "Zt": sb_(M, BF),
+    "uf": sb_(16, F32), "ut": sb_(16, F32), "offg": sb_(16, U16), "offs": sb_(32, U16), "ljo": sb_(16, U16), "ljs": sb_(16, F32), "lbo": sb_(16, U16),
+    "offt": sb_(32, U16), "pick": sb_(16, U16), "lbT": sb_(16, F32), "dT": sb_(16, F32), "mT": sb_(16, F32), "Tj": sb_(M, F32), "Dn": sb_(M, F32), "nc": sb_(M, F32),
+    "OH0": sb_(E + M, BF), "OH1": sb_(E + M, BF), "DW": sb_(E + M, F32), "Zw": sb_(E + M, BF), "Ge": sb_(M, F32), "t": sb_(M, F32), "u": sb_(M, F32), "zm": sb_(M, BF),
+    "zr": sb_(M, F32), "c2": sb_(16, I32), "c3": sb_(16, I32), "bb": sb_(M, BF), "ybo": sb_(M, F32),
+}
+for _c in "jgw":
+    SCRATCH["P" + _c] = sb_(M + 8, F32); SCRATCH["Pm" + _c] = sb_(24, F32); SCRATCH["step" + _c] = sb_(M + 16, BF)
+for _r in range(RO):
+    SCRATCH["sS%d" % _r] = sb_(M, U16); SCRATCH["rS%d" % _r] = sb_(M, U16)
+    SCRATCH["sY%d" % _r] = sb_(E, BF); SCRATCH["rY%d" % _r] = sb_(E, BF)
+    SCRATCH["sF%d" % _r] = sb_(M, BF); SCRATCH["rF%d" % _r] = sb_(M, BF)
+    SCRATCH["sX%d" % _r] = sb_(E, BF); SCRATCH["rX%d" % _r] = sb_(E + M, BF)
+for _b in range(8):
+    SCRATCH["B%d" % _b] = ("psum", [128, 512], F32)
+BUF, PLACE = dict(SCRATCH), {}
+for _d in (F32, BF, I32, U16):
+    _w = 0
+    for _n, (_where, _s, _t) in BUF.items():
+        if _where == "sbuf" and _t == _d and _s[1] <= 1024 and _n[1:].rstrip("0123") not in ("S", "Y", "F", "X") and _n not in ("lai", "lwi", "b0i", "thi", "z"):
+            PLACE[_n] = ("pk_" + _d, _w); _w += (_s[1] + 15) // 16 * 16
+            del SCRATCH[_n]
+    SCRATCH["pk_" + _d] = sb_(_w, _d)
+DMAS = ["d_xo0", "d_xo1", "d_xo2", "d_xo3", "d_la", "d_b0", "d_lw", "d_z", "d_th", "d_sb", "d_x0", "d_x1", "o_x", "o_l", "o_w", "o_z", "o_b"]
+SEMAPHORES = ["cV", "cA", "cP", "cG", "sent"] + DMAS + ["a%s%d" % (k, r) for k in "SYFX" for r in range(RO)]
+SIZE = {F32: 4, I32: 4, BF: 2, U16: 2}
+
+
+def R(name, a=None, b=None, step=None, parts=None):
+    if a is None:
+        a, b = 0, BUF[name][1][1]
+    return ("r", name, a, b, step, parts)
+
+
+def IN(win, off):
+    return ("i", win, off)
+
+
+def width(r):
+    return 16 * width(r[2]) if r[0] == "i" else len(range(r[2], r[3], r[4] or 1))
+
+
+def rank_program(g, core, T, topo):
+    rank = T.rank_of(core)
+    if rank is None:
+        return
+    op = AluOpType
+    AF = ActivationFunctionType
+    C = CFG
+    n = len(T.cores)
+    Q = {"V": g.vector, "A": g.scalar, "P": g.tensor, "G": g, "S": g.sync}
+    ops, cur = [], [1e9]
+
+    def ap(r):
+        if r[0] == "i":
+            return ap(r[1]).indirect(ap(r[2]))
+        ps = slice(0, r[5]) if r[5] else slice(None)
+        nm, o = PLACE.get(r[1], (r[1], 0))
+        return T[nm][ps, o + r[2]:o + r[3]:r[4]] if r[4] else T[nm][ps, o + r[2]:o + r[3]]
+
+    def add(q, fn, outs, ins, cost, done=None, free=False, after=0.0):
+        w, rd = [], []
+        for x in ins:
+            if isinstance(x, tuple):
+                rd += [x[1], x[2]] if x[0] == "i" else [x]
+        for o in outs:
+            if o[0] == "i":
+                w.append(o[1]); rd.append(o[2])
+            else:
+                w.append(o)
+        ops.append({"q": q, "fn": fn, "w": w, "r": rd, "done": done, "cost": cost, "free": free, "after": after, "also": [], "pr": cur[0],
+                    "sc": any(o[0] == "i" for o in outs)})
+
+    def cost(o, a, per):
+        if a[0] == "i" or o[0] == "i":
+            return 0.05 + width(o) * C["cyc"] * (C["g"] if a[0] == "i" else C["sc"])
+        return C["fix"] + max(64, width(a) * per) * C["cyc"]
+
+    def half(*rs):
+        return 0.5 if all(x[0] == "r" and SIZE[BUF[x[1]][2]] == 2 for x in rs) else 1
+
+    def val(s):
+        return ap(s) if isinstance(s, tuple) else s
+
+    def cp(o, i):
+        add("V", lambda: g.vector.tensor_copy(ap(o), ap(i)), [o], [i], cost(o, i, half(o, i)))
+
+    def tt(o, a, b, f):
+        ps = BUF[b[1]][0] == "psum" or (a[0] == "r" and BUF[a[1]][0] == "psum")
+        add("V", lambda: g.vector.tensor_tensor(ap(o), ap(a), ap(b), f), [o], [a, b], cost(o, a, 1 if ps else 2))
+
+    def ts(o, a, s1, f1, s2=None, f2=None):
+        if f2 is None:
+            add("V", lambda: g.vector.tensor_scalar(ap(o), ap(a), val(s1), None, f1), [o], [a, s1], cost(o, a, half(o, a)))
+        else:
+            add("V", lambda: g.vector.tensor_scalar(ap(o), ap(a), val(s1), val(s2), f1, f2), [o], [a, s1, s2], cost(o, a, half(o, a)))
+
+    def scan(o, d0, d1, f0, f1):
+        add("V", lambda: g.vector.tensor_tensor_scan(ap(o), ap(d0), ap(d1), 0.0, f0, f1), [o], [d0, d1], cost(o, d0, half(o, d0, d1)))
+
+    def ms(o, c):
+        add("V", lambda: g.vector.memset(ap(o), c), [o], [], cost(o, o, 0.5))
+
+    def act(o, i, f=None, bias=0.0, scale=1.0):
+        if f is None:
+            add("A", lambda: g.scalar.activation(ap(o), ap(i), AF.Copy), [o], [i], cost(o, i, 1))
+        else:
+            add("A", lambda: g.scalar.activation(ap(o), ap(i), f, bias=bias, scale=scale), [o], [i], cost(o, i, 1))
+
+    def mm(o, l, r, st, sp):
+        c = max(min(64, width(l)), width(r)) * (4 if BUF[l[1]][2] == F32 else 1) * C["pe"]
+        add("P", lambda: g.tensor.matmul(ap(o), ap(l), ap(r), st, sp), [o], [l, r], c, free=not (st or sp))
+
+    def iota(o, pat, base, cm):
+        if BUF[o[1]][2] == I32:
+            add("G", lambda: g.iota(ap(o), pat, base, cm), [o], [], 0.13 + 2 * width(o) * C["cyc"])
+        else:
+            add("G", lambda: g.iota(ap(o), pat, base, cm, allow_small_or_imprecise_dtypes=True), [o], [], 0.13 + 2 * width(o) * C["cyc"])
+
+    def load(q, o, src, sem, after):
+        add(q, lambda: Q[q].dma_start(ap(o), src), [o], [], 0.05, (sem, 16), after=after)
+
+    def store(q, dst, i, sem, after=2.5):
+        add(q, lambda: Q[q].dma_start(dst, ap(i)), [], [i], 0.05, (sem, 16), after=after)
+
+    nsent, sends = [0], {}
+
+    def send(kind, r, to):
+        dst = T.cores[to]
+        rid, pid = topo.addr(dst)[:2]
+        mask, ne = topo.mask(core, dst), len(topo.engines(core, dst))
+        src, sem = R("s%s%d" % (kind, r)), "a%s%d" % (kind, r)
+        land = R("r%s%d" % (kind, r), 0, src[3])
+        nsent[0] += ne
+        sends[kind, r] = len(ops)
+        add("G", lambda: g.remote_dma(ap(land), ap(src), T.sem[sem], T.sem.sent, pid, rid, mask), [], [src], 0.5, ("sent", 0), after=C["lat"] - 0.5)
+
+    def arrive(kind, r, frm):
+        ne = len(topo.engines(T.cores[frm], core))
+        add(None, None, [R("r%s%d" % (kind, r), 0, BUF["s%s%d" % (kind, r)][1][1])], [], 0.0, ("a%s%d" % (kind, r), ne))
+        ops[-1]["also"].append(sends[kind, r])
+
+    col = lambda j: R("kc", j, j + 1)
+    B = lambda b, a=0, e=M, st=None, parts=None: R("B%d" % b, a, e, st, parts)
+    row = lambda nm, w=M: R(nm, 0, w, None, 1)
+    H = lambda nm, h, o=0: R(nm, 128 * h + o, 128 * h + 128 + o)
+    P8 = lambda nm, a, b: R(nm, a, b, None, 8)
+    XA, XW, TW = R("x", 0, A), R("x"), R("tile")
+    HH = (0, 1)
+
+    load("S", R("lai"), T.la[:], "d_la", 2.5)
+    load("A", P8("b0i", 0, M), T.b0[:], "d_b0", 2.5)
+    load("S", R("sbi"), T.sb[:], "d_sb", 7.0)
+    load("S", R("x", 0, A), T.xs[:, 0:A], "d_x0", 8.8)
+    load("S", R("z"), T.z0[:], "d_z", 9.0)
+    load("S", R("lwi"), T.lw[:], "d_lw", 9.5)
+    load("S", P8("thi", 0, 1), T.th[:], "d_th", 9.5)
+    load("S", R("x", A, V), T.xs[:, A:V], "d_x1", 11.5)
+    load("S", R("xo0"), T.xs[:, 0:A], "d_xo0", 14.0)
+    nload = len(ops)
+
+    iota(R("ci2", 0, 2), [[0, 2]], 0, 1)
+    iota(R("kio"), [[0, 16], [1, 16]], 0, 0)
+    iota(R("tmpa"), [[1, 8], [0, 16]], 0, 0)
+    iota(R("ci3"), [[1, 16]], 0, 0)
+    iota(R("tmpb"), [[1, 128]], 0, -1)
+    iota(R("tmpe"), [[1, 144]], 0, 0)
+    cur[0] = 5
+    ts(R("ci2", 4, 5), R("ci2", 0, 1), 15, op.bitwise_and)
+    ts(R("ci2", 5, 6), R("ci2", 0, 1), 4, op.arith_shift_right)
+    ts(R("ci2", 6, 7), R("ci2", 0, 1), 0, op.arith_shift_right)
+    cp(R("kc", 0, 3), R("ci2", 4, 7))
+    ts(R("kc", 3, 4), col(0), float(V), op.add)
+    ts(R("kc", 4, 5), col(0), float(A), op.add)
+    ts(R("kc", 5, 6), col(0), 0.0, op.is_equal, 1000.0, op.mult)
+    ts(R("b8t"), R("tmpa"), col(2), op.is_equal)
+    ts(R("b8"), R("kio", 0, 8), col(1), op.is_equal)
+    ts(R("diag"), R("kio"), col(0), op.is_equal)
+    ts(R("id32"), R("tmpb"), 0.0, op.is_equal)
+    ts(R("blk"), R("tmpa"), col(1), op.is_equal)
+    ts(R("kc", 6, 7), col(1), 16.0, op.mult, 16.0, op.add)
+    ts(R("wd"), R("tmpe"), col(6), op.is_equal, col(0), op.mult)
+    for nm, c in (("idb", 1.0), ("id16", 16.0), ("penb", 2.0 ** 18), ("nidb", -1.0), ("hidb", 0.5), ("nbig", -8192.0), ("bigb", 8192.0), ("nid32", -1.0)):
+        act(R(nm), R("id32"), AF.Identity, 0.0, c)
+    for nm, c in (("b8s", 2.0 ** -13), ("b8b", 1.0), ("bo16", 16.0), ("bm32", -32.0), ("bm16", -16.0), ("kb8", col(0))):
+        ts(R(nm), R("b8"), c, op.mult)
+    act(R("nblk"), R("blk"), AF.Identity, 0.0, -1.0)
+    cp(R("exp"), R("ci3"))
+    ts(R("last"), R("ci3"), 16.0, op.mult, 15.0, op.add)
+    ts(R("exps"), R("ci3"), col(5), op.add, 16.0, op.min)
+    ts(R("ncon"), R("ci3"), 16.0, op.mult, col(0), op.add)
+    ms(R("ones"), 1.0); ms(R("zero"), 0.0); ms(R("ones32"), 1.0); ms(R("two"), 2.0); ms(R("quart"), -0.25)
+    ms(R("x", V, V + 16), 0.0); ms(R("tile", A, A + 16), 0.0)
+    for c in "jgw":
+        ms(R("P" + c, 0, 8), -1.0e9); ms(R("Pm" + c, 16, 24), 1.0e9); ms(R("step" + c, M, M + 16), 0.0)
+    ms(R("OH0", M, E), 0.0); ms(R("OH1", M, E), 0.0); ms(R("DW", 0, E), 0.0); ms(R("Zw", 0, E), 0.0)
+    ms(R("sY0", M, E), -10.0)
+    ts(R("e15"), R("kio", 0, 128), 15.0, op.is_equal)
+    for j in range(4):
+        act(R("r01", M * j, M * j + M), R("kio"), AF.Sign)
+    act(R("rbig"), R("r01", 0, M), AF.Identity, 2.0 ** 22, -2.0 ** 22)
+    ts(R("trio"), R("kio"), col(0), op.is_gt, 1.0e6, op.mult)
+    act(R("trix"), R("diag"), AF.Identity, 0.0, 8192.0)
+    tt(R("trix"), R("trix"), R("trio"), op.add)
+    act(R("tmpd"), R("diag"), AF.Identity, 1.0, -2.0)
+    tt(R("rown"), R("tmpd"), R("r01", 0, M), op.mult)
+    act(R("diage"), R("diag"), AF.Identity, 0.0, float(E))
+    cp(P8("thf", 0, 1), P8("thi", 0, 1))
+    ts(P8("thf", 1, 2), P8("thf", 0, 1), 16.0, op.mult)
+    ts(P8("tmpc", 0, 128), P8("kio", 0, 128), P8("thf", 1, 2), op.add)
+    for h in HH:
+        tt(P8("throw", 128 * h, 128 * h + 128), P8("tmpc", 0, 128), P8("b8t", 0, 128), op.mult)
+
+    cp(P8("bb", 0, M), P8("b0i", 0, M))
+    mm(B(7), P8("b8t", 0, 128), P8("bb", 0, M), True, True)
+    cur[0] = 1
+    cp(R("L"), R("lai")); cp(R("L16"), R("lai"))
+    cur[0] = 5
+    ts(R("OH0", 0, M), B(7), col(0), op.is_equal)
+    tt(R("u"), R("OH0", 0, M), R("L"), op.mult)
+    for h in HH:
+        mm(B(4, 8 * h, 8 * h + 8), H("u", h), R("b8"), True, True)
+    cp(R("lbT"), B(4, 0, 16))
+    cp(R("W"), R("lwi")); cp(R("W16"), R("lwi"))
+
+    def bound(r):
+        tt(R("XmB"), IN(R("lbT"), R("exp")), R("diag"), op.mult)
+        act(R("XfB"), IN(R("lbT"), R("exp")))
+        for h in HH:
+            mm(B(4, M + 8 * h, M + 8 * h + 8), H("XmB", h), R("b8s"), True, True)
+        ts(R("lbo"), B(4, M, M + 16), 8192.0, op.mult)
+        act(R("sY%d" % r, 0, M), IN(XA, R("lbo")))
+        send("Y", r, (rank + HOPS[r]) % n)
+
+    def waiting():
+        if C["dwv"]:
+            for h in HH:
+                mm(B(7, 128 * h, 128 * h + 128), H("XfB", h), R("id32"), True, True)
+            tt(R("DW", E, E + M), B(7), R("W"), op.subtract)
+        else:
+            mm(B(7), R("nid32"), R("W"), True, False)
+            for h in HH:
+                mm(B(7, 128 * h, 128 * h + 128), H("XfB", h), R("id32"), False, h == 1)
+            act(R("DW", E, E + M), B(7))
+
+    cur[0] = 0
+    bound(0)
+    cp(R("sS0"), IN(R("sbi"), R("lbo")))
+    send("S", 0, (rank + HOPS[0]) % n)
+    cur[0] = 50
+    for j in range(4):
+        cp(R("tile", 512 * j, 512 * j + 512), R("sbi", 512 * j, 512 * j + 512))
+    waiting()
+
+    def raw(buf, win, off, nv, ch):
+        for a in range(0, M, ch):
+            (cp if a < nv else act)(R(buf, 16 * a, 16 * (a + ch)), IN(win, R(off, a, a + ch)))
+
+    def score(bank, rawb, minb, yb, wt, other, dist, na, wide):
+        todo = []
+        top = 16 - max(na)
+        wide = range(top - min(wide, top), top)
+        for h in HH:
+            src = lambda k: R(rawb, 2048 * h + k, 2048 * h + 2048, 16)
+            dst = lambda k: R(minb, M * k + 128 * h, M * k + 128 * h + 128)
+            far = lambda k, w=1: R(minb, V + 2048 * h + 128 * k, V + 2048 * h + 128 * (k + w))
+            key = lambda k: B(bank, 128 * h + k, 128 * h + 128, 16)
+            for k in range(16 - na[h]):
+                if dist:
+                    todo.append((key(k), src(k), "bo16"))
+                if k not in wide:
+                    tt(dst(k), src(k), B(yb, 128 * h, 128 * h + 128), op.min)
+                elif h == 0:
+                    tt(R(minb, M * k, M * k + M), R(rawb, k, V, 16), B(yb), op.min)
+                todo.append((key(k), dst(k), wt))
+            for k0 in range(16 - na[h], 16, 4):
+                db = {"miny": (5, 7), "ming": (6, 6), "minw": (5, 6)}[minb][(k0 // 4) % 2]
+                for j in range(4):
+                    mm(B(db, 128 * j, 128 * j + 128), R("nidb"), src(k0 + j), True, False)
+                    mm(B(db, 128 * j, 128 * j + 128), R("idb"), H(other, h), False, True)
+                act(far(k0, 4), B(db, 0, 512), AF.Abs if dist else AF.Relu)
+                for j in range(4):
+                    if na[h] < 16 or not dist:
+                        todo.append((key(k0 + j), H(other, h), "bm16"))
+                    todo.append((key(k0 + j), far(k0 + j), "bo16"))
+        for i, (o, l, w) in enumerate(todo):
+            mm(o, l, R(w), False, i == len(todo) - 1)
+
+    def least(c, bank):
+        scan(R("P" + c, 8, M + 8), R("rbig"), B(bank), op.add, op.min)
+        cp(R("Pm" + c, 0, 16), R("P" + c, 23, M + 8, 16))
+        tt(R("step" + c, 0, M), IN(R("Pm" + c), R("exps")), R("P" + c, 7, M + 7), op.is_equal)
+
+    def turn(bank, src):
+        mm(B(bank), row("ones", 128), row("zero"), True, False)
+        for h in HH:
+            mm(B(bank, 128 * h, 128 * h + 128), H(src, h), R("id32"), False, False)
+
+    def chosen(c, bank, out):
+        mm(B(bank), R("nbig"), R("step" + c, 0, M), False, True)
+        scan(R(out), R("step" + c, 0, M), B(bank), op.mult, op.max)
+
+    def onehot(c, bank, o):
+        mm(B(bank, o, o + M), row("e15", 128), row("ones"), True, False)
+        for h in HH:
+            mm(B(bank, o + 128 * h, o + 128 * h + 128), H("step" + c, h, 1), R("idb"), False, False)
+            mm(B(bank, o + 128 * h, o + 128 * h + 128), H("step" + c, h), R("nidb"), False, h == 1)
+
+    def pairs(xm, xf, xn=None):
+        mm(B(6), row("ones", 128), row("zero"), True, False)
+        for h in HH:
+            if xn:
+                mm(B(6, 128 * h, 128 * h + 128), H(xn, h), R("bigb"), False, False)
+            mm(B(6, 128 * h, 128 * h + 128), H(xm, h), R("nblk"), False, False)
+            mm(B(6, 128 * h, 128 * h + 128), H(xf, h), R("id32"), False, h == 1)
+
+    def slot(out, oh, o):
+        mm(B(4, o, o + 16), R("id16"), R("ncon"), True, False)
+        for b in range(16):
+            mm(B(4, o, o + 16), R("wd", 16 - b, 144 - b), R(oh, b, M, 16), False, b == 15)
+        cp(R(out), B(4, o, o + 16))
+
+    def count(rY):
+        act(R("sg"), B(2), AF.Sign, 15.5, -1.0)
+        scan(R("cn"), R("r01", 0, M), R("sg"), op.mult, op.add)
+
+    for r in range(RO):
+        lastr = r == RO - 1
+        to, frm = (rank + HOPS[r]) % n, (rank - HOPS[r]) % n
+        sX, rX, rY, rS, OH, OHn = "sX%d" % r, "rX%d" % r, "rY%d" % r, "rS%d" % r, "OH%d" % (r % 2), "OH%d" % ((r + 1) % 2)
+
+        def pr(k):
+            cur[0] = 100 * r + PR[k]
+        pr("rawy")
+        if r == 0:
+            raw("rawy", XA, "L16", C["v1"], C["ch"])
+        pr("s1")
+        mm(B(1), R("idb"), R("z"), True, True)
+        mm(B(3), row("ones", 128), row("kio"), True, False)
+        for h in HH:
+            mm(B(3, 128 * h, 128 * h + 128), H(OH, h), R("penb"), False, False)
+        score(3, "rawy", "miny", 1, "bm32", "z", True, C["abs1"], C["w1"])
+        pr("cj")
+        turn(7, "L")
+        least("j", 3)
+        chosen("j", 7, "selo")
+        onehot("j", 7, M)
+        act(R(OH, E, E + M), B(7, M, 2 * M))
+        tt(R("XmJ"), IN(R("selo"), R("last")), R("diag"), op.mult)
+        for h in HH:
+            mm(B(3, M + 8 * h, M + 8 * h + 8), H("XmJ", h), R("b8s"), True, True)
+        ts(R("ljo"), B(3, M, E), 8192.0, op.mult)
+        act(R(rX, E, E + M), IN(R("xo%d" % (r % 2)), R("ljo")))
+        if not lastr:
+            ts(R("ljs"), B(3, M, E), 1.0, op.add)
+            tt(R("dT"), R("selo", 15, M, 16), R("lbT"), op.subtract)
+        pr("s2")
+        arrive("Y", r, frm); arrive("S", r, frm)
+        raw("rawg", XW, rS, C["v2"], C["ch"])
+        cp(R("S32"), R(rS))
+        mm(B(0), R("idb"), R(rY, 0, M), True, True)
+        mm(B(2), P8("ones32", 0, 128), P8("throw", 0, M), True, False)
+        turn(4, "S32")
+        score(2, "rawg", "ming", 0, "bm16", rY, False, C["abs2"], C["w2"])
+        pr("cx")
+        act(R("q0"), R(rY, 0, M), AF.Identity, 191.625, 0.25)
+        act(R("q"), R("q0"), AF.Identity, -192.0, 1.0)
+        act(R("nq"), R("q0"), AF.Identity, 192.0, -1.0)
+        least("g", 2)
+        count(rY)
+        tt(R("noc"), R("cn", 15, M, 16), R(rY, M, E), op.is_lt)
+        act(R("XN"), IN(R("noc"), R("exp")))
+        chosen("g", 4, "selg")
+        tt(R("Xm"), IN(R("selg"), R("last")), R("diag"), op.mult)
+        act(R("Xf"), IN(R("selg"), R("last")))
+        for h in HH:
+            mm(B(4, M + 8 * h, M + 8 * h + 8), H("Xm", h), R("b8s"), True, True)
+        pairs("Xm", "Xf", "XN")
+        ts(R("offg"), B(4, M, M + 16), 8192.0, op.mult)
+        tt(R("mx"), IN(XW, R("offg")), R("q"), op.max)
+        tt(R("Z"), B(6), R("trix"), op.is_equal)
+        scan(R("Zs"), R("r01", 0, M), R("Z"), op.mult, op.max)
+        tt(R("uf"), R("Zs", 15, M, 16), B(4, M, M + 16), op.add)
+        ts(R("offs", 0, 32, 2), R("uf"), 8192.0, op.mult, col(3), op.min)
+        for a in range(15, -1, -1):
+            tt(IN(XW, R("offs", 2 * a, 2 * a + 1)), R("mx", 16 * a, 16 * a + 16), R("nq", 16 * a, 16 * a + 16), op.add)
+        if lastr:
+            store("S", T.yx[:], R("x", 0, V), "o_x", 6.5)
+        else:
+            xo = R("xo%d" % ((r + 1) % 2))
+            add("S", lambda xo=xo: g.sync.dma_start(ap(xo), ap(XA)), [xo], [XA], 0.05, ("d_xo%d" % (r + 1), 16), after=4.0)
+            pr("fill")
+            act(R("XfJ"), IN(R("selo"), R("last")))
+            act(R("Tj"), IN(TW, R("ljo")))
+            pairs("XmJ", "XfJ")
+            tt(R("Zw", E, E + M), B(6), R("trio"), op.is_equal)
+            if C["dnv"]:
+                tt(R("Dn"), IN(TW, R("lbo")), R("Tj"), op.subtract)
+            else:
+                act(R("So"), IN(TW, R("lbo")))
+                mm(B(7), R("id32"), R("So"), True, False)
+                mm(B(7), R("nid32"), R("Tj"), False, True)
+                act(R("Dn"), B(7))
+        pr("f")
+        raw("rawg", XW, rS, C["v4"], C["ch"])
+        for a in range(0, V, 16 * C["chq"]):
+            scan(R("fsc", a, a + 16 * C["chq"]), R("r01", 0, 16 * C["chq"]), R("rawg", a, a + 16 * C["chq"]), op.mult, op.max)
+        cp(R("sF%d" % r), R("fsc", 15, V, 16))
+        send("F", r, frm)
+        pr("s4")
+        act(R(sX, 0, M), IN(XW, R("offg")))
+        mm(B(2), P8("ones32", 0, 128), P8("throw", 0, M), True, False)
+        score(2, "rawg", "ming", 0, "bm16", rY, False, C["abs4"], C["w4"])
+        count(rY)
+        tt(R("lt"), R("cn", 15, M, 16), R(rY, M, E), op.is_lt)
+        tt(R(sX, M, E), R("lt"), R("noc"), op.max)
+        send("X", r, frm)
+        pr("raww")
+        raw("raww", XA, "W16", 0, C["ch"])
+        pr("s5")
+        arrive("F", r, to)
+        mm(B(1), R("idb"), R("rF%d" % r), True, True)
+        mm(B(3), row("ones", 128), row("kio"), True, False)
+        score(3, "raww", "minw", 1, "bm32", "rF%d" % r, True, C["abs5"], C["w5"])
+        least("w", 3)
+        pr("ex")
+        arrive("X", r, to)
+        eT = R(rX, M, E)
+        tt(R("XE"), IN(eT, R("exp")), R("diage"), op.mult)
+        mm(B(4, 0, 16), R("idb"), R("ncon"), True, False)
+        for h in HH:
+            mm(B(4, 8 * h, 8 * h + 8), H("XE", h), R("b8b"), False, h == 1)
+        cp(R("pick"), B(4, 0, 16))
+        act(R("Ge"), IN(R("DW"), R("pick")))
+        if not lastr:
+            act(R("Ze"), IN(R("Zw"), R("pick")))
+            for h in HH:
+                mm(B(4, 16 + 8 * h, 24 + 8 * h), R("two"), R(rX, M, M + 8), True, False)
+                mm(B(4, 16 + 8 * h, 24 + 8 * h), R("two"), R(rX, M + 8, E), False, True)
+            cp(R("c2"), B(4, 16, 32))
+            ts(R("c3"), R("c2"), 2, op.bitwise_and)
+            ts(R("sY%d" % (r + 1), M, E), R("c3"), -10.0, op.add)
+            tt(R("mT"), eT, R("dT"), op.mult)
+            tt(R("lbT"), R("lbT"), R("mT"), op.add)
+            bound(r + 1)
+            scan(R("Zt"), R("rown"), R("Ze"), op.mult, op.add)
+            tt(R("ut"), R("ljs"), R("Zt", 15, M, 16), op.subtract)
+            ts(R("offt", 0, 32, 2), R("ut"), 8192.0, op.mult, col(4), op.min)
+        onehot("w", 5, 0)
+        if not lastr:
+            pr("pre")
+            raw("rawy", XA, "L16", 0, C["ch"])
+            slot("offb", OH, 288)
+            pr("patch")
+            onehot("w", 6, 0)
+            act(R("ohw"), B(6))
+            slot("offw", "ohw", 304)
+            act(R("vw"), IN(R("raww"), R("offw")))
+            cp(IN(R("rawy"), R("offb")), R("vw"))
+            pr("tile")
+            tt(R("nc"), B(5), R("Dn"), op.mult)
+            for a in range(15, -1, -1):
+                tt(IN(TW, R("offt", 2 * a, 2 * a + 1)), R("nc", 16 * a, 16 * a + 16), R("Tj", 16 * a, 16 * a + 16), op.add)
+            cp(R("sS%d" % (r + 1)), IN(TW, R("lbo")))
+            send("S", r + 1, (rank + HOPS[r + 1]) % n)
+        pr("L")
+        tt(R("t"), B(5), R("Ge"), op.mult)
+        mm(B(2), R("blk"), R("t"), True, True)
+        tt(B(2), B(2), R(OH, 0, M), op.mult)
+        tt(R("L"), R("L"), B(2), op.subtract)
+        if r < RO - 2:
+            cp(R("L16"), R("L"))
+        pr("z")
+        act(R("zm"), IN(R(rX), R("pick")))
+        act(R(OHn, 0, M), IN(R(OH), R("pick")))
+        mm(B(1), row("ones", 128), row("quart"), True, False)
+        mm(B(1), R("hidb"), R("z"), False, False)
+        mm(B(1), R("hidb"), R("zm"), False, True)
+        act(R("zr"), B(1), AF.Identity, 12582912.0, 1.0)
+        act(R("z"), R("zr"), AF.Identity, -12582912.0, 1.0)
+        pr("W")
+        if lastr:
+            tt(R("W"), R("W"), R("t"), op.add)
+            mm(B(3, 0, M, None, 8), R("kb8"), R(OHn, 0, M), True, True)
+            cp(P8("ybo", 0, M), B(3, 0, M, None, 8))
+            store("S", T.yz[:], R("z"), "o_z")
+            store("A", T.yb[:], P8("ybo", 0, M), "o_b")
+            store("S", T.yw[:], R("W"), "o_w")
+            store("A", T.yl[:], R("L"), "o_l")
+        else:
+            mm(B(5), R("id32"), R("W"), True, False)
+            mm(B(5), R("id32"), R("t"), False, True)
+            cp(R("W16"), B(5))
+            act(R("W"), B(5))
+            waiting()
+
+    def meet(a, b):
+        return a[2] < b[3] and b[2] < a[3]
+
+    acc, era = {}, {}
+    for i, o in enumerate(ops):
+        q = o["q"]
+        o["key"] = o["done"][0] if o["done"] else "c" + q
+        pre = {j: False for j in o["also"]}
+        if 0 < i < nload:
+            pre[i - 1] = False
+        for kind, rs in (("r", o["r"]), ("w", o["w"])):
+            for x in rs:
+                psum = BUF[x[1]][0] == "psum"
+                if psum:
+                    e = era.setdefault(x[1], [q, []])
+                    if e[0] != q:
+                        e[0], e[1], acc[x[1]] = q, [j for j, k2, y in acc[x[1]]], []
+                    for j in e[1]:
+                        pre[j] = True
+                for (j, k2, y) in acc.get(x[1], []):
+                    p = ops[j]
+                    if j == i:
+                        continue
+                    if psum and q == "P":
+                        if not (o["free"] and p["free"]):
+                            pre.setdefault(j, False)
+                    elif meet(x, y) and (kind == "w" or k2 == "w"):
+                        same = p["q"] == q and not p["done"] and not o["done"]
+                        pre[j] = pre.get(j, False) or not same or kind == "r" or C["sameq"]
+        o["pre"] = pre
+        for kind, rs in (("r", o["r"]), ("w", o["w"])):
+            for x in rs:
+                lst = acc.setdefault(x[1], [])
+                if kind == "w" and not x[4] and not x[5] and BUF[x[1]][0] != "psum":
+                    lst[:] = [e for e in lst if not (x[2] <= e[2][2] and e[2][3] <= x[3])]
+                lst.append((i, kind, x))
+    for i, o in enumerate(ops):
+        o["post"] = []
+    for i, o in enumerate(ops):
+        for j in o["pre"]:
+            ops[j]["post"].append(i)
+
+    def lag(j, i):
+        p = ops[j]
+        if ops[i]["pre"][j]:
+            return p["cost"] + p["after"] + C["hop"]
+        return p["cost"] + (p["after"] if ops[i]["q"] is None else 0.0)
+
+    for i in range(len(ops) - 1, -1, -1):
+        o = ops[i]
+        o["rest"] = max([lag(i, k) + ops[k]["rest"] for k in o["post"]] + [o["cost"] + o["after"]])
+    N = len(ops)
+    true = [[(j, lag(j, i)) for j in ops[i]["pre"]] for i in range(N)]
+    room = lambda j, i: C["gap"] if ops[i].get("sc") and ops[j].get("sc") else 0.0
+    fwd = [[(j, lag(j, i) + room(j, i)) for j in ops[i]["pre"]] for i in range(N)]
+    bwd = [[(k, lag(i, k) + room(i, k) + ops[k]["cost"] - ops[i]["cost"]) for k in ops[i]["post"]] for i in range(N)]
+
+    def place(seq, edges, first):
+        at = [0.0] * N
+        line = {q: ([], []) for q in Q}
+        for i in seq:
+            t = first[i]
+            for j, d in edges[i]:
+                if at[j] + d > t:
+                    t = at[j] + d
+            q, c = ops[i]["q"], ops[i]["cost"]
+            if q is not None:
+                st, en = line[q]
+                p = int(np.searchsorted(en, t, side="right")) if en and en[-1] > t else len(en)
+                while p < len(st) and st[p] < t + c - 1e-9:
+                    t = max(t, en[p]); p += 1
+                st.insert(p, t); en.insert(p, t + c)
+            at[i] = t
+        return at
+
+    for i in range(N - 1, -1, -1):
+        ops[i]["pr"] = min([ops[i]["pr"]] + [ops[k]["pr"] for k in ops[i]["post"]])
+    seq = sorted(range(N), key=lambda i: (ops[i]["pr"], i))
+    best = None
+    for it in range(C["iters"]):
+        at = place(seq, fwd, [0.0] * N)
+        order = sorted(range(N), key=lambda i: (at[i], i))
+        real, free = [0.0] * N, {q: 0.0 for q in Q}
+        for i in order:
+            q = ops[i]["q"]
+            real[i] = max([real[j] + d for j, d in true[i]] + [free.get(q, 0.0)])
+            if q is not None:
+                free[q] = real[i] + ops[i]["cost"]
+        span = max(real[i] + ops[i]["cost"] + ops[i]["after"] for i in range(N))
+        if best is None or span < best[0]:
+            best = (span, order)
+        back = place(sorted(range(N), key=lambda i: (-at[i], -i)), bwd, [o["after"] for o in ops])
+        seq = sorted(range(N), key=lambda i: (-back[i] - ops[i]["cost"], i))
+    order = best[1]
+    C["span"] = best[0]
+    if C.get("dry"):
+        return
+    known = {q: {} for q in Q}
+    pos = {i: p for p, i in enumerate(order)}
+    for i in order:
+        o = ops[i]
+        o["waits"], o["clock"] = [], {}
+        if o["q"] is not None:
+            kn = known[o["q"]]
+            for j in sorted((j for j, w in o["pre"].items() if w), key=lambda j: -pos[j]):
+                key = ops[j]["key"]
+                if kn.get(key, -1) < pos[j]:
+                    o["waits"].append(j)
+                    ops[j]["sig"] = True
+                    kn[key] = pos[j]
+                    for k3, j3 in ops[j]["clock"].items():
+                        if kn.get(k3, -1) < j3:
+                            kn[k3] = j3
+            o["clock"] = dict(kn)
+    total = {}
+    for i in order:
+        o = ops[i]
+        key = o["key"]
+        for j in o["waits"]:
+            Q[o["q"]].wait_ge(T.sem[ops[j]["key"]], ops[j]["val"])
+        ins = o["fn"]() if o["fn"] else None
+        if o["done"]:
+            if key != "sent":
+                total[key] = o["val"] = o["done"][1]
+                if ins is not None:
+                    ins.then_inc(T.sem[key], 16)
+        elif o.get("sig"):
+            total[key] = o["val"] = total.get(key, 0) + 1
+            ins.then_inc(T.sem[key], 1)
+    total["sent"] = nsent[0]
+    for key, c in total.items():
+        g.wait_ge(T.sem[key], c)

@@ -1,19 +1,50 @@
 import numpy as np
 from concourse.mybir import AluOpType, ActivationFunctionType
 
-F32, BF, I32, U16 = "float32", "bfloat16", "int32", "uint16"
+F32, BF, I32, U16, F16 = "float32", "bfloat16", "int32", "uint16", "float16"
 V, A, M, RO = 4096, 2048, 256, 4
 HOPS = [1, 2, 3, 1]
 E = M + 16
-CFG = {"sameq": True, "gap": 0.1, "abs1": (0, 16), "abs5": (0, 8), "v2": 64, "v4": 64, "ch": 32, "chq": 64, "dwv": False,
-       "cyc": 1.04e-3, "pe": 0.8e-3, "g": 1.56, "sc": 3.8, "hop": 0.08, "fix": 0.03, "lat": 4.7, "iters": 1, "v1": 0,
-       "abs2": (0, 0), "abs4": (0, 0), "w1": 0, "w2": 0, "w4": 8, "w5": 8, "dnv": True}
-PR = {"rawy": 10, "s2": 20, "cx": 30, "s1": 40, "cj": 45, "f": 60, "s4": 62, "raww": 64, "fill": 66, "s5": 70, "ex": 72, "tile": 74, "patch": 75,
-      "z": 76, "pre": 77, "L": 78, "W": 125}
-PR.update({'rawy': -10, 's2': 24, 'cx': 38, 's1': 60, 'cj': 51, 'f': 48, 's4': 59, 'raww': 89, 'fill': 89, 's5': 158, 'ex': 55, 'tile': 76, 'patch': 84, 'z': 48, 'pre': 63, 'L': 60, 'W': 165})
-CFG.update({'iters': 2, 'abs1': (0, 16), 'abs5': (0, 4), 'v1': 64, 'v2': 64, 'v4': 64, 'dwv': False, 'chq': 64, 'abs2': (0, 4), 'abs4': (0, 0), 'w1': 8, 'w2': 0, 'w4': 12, 'w5': 12, 'dnv': True, 'ch': 32})
-PR.update({'rawy': -8, 's2': 51, 'cx': 29, 's1': 42, 'cj': 60, 'f': 38, 's4': 58, 'raww': 102, 'fill': 59, 's5': 151, 'ex': 68, 'tile': 92, 'patch': 116, 'z': 48, 'pre': 61, 'L': 65, 'W': 142})
-CFG.update({'abs1': (16, 4), 'abs5': (0, 4), 'v1': 0, 'v2': 64, 'v4': 64, 'dwv': False, 'chq': 64, 'abs2': (0, 4), 'abs4': (0, 0), 'w1': 0, 'w2': 0, 'w4': 12, 'w5': 4, 'dnv': True, 'ch': 32, 'gap': 0.1})
+SP = 32
+CFG = {"blk": 32, "a1": (16, 4), "a2": (0, 4), "a4": (0, 0), "a5": (0, 4), "early1": 0, "v1": 0, "v2": 64, "v4": 64, "v5": 0, "w1": 0, "w2": 0, "w4": 12, "w5": 4,
+       "ch": 32, "chq": 64, "dwv": True, "dnv": True, "gap": 0.1, "iters": 2, "mix": 0.0, "round": 30, "slope": 1.0,
+       "cyc": 0.95e-3, "pe": 0.48e-3, "g": 1.56, "sc": 3.8, "hop": 0.08, "fix": 0.0, "lat": 4.2}
+PR = {"rawy": -3, "s1": 0, "s1b": 5, "s2": -6, "m2": -5, "cx": -4, "f": 5, "fs": 7, "s4": 9, "x4": 10, "cj": 14, "fill": 16, "raww": 13, "s5": 15,
+      "ex": 16, "tile": 16, "lb": 18, "L": 19, "z": 24, "W": 30}
+CFG.update({'blk': 32, 'a1': (8, 8), 'a2': (0, 5), 'a4': (0, 4), 'a5': (1, 6), 'early1': 0, 'v1': 96, 'v2': 80, 'v4': 80, 'v5': 0, 'w1': 0, 'w2': 0, 'w4': 0, 'w5': 0, 'ch': 48, 'chq': 32, 'dwv': True, 'dnv': True, 'gap': 0.0, 'cyc': 0.00095, 'hop': 0.1, 'lat': 4.2})
+CFG.update(blkg=32, blkj=32, fix=0.05, afix=0.25, gfix=0.015, ona=())
+PR.update({'xs': 12, 'rawy': 9, 's1': 0, 's1b': 4, 's2': -6, 'm2': -5, 'cx': -4, 'f': 1, 'fs': 6, 's4': 9, 'x4': 10, 'cj': 25, 'fill': 20, 'raww': 36, 's5': 27, 'ex': 18, 'tile': 18, 'lb': 21, 'L': 27, 'z': 29, 'W': 30})
+CFG.update({'a1': (16, 16), 'a2': (4, 8), 'a4': (4, 3), 'a5': (0, 8), 'early1': 0, 'v1': 128, 'v2': 96, 'v4': 80, 'v5': 0, 'w1': 4, 'w2': 4, 'w4': 16, 'w5': 16, 'ch': 64, 'chq': 64, 'dwv': True, 'dnv': True, 'gap': 0.05, 'slope': 0.5, 'cyc': 0.00085, 'hop': 0.06, 'fix': 0.05, 'lat': 4.2, 'blkg': 32, 'blkj': 32, 'noca': False})
+PR.update({'rawy': 3, 's1': 21, 's1b': -1, 's2': -8, 'm2': 5, 'cx': -5, 'f': 8, 'fs': 3, 's4': 47, 'x4': 8, 'cj': 12, 'fill': 15, 'raww': 9, 's5': 16, 'ex': 32, 'tile': 19, 'lb': 17, 'L': 14, 'z': 23, 'W': 14, 'xs': 12})
+CFG.update({'a1': (12, 12), 'a2': (4, 8), 'a4': (4, 3), 'a5': (1, 8), 'early1': 0, 'v1': 32, 'v2': 112, 'v4': 32, 'v5': 0, 'w1': 4, 'w2': 4, 'w4': 16, 'w5': 16, 'ch': 64, 'chq': 32, 'dwv': True, 'dnv': True, 'gap': 0.1, 'slope': 0, 'cyc': 0.00085, 'hop': 0.07, 'fix': 0.05, 'lat': 3.5, 'blkg': 32, 'blkj': 32, 'ona': ('par',)})
+PR.update({'rawy': -9, 's1': 31, 's1b': -2, 's2': -7, 'm2': -2, 'cx': -5, 'f': -4, 'fs': 7, 's4': 39, 'x4': 8, 'cj': 10, 'fill': 15, 'raww': 15, 's5': 13, 'ex': 62, 'tile': 31, 'lb': 16, 'L': 11, 'z': 33, 'W': 27, 'xs': 12})
+CFG.update(t2=12, u2=0, ch2=4, s32a=False)
+PR.update(sh=-2)
+CFG.update(polish=0, seed=1, cases=1, alpha=0.0)
+CASES = [{"weight": 1.0},
+         {"weight": 1.0, "cyc": 0.83e-3, "pe": 0.40e-3, "g": 1.65, "fix": 0.06, "afix": 0.22, "hop": 0.09, "lat": 4.0},
+         {"weight": 0.65, "cyc": 1.3e-3, "pe": 0.65e-3, "g": 1.95, "sc": 5.5, "fix": 0.07, "afix": 0.18, "hop": 0.07, "lat": 4.8}]
+CFG.update({'a1': (16, 16), 'a2': (11, 1), 'a4': (4, 4), 'a5': (3, 4), 'early1': 2, 'v1': 64, 'v2': 96, 'v4': 64, 'v5': 0, 'w1': 8, 'w2': 0, 'w4': 16, 'w5': 12, 'ch': 96, 'chq': 64, 'dwv': True, 'dnv': False, 'gap': 0.05, 'slope': 0.5, 'cyc': 0.00095, 'hop': 0.07, 'fix': 0.04, 'lat': 3.5, 'blkg': 32, 'blkj': 32, 'afix': 0.15, 'ona': ('W', 'par', 'q0'), 't2': 12, 'u2': 0, 'ch2': 2, 's32a': True})
+PR.update({'rawy': -5, 's1': 22, 's1b': -3, 's2': -3, 'm2': -5, 'cx': -3, 'f': 6, 'fs': 6, 's4': 9, 'x4': 11, 'cj': 19, 'fill': 19, 'raww': 24, 's5': 15, 'ex': 29, 'tile': 23, 'lb': 18, 'L': 16, 'z': 24, 'W': 33, 'xs': 12, 'sh': -11})
+CFG.update(ttg=2.0, issue=0.9, t2=0, heat=0.5, two=0, load=3.6, v10=0, early=5, mid=5)
+CFG.update({'a1': (15, 12), 'a2': (4, 4), 'a4': (7, 4), 'a5': (2, 6), 'early1': 0, 'v1': 96, 'v2': 96, 'v4': 64, 'v5': 32, 'w1': 16, 'w2': 16, 'w4': 16, 'w5': 8, 'ch': 64, 'chq': 64, 'dwv': True, 'dnv': False, 'gap': 0.0, 'slope': 0, 'cyc': 0.0009, 'hop': 0.07, 'fix': 0.04, 'lat': 5.0, 'blkg': 32, 'blkj': 32, 'afix': 0.16, 'ona': ('W', 'new', 'q0', 't1'), 'two': 0, 'load': 4.2, 'v10': 0})
+PR.update({'rawy': -5, 's1': 25, 's1b': 1, 's2': -2, 'm2': -11, 'cx': -6, 'f': 4, 'fs': 3, 's4': 27, 'x4': 7, 'cj': 29, 'fill': 17, 'raww': 18, 's5': 18, 'ex': 28, 'tile': 12, 'lb': 15, 'L': 33, 'z': 12, 'W': 32, 'xs': 13, 'sh': -12})
+CFG.update({'a1': (10, 12), 'a2': (4, 8), 'a4': (4, 3), 'a5': (1, 8), 'early1': 0, 'v1': 32, 'v2': 112, 'v4': 32, 'v5': 0, 'w1': 4, 'w2': 16, 'w4': 12, 'w5': 12, 'ch': 64, 'chq': 32, 'dwv': True, 'dnv': True, 'gap': 0.05, 'slope': 0, 'cyc': 0.00085, 'hop': 0.09, 'fix': 0.05, 'lat': 4.2, 'blkg': 32, 'blkj': 32, 'afix': 0.25, 'ona': ('par',), 'ttg': 0, 'issue': 0.6, 'two': 0, 'load': 5.2, 'v10': 0})
+PR.update({'rawy': -2, 's1': 31, 's1b': 6, 's2': -15, 'm2': -10, 'cx': -1, 'f': -3, 'fs': 6, 's4': 43, 'x4': 8, 'cj': 10, 'fill': 19, 'raww': 20, 's5': 21, 'ex': 62, 'tile': 38, 'lb': 14, 'L': 10, 'z': 28, 'W': 38, 'xs': 12, 'sh': 0})
+CFG.update(own=0.09, scan=1.0, pfix=0.0)
+CFG.update({'a1': (16, 16), 'a2': (4, 6), 'a4': (4, 3), 'a5': (0, 8), 'early1': 0, 'v1': 64, 'v2': 128, 'v4': 80, 'v5': 0, 'w1': 16, 'w2': 8, 'w4': 16, 'w5': 8, 'ch': 128, 'chq': 32, 'dwv': True, 'dnv': True, 'gap': 0.1, 'slope': 0, 'cyc': 0.00085, 'pe': 0.00048, 'hop': 0.14, 'fix': 0.04, 'lat': 4.2, 'blkg': 16, 'blkj': 16, 'afix': 0.2, 'gfix': 0.08, 'ona': ('OH', 'W', 'par', 'z', 'zr'), 'ttg': 0, 'issue': 0.9, 'two': 1, 'load': 5.0, 'v10': 32, 'own': 0.08, 'scan': 1.0, 'pfix': 0.02})
+PR.update({'rawy': 8, 's1': 27, 's1b': 11, 's2': -1, 'm2': -21, 'cx': 23, 'f': -3, 'fs': 13, 's4': 47, 'x4': -1, 'cj': 31, 'fill': 15, 'raww': 5, 's5': 28, 'ex': 53, 'tile': 31, 'lb': 21, 'L': -1, 'z': 22, 'W': 41, 'xs': 22, 'sh': 8})
+CFG.update(xin="F", two=0)
+CFG.update({'a1': (12, 9), 'a2': (4, 9), 'a4': (4, 3), 'a5': (1, 8), 'early1': 0, 'v1': 32, 'v2': 112, 'v4': 32, 'v5': 0, 'w1': 0, 'w2': 16, 'w4': 16, 'w5': 12, 'ch': 96, 'chq': 64, 'dwv': True, 'dnv': True, 'gap': 0.0, 'slope': 0, 'cyc': 0.00085, 'pe': 0.00048, 'hop': 0.14, 'fix': 0.04, 'lat': 4.2, 'blkg': 32, 'blkj': 32, 'afix': 0.15, 'gfix': 0.015, 'ona': ('W', 'z'), 'ttg': 0, 'issue': 2.0, 'load': 4.2, 'v10': 0, 'own': 0.03, 'scan': 1.0, 'pfix': 0.0, 'xin': 'E'})
+PR.update({'rawy': 1, 's1': 6, 's1b': 12, 's2': 3, 'm2': 9, 'cx': 11, 'f': -13, 'fs': 5, 's4': 54, 'x4': 8, 'cj': 10, 'fill': 15, 'raww': 13, 's5': 12, 'ex': 14, 'tile': 18, 'lb': 16, 'L': 10, 'z': 47, 'W': 42, 'xs': 16, 'sh': 4})
+CFG.update(ylag=3.0)
+CFG.update({'a1': (12, 12), 'a2': (4, 8), 'a4': (4, 3), 'a5': (1, 8), 'early1': 0, 'v1': 64, 'v2': 112, 'v4': 32, 'v5': 0, 'w1': 4, 'w2': 16, 'w4': 12, 'w5': 16, 'ch': 48, 'chq': 32, 'dwv': True, 'dnv': True, 'gap': 0.0, 'slope': 0, 'cyc': 0.00085, 'pe': 0.0006, 'hop': 0.1, 'fix': 0.06, 'lat': 5.0, 'blkg': 32, 'blkj': 32, 'afix': 0.25, 'gfix': 0.015, 'ona': ('par',), 'ttg': 0, 'issue': 3.0, 'load': 5.0, 'v10': 0, 'own': 0.03, 'scan': 1.0, 'pfix': 0.0, 'xin': 'X', 'ylag': 3.0})
+PR.update({'rawy': -5, 's1': 25, 's1b': 4, 's2': -11, 'm2': 8, 'cx': -7, 'f': -4, 'fs': 7, 's4': 45, 'x4': 9, 'cj': 10, 'fill': 7, 'raww': 21, 's5': 0, 'ex': 12, 'tile': 28, 'lb': 8, 'L': 9, 'z': 56, 'W': 26, 'xs': 0, 'sh': -7})
+CFG.update({'a1': (8, 8), 'a2': (3, 4), 'a4': (2, 0), 'a5': (2, 8), 'early1': 0, 'v1': 128, 'v2': 96, 'v4': 64, 'v5': 0, 'w1': 0, 'w2': 0, 'w4': 0, 'w5': 4, 'ch': 64, 'chq': 64, 'dwv': True, 'dnv': True, 'gap': 0.0, 'slope': 0, 'cyc': 0.00085, 'pe': 0.00042, 'hop': 0.18, 'fix': 0.0, 'lat': 2.6, 'blkg': 32, 'blkj': 32, 'afix': 0.05, 'gfix': 0.015, 'ona': ('OH', 'W', 'new', 'q0', 'sg', 'z', 'zr'), 'ttg': 0, 'issue': 0.6, 'load': 3.0, 'v10': 32, 'own': 0.24, 'scan': 1.0, 'pfix': 0.0, 'xin': 'X', 'ylag': 0})
+PR.update({'rawy': -14, 's1': 29, 's1b': 2, 's2': -5, 'm2': -1, 'cx': 3, 'f': 1, 'fs': 7, 's4': 31, 'x4': 18, 'cj': 28, 'fill': 26, 'raww': 10, 's5': 7, 'ex': 15, 'tile': 11, 'lb': 19, 'L': 30, 'z': 51, 'W': 44, 'xs': 11, 'sh': -7})
+KEPT = {}
+SEGS = {16: [(0, 16, 8, 0, 1)], 32: [(0, 16, 4, 0, 2), (128, 32, 4, 1, 2)]}
+NS = 384
 
 
 def sb_(w, d):
@@ -21,47 +52,50 @@ def sb_(w, d):
 
 
 SCRATCH = {
-    "x": sb_(V + 16, BF), "xo0": sb_(A, BF), "xo1": sb_(A, BF), "sbi": sb_(A, I32), "tile": sb_(A + 16, F32),
+    "x": sb_(V + 32, BF), "xo0": sb_(A, BF), "xo1": sb_(A, BF), "sbi": sb_(A, I32), "tile": sb_(A + 2 * SP, F32), "zh": sb_(M, F16), "r16": sb_(M, BF), "S32": sb_(E, F32), "TT": sb_(2 * M, F32), "perm": sb_(16, U16), "R1": sb_(192, BF), "num": sb_(A, F32),
     "lai": sb_(M, I32), "lwi": sb_(M, I32), "b0i": sb_(M, I32), "thi": sb_(8, I32),
-    "L": sb_(M, F32), "W": sb_(M, F32), "L16": sb_(M, U16), "W16": sb_(M, U16), "z": sb_(M, BF),
+    "L": sb_(M, F16), "Lo": sb_(M, F32), "W": sb_(M, F32), "L16": sb_(M, U16), "W16": sb_(M, U16), "z": sb_(M, BF),
     "rawy": sb_(V, BF), "raww": sb_(V, BF), "rawg": sb_(V, BF), "miny": sb_(2 * V, BF), "minw": sb_(2 * V, BF), "ming": sb_(2 * V, BF), "So": sb_(M, F32), "fsc": sb_(V, BF),
-    "ci2": sb_(16, I32), "ci3": sb_(16, I32), "kc": sb_(8, F32), "kio": sb_(M, BF), "ones": sb_(M, BF), "ones32": sb_(128, F32),
-    "zero": sb_(M, BF), "e15": sb_(128, BF), "idb": sb_(128, BF), "nidb": sb_(128, BF), "hidb": sb_(128, BF),
-    "penb": sb_(128, BF), "nbig": sb_(128, BF), "bigb": sb_(128, BF), "id32": sb_(128, F32), "nid32": sb_(128, F32), "blk": sb_(128, F32), "nblk": sb_(128, F32),
-    "b8": sb_(8, F32), "b8s": sb_(8, F32), "b8b": sb_(8, BF), "bo16": sb_(8, BF), "bm32": sb_(8, BF), "bm16": sb_(8, BF), "kb8": sb_(8, BF), "two": sb_(128, BF),
-    "b8t": sb_(128, BF), "quart": sb_(M, BF), "tmpa": sb_(128, F32), "tmpb": sb_(128, F32), "tmpc": sb_(M, F32), "tmpd": sb_(M, BF), "thf": sb_(8, F32), "throw": sb_(M, F32),
-    "diag": sb_(M, F32), "diage": sb_(M, BF), "trix": sb_(M, F32), "trio": sb_(M, F32), "rown": sb_(M, BF), "rbig": sb_(M, F32), "r01": sb_(1024, BF),
-    "last": sb_(16, U16), "exps": sb_(16, U16), "exp": sb_(16, U16), "ncon": sb_(16, BF),
-    "wd": sb_(144, BF), "tmpe": sb_(144, BF), "id16": sb_(128, BF),
-    "ohw": sb_(M, BF), "vw": sb_(M, BF), "offb": sb_(16, U16), "offw": sb_(16, U16),
-    "selo": sb_(M, F32), "selg": sb_(M, F32), "Xm": sb_(M, F32), "Xf": sb_(M, F32), "XmB": sb_(M, F32), "XfB": sb_(M, F32),
-    "XmJ": sb_(M, F32), "XfJ": sb_(M, F32), "XN": sb_(M, BF), "XE": sb_(M, BF), "sg": sb_(M, BF), "cn": sb_(M, BF), "noc": sb_(16, BF), "lt": sb_(16, BF),
-    "S32": sb_(M, F32), "q0": sb_(M, BF), "q": sb_(M, BF), "nq": sb_(M, BF), "mx": sb_(M, BF), "Z": sb_(M, BF), "Zs": sb_(M, BF), "Ze": sb_(M, BF), "Zt": sb_(M, BF),
-    "uf": sb_(16, F32), "ut": sb_(16, F32), "offg": sb_(16, U16), "offs": sb_(32, U16), "ljo": sb_(16, U16), "ljs": sb_(16, F32), "lbo": sb_(16, U16),
-    "offt": sb_(32, U16), "pick": sb_(16, U16), "lbT": sb_(16, F32), "dT": sb_(16, F32), "mT": sb_(16, F32), "Tj": sb_(M, F32), "Dn": sb_(M, F32), "nc": sb_(M, F32),
-    "OH0": sb_(E + M, BF), "OH1": sb_(E + M, BF), "DW": sb_(E + M, F32), "Zw": sb_(E + M, BF), "Ge": sb_(M, F32), "t": sb_(M, F32), "u": sb_(M, F32), "zm": sb_(M, BF),
+    "ci2": sb_(16, I32), "ci3": sb_(16, I32), "kc": sb_(16, F32), "kio": sb_(M, BF), "ones": sb_(M, BF), "ones32": sb_(128, F32),
+    "zero": sb_(M, BF), "e15": sb_(128, BF), "idb": sb_(128, BF), "nidb": sb_(128, BF), "hidb": sb_(128, BF), "id6": sb_(128, BF), "idE": sb_(128, BF),
+    "penb": sb_(128, BF), "nbig": sb_(128, BF), "id32": sb_(128, F32), "nid32": sb_(128, F32), "blk": sb_(128, BF),
+    "b8": sb_(8, F32), "bo16": sb_(8, BF), "bm32": sb_(8, BF), "bm16": sb_(8, BF), "kb8": sb_(8, BF), "two": sb_(128, BF),
+    "b8t": sb_(128, BF), "quart": sb_(M, BF), "c2k": sb_(M, BF), "c128k": sb_(M, BF), "tmpa": sb_(128, F32), "tmpb": sb_(128, F32), "tmpc": sb_(M, F32), "thf": sb_(8, F32), "throw": sb_(128, F16), "c16": sb_(128, BF), "tmpt": sb_(128, BF),
+    "diag": sb_(M, BF), "lane": sb_(M, BF), "rbig": sb_(M, F32), "r01": sb_(1024, BF), "exps": sb_(16, U16), "exp": sb_(16, U16),
+    "R2": sb_(192, BF), "M3": sb_(NS, BF), "rseg": sb_(NS, BF), "M4": sb_(M, BF), "M5": sb_(M, BF), "hold4": sb_(M, BF), "idm4": sb_(128, BF),
+    "selo": sb_(M, F32), "selg": sb_(M, F32), "valg": sb_(M, F16), "valj": sb_(M, F16), "Xg": sb_(M, F16), "Xj": sb_(M, F16), "Ug": sb_(NS, F32), "Uj": sb_(NS, F32),
+    "Z": sb_(NS, BF), "Zs": sb_(NS, F32), "Zw": sb_(NS, BF), "sA": sb_(M, F32), "sB": sb_(NS, F32), "XE": sb_(M, BF),
+    "sg": sb_(M, BF), "cn": sb_(M, BF), "noc": sb_(16, BF), "nocB": sb_(16, F32), "par": sb_(16, BF), "v": sb_(M, F16), "L32": sb_(M, F32),
+    "Sh": sb_(M, F16), "q0": sb_(M, BF), "t1": sb_(M, BF), "new": sb_(M, BF),
+    "uf": sb_(16, F32), "ut": sb_(16, F32), "nw": sb_(16, F32), "offg": sb_(16, U16), "offs": sb_(32, U16), "ljo": sb_(16, U16), "ljs": sb_(16, F32), "lbo": sb_(16, U16),
+    "offt": sb_(32, U16), "pick": sb_(16, U16), "lbs": sb_(16, F32), "dl": sb_(16, F32), "el": sb_(16, F32), "ml": sb_(16, F32), "Tj": sb_(M, F32), "Dn": sb_(M, F32), "nc": sb_(M, F32),
+    "OH0": sb_(2 * M, BF), "OH1": sb_(2 * M, BF), "DW": sb_(M, F32), "lbF": sb_(M, F32), "t": sb_(M, F16), "u": sb_(M, F16), "zm": sb_(M, BF),
     "zr": sb_(M, F32), "c2": sb_(16, I32), "c3": sb_(16, I32), "bb": sb_(M, BF), "ybo": sb_(M, F32),
 }
 for _c in "jgw":
     SCRATCH["P" + _c] = sb_(M + 8, F32); SCRATCH["Pm" + _c] = sb_(24, F32); SCRATCH["step" + _c] = sb_(M + 16, BF)
 for _r in range(RO):
-    SCRATCH["sS%d" % _r] = sb_(M, U16); SCRATCH["rS%d" % _r] = sb_(M, U16)
+    SCRATCH["sS%d" % _r] = sb_(2 * M, U16); SCRATCH["rS%d" % _r] = sb_(2 * M, U16)
     SCRATCH["sY%d" % _r] = sb_(E, BF); SCRATCH["rY%d" % _r] = sb_(E, BF)
-    SCRATCH["sF%d" % _r] = sb_(M, BF); SCRATCH["rF%d" % _r] = sb_(M, BF)
-    SCRATCH["sX%d" % _r] = sb_(E, BF); SCRATCH["rX%d" % _r] = sb_(E + M, BF)
+    SCRATCH["sF%d" % _r] = sb_(2 * M, BF); SCRATCH["rF%d" % _r] = sb_(3 * M, BF)
+    SCRATCH["sE%d" % _r] = sb_(2 * M, BF); SCRATCH["rE%d" % _r] = sb_(E + 2 * M, BF)
+SCRATCH.update({"top%d" % _k: sb_(128, BF) for _k in range(1, 17)})
+for _c in "gj":
+    SCRATCH.update({"src" + _c: sb_(192, BF), "Rs" + _c: sb_(192, BF)})
+    SCRATCH.update({_n + _c: sb_(NS, BF) for _n in ("J", "Ja", "M1", "M2", "hold")})
 for _b in range(8):
     SCRATCH["B%d" % _b] = ("psum", [128, 512], F32)
 BUF, PLACE = dict(SCRATCH), {}
-for _d in (F32, BF, I32, U16):
+for _d in (F32, BF, I32, U16, F16):
     _w = 0
     for _n, (_where, _s, _t) in BUF.items():
-        if _where == "sbuf" and _t == _d and _s[1] <= 1024 and _n[1:].rstrip("0123") not in ("S", "Y", "F", "X") and _n not in ("lai", "lwi", "b0i", "thi", "z"):
+        if _where == "sbuf" and _t == _d and _s[1] <= 1024 and _n[1:].rstrip("0123") not in ("S", "Y", "F", "X", "E", "T") and _n not in ("lai", "lwi", "b0i", "thi", "z"):
             PLACE[_n] = ("pk_" + _d, _w); _w += (_s[1] + 15) // 16 * 16
             del SCRATCH[_n]
     SCRATCH["pk_" + _d] = sb_(_w, _d)
 DMAS = ["d_xo0", "d_xo1", "d_xo2", "d_xo3", "d_la", "d_b0", "d_lw", "d_z", "d_th", "d_sb", "d_x0", "d_x1", "o_x", "o_l", "o_w", "o_z", "o_b"]
-SEMAPHORES = ["cV", "cA", "cP", "cG", "sent"] + DMAS + ["a%s%d" % (k, r) for k in "SYFX" for r in range(RO)]
-SIZE = {F32: 4, I32: 4, BF: 2, U16: 2}
+SEMAPHORES = ["cV", "cA", "cP", "cG", "sent"] + DMAS + ["a%s%d" % (k, r) for k in "SYFXETU" for r in range(RO)]
+SIZE = {F32: 4, I32: 4, BF: 2, U16: 2, F16: 2}
 
 
 def R(name, a=None, b=None, step=None, parts=None):
@@ -79,15 +113,17 @@ def width(r):
 
 
 def rank_program(g, core, T, topo):
+    if T.rank_of(core) is not None:
+        program(g, core, T, topo, CFG)
+
+
+def program(g, core, T, topo, C):
     rank = T.rank_of(core)
-    if rank is None:
-        return
     op = AluOpType
     AF = ActivationFunctionType
-    C = CFG
     n = len(T.cores)
     Q = {"V": g.vector, "A": g.scalar, "P": g.tensor, "G": g, "S": g.sync}
-    ops, cur = [], [1e9]
+    ops, cur = [], [0.0, {}, 0.0, "start", 0]
 
     def ap(r):
         if r[0] == "i":
@@ -106,8 +142,10 @@ def rank_program(g, core, T, topo):
                 w.append(o[1]); rd.append(o[2])
             else:
                 w.append(o)
-        ops.append({"q": q, "fn": fn, "w": w, "r": rd, "done": done, "cost": cost, "free": free, "after": after, "also": [], "pr": cur[0],
-                    "sc": any(o[0] == "i" for o in outs)})
+        ops.append({"q": q, "fn": fn, "w": w, "r": rd, "done": done, "cost": cost, "free": free, "after": after, "also": [], "pr": cur[0] + cur[1].get(q, 0.0),
+                    "sc": any(o[0] == "i" for o in outs), "tag": (cur[3], q, cur[1].get((q, 0), 0)), "round": cur[4]})
+        cur[1][q] = cur[1].get(q, 0.0) + cost * cur[2]
+        cur[1][q, 0] = cur[1].get((q, 0), 0) + 1
 
     def cost(o, a, per):
         if a[0] == "i" or o[0] == "i":
@@ -125,7 +163,10 @@ def rank_program(g, core, T, topo):
 
     def tt(o, a, b, f):
         ps = BUF[b[1]][0] == "psum" or (a[0] == "r" and BUF[a[1]][0] == "psum")
-        add("V", lambda: g.vector.tensor_tensor(ap(o), ap(a), ap(b), f), [o], [a, b], cost(o, a, 1 if ps else 2))
+        c = cost(o, a, 1 if ps else 2)
+        if a[0] == "i":
+            c = max(c, 0.05 + width(o) * C["ttg"] * C["cyc"])
+        add("V", lambda: g.vector.tensor_tensor(ap(o), ap(a), ap(b), f), [o], [a, b], c)
 
     def ts(o, a, s1, f1, s2=None, f2=None):
         if f2 is None:
@@ -134,19 +175,28 @@ def rank_program(g, core, T, topo):
             add("V", lambda: g.vector.tensor_scalar(ap(o), ap(a), val(s1), val(s2), f1, f2), [o], [a, s1, s2], cost(o, a, half(o, a)))
 
     def scan(o, d0, d1, f0, f1):
-        add("V", lambda: g.vector.tensor_tensor_scan(ap(o), ap(d0), ap(d1), 0.0, f0, f1), [o], [d0, d1], cost(o, d0, half(o, d0, d1)))
+        add("V", lambda: g.vector.tensor_tensor_scan(ap(o), ap(d0), ap(d1), 0.0, f0, f1), [o], [d0, d1], cost(o, d0, 0.5 if half(o, d0, d1) < 1 else C["scan"]))
 
     def ms(o, c):
         add("V", lambda: g.vector.memset(ap(o), c), [o], [], cost(o, o, 0.5))
 
     def act(o, i, f=None, bias=0.0, scale=1.0):
+        c = cost(o, i, 1) + (C["afix"] - C["fix"] if i[0] == "r" else C["gfix"])
         if f is None:
-            add("A", lambda: g.scalar.activation(ap(o), ap(i), AF.Copy), [o], [i], cost(o, i, 1))
+            add("A", lambda: g.scalar.activation(ap(o), ap(i), AF.Copy), [o], [i], c)
         else:
-            add("A", lambda: g.scalar.activation(ap(o), ap(i), f, bias=bias, scale=scale), [o], [i], cost(o, i, 1))
+            add("A", lambda: g.scalar.activation(ap(o), ap(i), f, bias=bias, scale=scale), [o], [i], c)
+
+    def lin(k, o, i, scale=1.0, bias=0.0, relu=False):
+        if k in C["ona"]:
+            act(o, i, AF.Relu if relu else AF.Identity, bias, scale)
+        elif relu:
+            ts(o, i, bias, op.add, 0.0, op.max)
+        else:
+            ts(o, i, scale, op.mult, bias, op.add)
 
     def mm(o, l, r, st, sp):
-        c = max(min(64, width(l)), width(r)) * (4 if BUF[l[1]][2] == F32 else 1) * C["pe"]
+        c = C["pfix"] + max(min(64, width(l)), width(r)) * (4 if BUF[l[1]][2] == F32 else 1) * C["pe"]
         add("P", lambda: g.tensor.matmul(ap(o), ap(l), ap(r), st, sp), [o], [l, r], c, free=not (st or sp))
 
     def iota(o, pat, base, cm):
@@ -163,19 +213,34 @@ def rank_program(g, core, T, topo):
 
     nsent, sends = [0], {}
 
+    def part(kind, r):
+        if kind in "SU" and C["two"]:
+            return "S%d" % r, 128 * (kind == "U"), 128 * (kind == "U") + 128
+        if kind == "X":
+            return "F%d" % r, M, 2 * M
+        return "%s%d" % (kind, r), 0, E if kind == "Y" else 2 * M if kind == C["xin"] or (kind == "S" and C["t2"]) else M
+
+    def landing(kind, r):
+        nm, a, b = part(kind, r)
+        o = 16 if kind == "E" else 0
+        return R("r" + nm, o + a, o + b)
+
     def send(kind, r, to):
         dst = T.cores[to]
         rid, pid = topo.addr(dst)[:2]
         mask, ne = topo.mask(core, dst), len(topo.engines(core, dst))
-        src, sem = R("s%s%d" % (kind, r)), "a%s%d" % (kind, r)
-        land = R("r%s%d" % (kind, r), 0, src[3])
+        src, sem = R("s" + part(kind, r)[0], *part(kind, r)[1:]), "a%s%d" % (kind, r)
+        land = landing(kind, r)
+        first = 2.0 if not sends else 0.0
         nsent[0] += ne
         sends[kind, r] = len(ops)
-        add("G", lambda: g.remote_dma(ap(land), ap(src), T.sem[sem], T.sem.sent, pid, rid, mask), [], [src], 0.5, ("sent", 0), after=C["lat"] - 0.5)
+        add("G", lambda: g.remote_dma(ap(land), ap(src), T.sem[sem], T.sem.sent, pid, rid, mask), [], [src], C["issue"] + first, ("sent", 0), after=C["lat"] - C["issue"] + (C["ylag"] if kind == "Y" else 0.0))
+        if kind == "S" and C["ylag"]:
+            ops[-1]["also"].append(sends["Y", r])
 
     def arrive(kind, r, frm):
         ne = len(topo.engines(T.cores[frm], core))
-        add(None, None, [R("r%s%d" % (kind, r), 0, BUF["s%s%d" % (kind, r)][1][1])], [], 0.0, ("a%s%d" % (kind, r), ne))
+        add(None, None, [landing(kind, r)], [], 0.0, ("a%s%d" % (kind, r), ne))
         ops[-1]["also"].append(sends[kind, r])
 
     col = lambda j: R("kc", j, j + 1)
@@ -183,354 +248,511 @@ def rank_program(g, core, T, topo):
     row = lambda nm, w=M: R(nm, 0, w, None, 1)
     H = lambda nm, h, o=0: R(nm, 128 * h + o, 128 * h + 128 + o)
     P8 = lambda nm, a, b: R(nm, a, b, None, 8)
-    XA, XW, TW = R("x", 0, A), R("x"), R("tile")
+    XA, XG, XW, TW = R("x", SP, SP + A), R("x", SP, SP + V), R("x"), R("tile", SP, SP + A)
     HH = (0, 1)
+    segs = {c: SEGS[C["blk" + c]] for c in "gj"}
+    ns = {c: sum(2 * w * k for c0, w, k, b0, bs in segs[c]) for c in "gj"}
+    nb = {c: C["blk" + c] // 16 for c in "gj"}
+    ends = lambda nm, s: R(nm, s[0] + s[1] - 1, s[0] + 2 * s[1] * s[2], s[1])
+    blocks = lambda nm, s: R(nm, s[3], 16, s[4])
+    off = lambda nm, a, c: R(nm, 2 * a, 2 * a + nb[c])
+    offs_of = lambda nm, s: R(nm, s[3], 16, 2) if s[4] == 2 else R(nm, 0, 32, 2)
+    N_ = lambda nm, c: R(nm, 0, ns[c])
 
     load("S", R("lai"), T.la[:], "d_la", 2.5)
     load("A", P8("b0i", 0, M), T.b0[:], "d_b0", 2.5)
-    load("S", R("sbi"), T.sb[:], "d_sb", 7.0)
-    load("S", R("x", 0, A), T.xs[:, 0:A], "d_x0", 8.8)
-    load("S", R("z"), T.z0[:], "d_z", 9.0)
-    load("S", R("lwi"), T.lw[:], "d_lw", 9.5)
-    load("S", P8("thi", 0, 1), T.th[:], "d_th", 9.5)
-    load("S", R("x", A, V), T.xs[:, A:V], "d_x1", 11.5)
-    load("S", R("xo0"), T.xs[:, 0:A], "d_xo0", 14.0)
+    load("A", P8("thi", 0, 1), T.th[:], "d_th", 2.5)
+    mb = C["load"]
+    load("S", XA, T.xs[:, 0:A], "d_x0", 2 + 0.63 * mb)
+    load("S", R("z"), T.z0[:], "d_z", 2 + 0.69 * mb)
+    load("S", R("sbi"), T.sb[:], "d_sb", 2 + 1.69 * mb)
+    load("S", R("x", SP + A, SP + V), T.xs[:, A:V], "d_x1", 2 + 2.19 * mb)
+    load("S", R("lwi"), T.lw[:], "d_lw", 2 + 2.32 * mb)
+    load("S", R("xo0"), T.xs[:, 0:A], "d_xo0", 2 + 2.82 * mb)
     nload = len(ops)
 
+    cur[0] = 1
     iota(R("ci2", 0, 2), [[0, 2]], 0, 1)
     iota(R("kio"), [[0, 16], [1, 16]], 0, 0)
     iota(R("tmpa"), [[1, 8], [0, 16]], 0, 0)
-    iota(R("ci3"), [[1, 16]], 0, 0)
     iota(R("tmpb"), [[1, 128]], 0, -1)
-    iota(R("tmpe"), [[1, 144]], 0, 0)
+    iota(R("ci3"), [[1, 16]], 0, 0)
     cur[0] = 5
+    iota(R("lane"), [[1, M]], 0, 0)
+    for c in "gj":
+        c1 = 0
+        for c0, w, k, b0, bs in segs[c]:
+            iota(R("src" + c, c1, c1 + w * k), [[16 * bs, k], [-1, w]], 16 * b0 + 15, -1)
+            iota(R("J" + c, c0, c0 + 2 * w * k), [[0, 2 * k], [1, w]], 0, 0)
+            c1 += w * k
+    cur[0] = 40
+    iota(R("num"), [[1, A]], 0, 0)
+    cur[0] = 2
     ts(R("ci2", 4, 5), R("ci2", 0, 1), 15, op.bitwise_and)
     ts(R("ci2", 5, 6), R("ci2", 0, 1), 4, op.arith_shift_right)
     ts(R("ci2", 6, 7), R("ci2", 0, 1), 0, op.arith_shift_right)
     cp(R("kc", 0, 3), R("ci2", 4, 7))
-    ts(R("kc", 3, 4), col(0), float(V), op.add)
-    ts(R("kc", 4, 5), col(0), float(A), op.add)
-    ts(R("kc", 5, 6), col(0), 0.0, op.is_equal, 1000.0, op.mult)
     ts(R("b8t"), R("tmpa"), col(2), op.is_equal)
-    ts(R("b8"), R("kio", 0, 8), col(1), op.is_equal)
+    ts(R("blk"), R("tmpa"), col(1), op.is_equal)
     ts(R("diag"), R("kio"), col(0), op.is_equal)
     ts(R("id32"), R("tmpb"), 0.0, op.is_equal)
-    ts(R("blk"), R("tmpa"), col(1), op.is_equal)
-    ts(R("kc", 6, 7), col(1), 16.0, op.mult, 16.0, op.add)
-    ts(R("wd"), R("tmpe"), col(6), op.is_equal, col(0), op.mult)
-    for nm, c in (("idb", 1.0), ("id16", 16.0), ("penb", 2.0 ** 18), ("nidb", -1.0), ("hidb", 0.5), ("nbig", -8192.0), ("bigb", 8192.0), ("nid32", -1.0)):
+    act(R("idb"), R("id32"))
+    act(R("M5"), R("diag"), AF.Identity, -4096.0, 4096.0)
+    act(R("hold4"), R("diag"), AF.Identity, 0.0, -8192.0)
+    if C["t2"]:
+        tt(R("ci2", 8, 9), R("ci2", 0, 1), R("ci2", 5, 6), op.add)
+        ts(R("ci2", 9, 10), R("ci2", 0, 1), 15.0, op.add)
+        ts(R("ci2", 10, 11), R("ci2", 8, 9), 1, op.bitwise_and)
+        ts(R("ci2", 11, 12), R("ci2", 9, 10), 15, op.bitwise_and)
+        cp(R("kc", 8, 10), R("ci2", 10, 12))
+        ts(R("kc", 10, 11), col(9), col(0), op.subtract, 16.0, op.add)
+        ts(R("kc", 11, 12), col(10), col(8), op.mult, col(0), op.add)
+        ts(R("kc", 12, 13), col(11), 16.0, op.mult)
+        ts(R("perm"), R("ci3"), col(12), op.add)
+    cur[0] = 5
+    for j, c in ((4, SP + A), (6, 16), (7, SP + A + 16)):
+        ts(R("kc", j, j + 1), col(0), float(c), op.add)
+    ts(R("kc", 5, 6), col(0), 0.0, op.is_equal, 1000.0, op.mult)
+    ts(R("b8"), R("kio", 0, 8), col(1), op.is_equal)
+    for nm, c in (("penb", 2.0 ** 18), ("nidb", -1.0), ("hidb", 0.5), ("nbig", -8192.0), ("nid32", -1.0), ("id6", 24576.0), ("idE", float(M)), ("idm4", -4.0)):
         act(R(nm), R("id32"), AF.Identity, 0.0, c)
-    for nm, c in (("b8s", 2.0 ** -13), ("b8b", 1.0), ("bo16", 16.0), ("bm32", -32.0), ("bm16", -16.0), ("kb8", col(0))):
+    for nm, c in (("bo16", 16.0), ("bm32", -32.0), ("bm16", -16.0), ("kb8", col(0))):
         ts(R(nm), R("b8"), c, op.mult)
-    act(R("nblk"), R("blk"), AF.Identity, 0.0, -1.0)
     cp(R("exp"), R("ci3"))
-    ts(R("last"), R("ci3"), 16.0, op.mult, 15.0, op.add)
     ts(R("exps"), R("ci3"), col(5), op.add, 16.0, op.min)
-    ts(R("ncon"), R("ci3"), 16.0, op.mult, col(0), op.add)
-    ms(R("ones"), 1.0); ms(R("zero"), 0.0); ms(R("ones32"), 1.0); ms(R("two"), 2.0); ms(R("quart"), -0.25)
-    ms(R("x", V, V + 16), 0.0); ms(R("tile", A, A + 16), 0.0)
-    for c in "jgw":
-        ms(R("P" + c, 0, 8), -1.0e9); ms(R("Pm" + c, 16, 24), 1.0e9); ms(R("step" + c, M, M + 16), 0.0)
-    ms(R("OH0", M, E), 0.0); ms(R("OH1", M, E), 0.0); ms(R("DW", 0, E), 0.0); ms(R("Zw", 0, E), 0.0)
-    ms(R("sY0", M, E), -10.0)
+    for nm, c in (("ones", 1.0), ("zero", 0.0), ("ones32", 1.0), ("two", 2.0), ("quart", -0.25), ("c2k", 2048.0), ("c128k", 131072.0),
+                  ("valg", 0.0), ("valj", 0.0)):
+        if BUF[nm][2] == F16:
+            ts(R(nm), R("kio"), 0.0, op.mult)
+        else:
+            ms(R(nm), c)
+    ms(R("x", 0, SP), 0.0); ms(R("tile", 0, SP), 0.0); ms(R("tile", SP + A, 2 * SP + A), 0.0)
+    ms(R("Pj", 0, 8), -1.0e9); ms(R("Pmj", 16, 24), 1.0e9); ms(R("stepj", M, M + 16), 0.0); ms(R("stepw", 0, 16), 0.0)
+    for r in range(RO):
+        ms(R("sE%d" % r, 0, M), 0.0); ms(R("rE%d" % r, 0, 16), 0.0)
+    need = -10.0
+    ms(R("sY0", M, E), need)
     ts(R("e15"), R("kio", 0, 128), 15.0, op.is_equal)
     for j in range(4):
         act(R("r01", M * j, M * j + M), R("kio"), AF.Sign)
     act(R("rbig"), R("r01", 0, M), AF.Identity, 2.0 ** 22, -2.0 ** 22)
-    ts(R("trio"), R("kio"), col(0), op.is_gt, 1.0e6, op.mult)
-    act(R("trix"), R("diag"), AF.Identity, 0.0, 8192.0)
-    tt(R("trix"), R("trix"), R("trio"), op.add)
-    act(R("tmpd"), R("diag"), AF.Identity, 1.0, -2.0)
-    tt(R("rown"), R("tmpd"), R("r01", 0, M), op.mult)
-    act(R("diage"), R("diag"), AF.Identity, 0.0, float(E))
-    cp(P8("thf", 0, 1), P8("thi", 0, 1))
-    ts(P8("thf", 1, 2), P8("thf", 0, 1), 16.0, op.mult)
-    ts(P8("tmpc", 0, 128), P8("kio", 0, 128), P8("thf", 1, 2), op.add)
-    for h in HH:
-        tt(P8("throw", 128 * h, 128 * h + 128), P8("tmpc", 0, 128), P8("b8t", 0, 128), op.mult)
+    act(R("r16"), R("r01", 0, M), AF.Identity, 16.0, -528.0)
+    for c, sh, never in (("g", (2048 + SP) / 8192, op.is_lt), ("j", 0.25, op.is_le)):
+        ts(R("Rs" + c, 0, ns[c] // 2), R("src" + c, 0, ns[c] // 2), 0.0, op.is_equal, 2.0 ** -13, op.mult)
+        ts(N_("Ja" + c, c), N_("J" + c, c), col(0), op.add, 15.0, op.subtract)
+        ts(N_("hold" + c, c), N_("Ja" + c, c), 0.0, op.is_equal, -4.0, op.mult)
+        act(N_("M1" + c, c), N_("hold" + c, c), AF.Identity, -2.0, -(2 + sh) / 4)
+        ts(N_("M2" + c, c), N_("Ja" + c, c), 0.0, never, 128.0, op.mult)
+        ts(N_("M2" + c, c), N_("M2" + c, c), sh, op.max)
+    ts(R("R1", 0, ns["j"] // 2), R("srcj", 0, ns["j"] // 2), 0.0, op.is_equal)
+    ts(R("R2", 0, ns["j"] // 2), R("srcj", 0, ns["j"] // 2), 0.0, op.is_equal, 8192.0, op.mult)
+    act(N_("M3", "j"), N_("holdj", "j"), AF.Identity, -26624.0, (2048 + SP - 8192 + 26624) / -4)
+    act(N_("rseg", "j"), N_("Jj", "j"), AF.Sign)
+    tt(R("M4"), R("diag"), R("lane"), op.mult)
+    tt(R("M4"), R("M4"), R("M5"), op.add)
+    ts(P8("thf", 0, 1), P8("thi", 0, 1), -2048.0, op.add)
+    ts(P8("throw", 0, 128), P8("b8t", 0, 128), P8("thf", 0, 1), op.mult)
+    ms(P8("c16", 0, 128), 16.0)
+    for na in sorted(set(C["a1"] + C["a2"] + C["a4"] + C["a5"]) - {0}):
+        ts(R("tmpt"), R("kio", 0, 128), 15.5 - na, op.is_ge, -16.0, op.mult)
+        tt(R("top%d" % na), R("tmpt"), R("blk"), op.mult)
 
+    def threshold(bank):
+        mm(B(bank), row("ones", 128), row("kio"), True, False)
+        for h in HH:
+            mm(B(bank, 128 * h, 128 * h + 128), P8("c16", 0, 128), P8("throw", 0, 128), False, False)
+
+    cur[0] = 1
     cp(P8("bb", 0, M), P8("b0i", 0, M))
     mm(B(7), P8("b8t", 0, 128), P8("bb", 0, M), True, True)
-    cur[0] = 1
-    cp(R("L"), R("lai")); cp(R("L16"), R("lai"))
-    cur[0] = 5
+    cp(R("L"), R("lai")); cp(R("L16"), R("L"))
     ts(R("OH0", 0, M), B(7), col(0), op.is_equal)
     tt(R("u"), R("OH0", 0, M), R("L"), op.mult)
-    for h in HH:
-        mm(B(4, 8 * h, 8 * h + 8), H("u", h), R("b8"), True, True)
-    cp(R("lbT"), B(4, 0, 16))
+    mm(B(4), R("idb"), R("M5"), True, False)
+    mm(B(4), R("blk"), R("u"), False, True)
+    scan(R("sA"), R("hold4"), B(4), op.add, op.max)
+    ts(R("lbs"), R("sA", 15, M, 16), 2.0 ** -13, op.mult)
+    cur[0] = 30
     cp(R("W"), R("lwi")); cp(R("W16"), R("lwi"))
 
     def bound(r):
-        tt(R("XmB"), IN(R("lbT"), R("exp")), R("diag"), op.mult)
-        act(R("XfB"), IN(R("lbT"), R("exp")))
-        for h in HH:
-            mm(B(4, M + 8 * h, M + 8 * h + 8), H("XmB", h), R("b8s"), True, True)
-        ts(R("lbo"), B(4, M, M + 16), 8192.0, op.mult)
+        ts(R("lbo"), R("lbs"), 8192.0, op.mult)
         act(R("sY%d" % r, 0, M), IN(XA, R("lbo")))
         send("Y", r, (rank + HOPS[r]) % n)
 
+    def tiles(r, win):
+        to = (rank + HOPS[r]) % n
+        if not C["t2"]:
+            for kind in "SU"[:1 + C["two"]]:
+                nm, a, b = part(kind, r)
+                cp(R("s" + nm, a, b), IN(win, R("lbo", a // 16, b // 16)))
+                send(kind, r, to)
+            return
+        get = act if r and C["s32a"] else cp
+        get(R("S32", 0, M), IN(win, R("lbo")))
+        get(R("S32", M, E), IN(win, R("lbo", 0, 1)))
+        for j in HH:
+            o, i = R("TT", M * j, M * j + M), R("S32", 16 * j, 16 * j + M)
+            add("V", lambda o=o, i=i: g.vector.transpose(ap(o), ap(i)), [o], [i], cost(o, i, 1))
+        cp(R("sS%d" % r, M, 2 * M), IN(R("TT"), R("perm")))
+        cp(R("sS%d" % r, 0, M), R("S32", 0, M))
+        send("S", r, to)
+
     def waiting():
         if C["dwv"]:
-            for h in HH:
-                mm(B(7, 128 * h, 128 * h + 128), H("XfB", h), R("id32"), True, True)
-            tt(R("DW", E, E + M), B(7), R("W"), op.subtract)
+            tt(R("DW"), IN(R("num"), R("lbo")), R("W"), op.subtract)
         else:
+            act(R("lbF"), IN(R("num"), R("lbo")))
             mm(B(7), R("nid32"), R("W"), True, False)
-            for h in HH:
-                mm(B(7, 128 * h, 128 * h + 128), H("XfB", h), R("id32"), False, h == 1)
-            act(R("DW", E, E + M), B(7))
+            mm(B(7), R("id32"), R("lbF"), False, True)
+            act(R("DW"), B(7))
 
     cur[0] = 0
     bound(0)
-    cp(R("sS0"), IN(R("sbi"), R("lbo")))
-    send("S", 0, (rank + HOPS[0]) % n)
+    tiles(0, R("sbi"))
     cur[0] = 50
     for j in range(4):
-        cp(R("tile", 512 * j, 512 * j + 512), R("sbi", 512 * j, 512 * j + 512))
+        cp(R("tile", SP + 512 * j, SP + 512 * j + 512), R("sbi", 512 * j, 512 * j + 512))
     waiting()
 
     def raw(buf, win, off, nv, ch):
-        for a in range(0, M, ch):
-            (cp if a < nv else act)(R(buf, 16 * a, 16 * (a + ch)), IN(win, R(off, a, a + ch)))
+        cuts = list(range(0, nv, ch)) + list(range(nv, M, ch)) + [M]
+        for a, b in zip(cuts, cuts[1:]):
+            (cp if a < nv else act)(R(buf, 16 * a, 16 * b), IN(win, R(off, a, b)))
 
-    def score(bank, rawb, minb, yb, wt, other, dist, na, wide):
-        todo = []
+    turnb = [0]
+
+    def score(bank, rawb, minb, yb, wt, other, dist, na, wide, twice=False):
         top = 16 - max(na)
         wide = range(top - min(wide, top), top)
-        for h in HH:
-            src = lambda k: R(rawb, 2048 * h + k, 2048 * h + 2048, 16)
-            dst = lambda k: R(minb, M * k + 128 * h, M * k + 128 * h + 128)
-            far = lambda k, w=1: R(minb, V + 2048 * h + 128 * k, V + 2048 * h + 128 * (k + w))
-            key = lambda k: B(bank, 128 * h + k, 128 * h + 128, 16)
+        held = []
+
+        def flush(stop):
+            o, l, w = held.pop()
+            mm(o, l, w, False, stop)
+            if twice:
+                mm(("r", "B5") + o[2:], l, w, False, stop)
+
+        def emit(o, l, w):
+            if held:
+                flush(False)
+            held.append((o, l, R(w)))
+
+        def onv(h):
             for k in range(16 - na[h]):
+                src, dst = R(rawb, 2048 * h + k, 2048 * h + 2048, 16), R(minb, M * k + 128 * h, M * k + 128 * h + 128)
+                key = B(bank, 128 * h + k, 128 * h + 128, 16)
                 if dist:
-                    todo.append((key(k), src(k), "bo16"))
+                    emit(key, src, "bo16")
                 if k not in wide:
-                    tt(dst(k), src(k), B(yb, 128 * h, 128 * h + 128), op.min)
-                elif h == 0:
+                    tt(dst, src, B(yb, 128 * h, 128 * h + 128), op.min)
+                elif h == 1:
                     tt(R(minb, M * k, M * k + M), R(rawb, k, V, 16), B(yb), op.min)
-                todo.append((key(k), dst(k), wt))
-            for k0 in range(16 - na[h], 16, 4):
-                db = {"miny": (5, 7), "ming": (6, 6), "minw": (5, 6)}[minb][(k0 // 4) % 2]
-                for j in range(4):
-                    mm(B(db, 128 * j, 128 * j + 128), R("nidb"), src(k0 + j), True, False)
-                    mm(B(db, 128 * j, 128 * j + 128), R("idb"), H(other, h), False, True)
-                act(far(k0, 4), B(db, 0, 512), AF.Abs if dist else AF.Relu)
-                for j in range(4):
-                    if na[h] < 16 or not dist:
-                        todo.append((key(k0 + j), H(other, h), "bm16"))
-                    todo.append((key(k0 + j), far(k0 + j), "bo16"))
-        for i, (o, l, w) in enumerate(todo):
-            mm(o, l, R(w), False, i == len(todo) - 1)
+                    emit(B(bank, k, 128, 16), R(minb, M * k, M * k + 128), wt)
+                if k not in wide or h == 1:
+                    emit(key, dst, wt)
 
-    def least(c, bank):
-        scan(R("P" + c, 8, M + 8), R("rbig"), B(bank), op.add, op.min)
-        cp(R("Pm" + c, 0, 16), R("P" + c, 23, M + 8, 16))
-        tt(R("step" + c, 0, M), IN(R("Pm" + c), R("exps")), R("P" + c, 7, M + 7), op.is_equal)
+        def ona(h, k0):
+            ks = range(k0, min(k0 + 4, 16))
+            db = 6 + turnb[0] % 2
+            turnb[0] += 1
+            far = lambda k, w=1: R(minb, V + 2048 * h + 128 * k, V + 2048 * h + 128 * (k + w))
+            for j, k in enumerate(ks):
+                mm(B(db, 128 * j, 128 * j + 128), R("nidb"), R(rawb, 2048 * h + k, 2048 * h + 2048, 16), True, False)
+                mm(B(db, 128 * j, 128 * j + 128), R("idb"), H(other, h), False, True)
+            act(far(k0, len(ks)), B(db, 0, 128 * len(ks)), AF.Abs if dist else AF.Relu)
+            if k0 == 16 - na[h] and (na[h] < 16 or not dist):
+                emit(B(bank, 128 * h, 128 * h + 128), H(other, h), "top%d" % na[h])
+            for k in ks:
+                emit(B(bank, 128 * h + k, 128 * h + 128, 16), far(k), "bo16")
 
-    def turn(bank, src):
-        mm(B(bank), row("ones", 128), row("zero"), True, False)
-        for h in HH:
-            mm(B(bank, 128 * h, 128 * h + 128), H(src, h), R("id32"), False, False)
+        parts = [lambda h=h: onv(h) for h in HH] + [lambda h=h, k0=k0: ona(h, k0) for h in HH for k0 in range(16 - na[h], 16, 4)]
+        return parts, lambda: flush(True)
 
-    def chosen(c, bank, out):
-        mm(B(bank), R("nbig"), R("step" + c, 0, M), False, True)
-        scan(R(out), R("step" + c, 0, M), B(bank), op.mult, op.max)
+    def fused(r, nv, nu):
+        y, offs = R("rY%d" % r, 0, M), lambda a, b: R("rS%d" % r, M + 16 * a, M + 16 * b)
+        keys = []
+        for a in range(nv, 16, C["ch2"]):
+            b = min(a + C["ch2"], 16)
+            act(R("rawg", M * a, M * b), IN(XG, offs(a, b)))
+        for k0 in range(nv + nu, 16, 2):
+            ks = range(k0, min(k0 + 2, 16))
+            db = 6 + turnb[0] % 2
+            turnb[0] += 1
+            mm(B(db, 0, M * len(ks)), R("nidb"), R("rawg", M * k0, M * (k0 + len(ks))), True, False)
+            for j, k in enumerate(ks):
+                mm(B(db, M * j, M * j + M), R("idb"), y, False, k == ks[-1])
+            act(R("ming", M * k0, M * (k0 + len(ks))), B(db, 0, M * len(ks)), AF.Relu)
+        for k in range(16):
+            if k < nv:
+                tt(R("ming", M * k, M * k + M), IN(XG, offs(k, k + 1)), y, op.min)
+            elif k < nv + nu:
+                tt(R("ming", M * k, M * k + M), R("rawg", M * k, M * k + M), B(0), op.min)
+            for h in HH:
+                key = B(2, 128 * h + k, 128 * h + 128, 16)
+                if k >= nv + nu:
+                    keys.insert(0, (key, H(y[1], h), R("bm16")))
+                keys.append((key, H("ming", h, M * k), R("bm16" if k < nv + nu else "bo16")))
+        if "sg" in C["ona"]:
+            threshold(5)
+        for i, (o, l, w) in enumerate(keys):
+            mm(o, l, w, False, i == len(keys) - 1)
+            if "sg" in C["ona"]:
+                mm(("r", "B5") + o[2:], l, w, False, i == len(keys) - 1)
 
-    def onehot(c, bank, o):
-        mm(B(bank, o, o + M), row("e15", 128), row("ones"), True, False)
-        for h in HH:
-            mm(B(bank, o + 128 * h, o + 128 * h + 128), H("step" + c, h, 1), R("idb"), False, False)
-            mm(B(bank, o + 128 * h, o + 128 * h + 128), H("step" + c, h), R("nidb"), False, h == 1)
+    def whole(sc):
+        for p in sc[0]:
+            p()
+        sc[1]()
 
-    def pairs(xm, xf, xn=None):
-        mm(B(6), row("ones", 128), row("zero"), True, False)
-        for h in HH:
-            if xn:
-                mm(B(6, 128 * h, 128 * h + 128), H(xn, h), R("bigb"), False, False)
-            mm(B(6, 128 * h, 128 * h + 128), H(xm, h), R("nblk"), False, False)
-            mm(B(6, 128 * h, 128 * h + 128), H(xf, h), R("id32"), False, h == 1)
+    def pairs(c, both):
+        scan(R("X" + c), R("r01", 0, M), R("val" + c), op.mult, op.add)
+        for bank, m in ((4, "M1"), (5, "M2"))[:1 + both]:
+            mm(B(bank, 0, ns[c]), R("idb"), N_(m + c, c), True, False)
+            spread(bank, "X" + c, "Rs" + c, c, True)
+        scan(N_("U" + c, c), N_("hold" + c, c), B(4, 0, ns[c]), op.add, op.max)
 
-    def slot(out, oh, o):
-        mm(B(4, o, o + 16), R("id16"), R("ncon"), True, False)
-        for b in range(16):
-            mm(B(4, o, o + 16), R("wd", 16 - b, 144 - b), R(oh, b, M, 16), False, b == 15)
-        cp(R(out), B(4, o, o + 16))
+    def spread(bank, src, by, c, stop):
+        c1 = 0
+        for s in segs[c]:
+            w = s[1] * s[2]
+            for h in HH:
+                mm(B(bank, s[0] + w * h, s[0] + w * h + w), H(src, h), R(by, c1, c1 + w), False, stop and h == 1 and s is segs[c][-1])
+            c1 += w
 
-    def count(rY):
-        act(R("sg"), B(2), AF.Sign, 15.5, -1.0)
-        scan(R("cn"), R("r01", 0, M), R("sg"), op.mult, op.add)
+    def count(k, bank):
+        if k in C["ona"]:
+            act(R("sg"), B(bank), AF.Sign, 15.5 - 32768, -1.0)
+            scan(R("cn"), R("r01", 0, M), R("sg"), op.mult, op.add)
+        else:
+            ts(R("sg"), B(2), 15.5 - 32768, op.is_ge, -2.0, op.mult)
+            scan(R("cn"), R("r16"), R("sg"), op.max, op.add)
 
     for r in range(RO):
         lastr = r == RO - 1
         to, frm = (rank + HOPS[r]) % n, (rank - HOPS[r]) % n
-        sX, rX, rY, rS, OH, OHn = "sX%d" % r, "rX%d" % r, "rY%d" % r, "rS%d" % r, "OH%d" % (r % 2), "OH%d" % ((r + 1) % 2)
+        x0, xb = (E, "E") if C["xin"] == "E" else (M, "F")
+        sX, rX, rY, rS, OH, OHn = "s%s%d" % (xb, r), "r%s%d" % (xb, r), "rY%d" % r, "rS%d" % r, "OH%d" % (r % 2), "OH%d" % ((r + 1) % 2)
 
         def pr(k):
-            cur[0] = 100 * r + PR[k]
+            cur[:] = [100 + C["round"] * r + PR[k], {}, C["slope"], k, r]
         pr("rawy")
-        if r == 0:
-            raw("rawy", XA, "L16", C["v1"], C["ch"])
+        raw("rawy", XA, "L16", C["v1"] if r else C["v10"], C["ch"])
         pr("s1")
         mm(B(1), R("idb"), R("z"), True, True)
+        mm(B(1, M, 2 * M), row("ones", 128), row("zero"), True, False)
         mm(B(3), row("ones", 128), row("kio"), True, False)
         for h in HH:
+            mm(B(1, M + 128 * h, M + 128 * h + 128), H("L", h), R("idb"), False, False)
             mm(B(3, 128 * h, 128 * h + 128), H(OH, h), R("penb"), False, False)
-        score(3, "rawy", "miny", 1, "bm32", "z", True, C["abs1"], C["w1"])
-        pr("cj")
-        turn(7, "L")
-        least("j", 3)
-        chosen("j", 7, "selo")
-        onehot("j", 7, M)
-        act(R(OH, E, E + M), B(7, M, 2 * M))
-        tt(R("XmJ"), IN(R("selo"), R("last")), R("diag"), op.mult)
-        for h in HH:
-            mm(B(3, M + 8 * h, M + 8 * h + 8), H("XmJ", h), R("b8s"), True, True)
-        ts(R("ljo"), B(3, M, E), 8192.0, op.mult)
-        act(R(rX, E, E + M), IN(R("xo%d" % (r % 2)), R("ljo")))
-        if not lastr:
-            ts(R("ljs"), B(3, M, E), 1.0, op.add)
-            tt(R("dT"), R("selo", 15, M, 16), R("lbT"), op.subtract)
+        s1 = score(3, "rawy", "miny", 1, "bm32", "z", True, C["a1"], C["w1"])
+        early = 99 if r == 0 else 2 + C["early1"]
+        for p in s1[0][:early]:
+            p()
         pr("s2")
         arrive("Y", r, frm); arrive("S", r, frm)
-        raw("rawg", XW, rS, C["v2"], C["ch"])
-        cp(R("S32"), R(rS))
+        if C["two"]:
+            arrive("U", r, frm)
+        if not C["t2"]:
+            raw("rawg", XG, rS, C["v2"], C["ch"])
         mm(B(0), R("idb"), R(rY, 0, M), True, True)
-        mm(B(2), P8("ones32", 0, 128), P8("throw", 0, M), True, False)
-        turn(4, "S32")
-        score(2, "rawg", "ming", 0, "bm16", rY, False, C["abs2"], C["w2"])
-        pr("cx")
-        act(R("q0"), R(rY, 0, M), AF.Identity, 191.625, 0.25)
-        act(R("q"), R("q0"), AF.Identity, -192.0, 1.0)
-        act(R("nq"), R("q0"), AF.Identity, 192.0, -1.0)
-        least("g", 2)
-        count(rY)
-        tt(R("noc"), R("cn", 15, M, 16), R(rY, M, E), op.is_lt)
-        act(R("XN"), IN(R("noc"), R("exp")))
-        chosen("g", 4, "selg")
-        tt(R("Xm"), IN(R("selg"), R("last")), R("diag"), op.mult)
-        act(R("Xf"), IN(R("selg"), R("last")))
+        threshold(2)
+        pr("sh")
+        ts(R("Sh"), R(rS, 0, M), -2048.0, op.add)
+        mm(B(0, M, 2 * M), row("ones", 128), row("c2k"), True, False)
         for h in HH:
-            mm(B(4, M + 8 * h, M + 8 * h + 8), H("Xm", h), R("b8s"), True, True)
-        pairs("Xm", "Xf", "XN")
-        ts(R("offg"), B(4, M, M + 16), 8192.0, op.mult)
-        tt(R("mx"), IN(XW, R("offg")), R("q"), op.max)
-        tt(R("Z"), B(6), R("trix"), op.is_equal)
-        scan(R("Zs"), R("r01", 0, M), R("Z"), op.mult, op.max)
-        tt(R("uf"), R("Zs", 15, M, 16), B(4, M, M + 16), op.add)
-        ts(R("offs", 0, 32, 2), R("uf"), 8192.0, op.mult, col(3), op.min)
-        for a in range(15, -1, -1):
-            tt(IN(XW, R("offs", 2 * a, 2 * a + 1)), R("mx", 16 * a, 16 * a + 16), R("nq", 16 * a, 16 * a + 16), op.add)
+            mm(B(0, M + 128 * h, M + 128 * h + 128), H("Sh", h), R("idb"), False, False)
+        pr("m2")
+        if C["t2"]:
+            fused(r, C["t2"], C["u2"])
+        else:
+            if "sg" in C["ona"]:
+                threshold(5)
+            whole(score(2, "rawg", "ming", 0, "bm16", rY, False, C["a2"], C["w2"], "sg" in C["ona"]))
+        pr("s1b")
+        for p in s1[0][early:]:
+            p()
+        s1[1]()
+        pr("cx")
+        lin("q0", R("q0"), R(rY, 0, M), 0.25, 191.625)
+        scan(R("Pg", 8, M + 8), R("rbig"), B(2), op.add, op.min)
+        tt(R("stepg", 0, M), R("Pg", 8, M + 8), B(2), op.not_equal)
+        count("sg", 5)
+        mm(B(0, M, 2 * M), R("nbig"), R("stepg", 0, M), False, True)
+        scan(R("selg"), R("stepg", 0, M), B(0, M, 2 * M), op.mult, op.max)
+        tt(R("noc"), R("cn", 15, M, 16), R(rY, M, E), op.is_lt)
+        lin("nocB", R("nocB"), R("noc"), -8192.0, -2048.0)
+        tt(R("valg", 0, M, 16), R("selg", 15, M, 16), R("nocB"), op.add)
+        pairs("g", True)
+        for s in segs["g"]:
+            ts(blocks("offg", s), ends("Ug", s), 8192.0, op.mult, 0.0, op.max)
+        if "t1" in C["ona"]:
+            db = 6 + turnb[0] % 2
+            turnb[0] += 1
+            act(R("t1"), IN(XW, R("offg")))
+            mm(B(db), R("nidb"), R("q0"), True, False)
+            mm(B(db), R("idb"), R("t1"), False, True)
+            lin("new", R("new"), B(db), 1.0, 192.0, True)
+        else:
+            tt(R("t1"), IN(XW, R("offg")), R("q0"), op.subtract)
+            lin("new", R("new"), R("t1"), 1.0, 192.0, True)
+        tt(N_("Z", "g"), N_("Ug", "g"), B(5, 0, ns["g"]), op.not_equal)
+        scan(N_("Zs", "g"), N_("Z", "g"), B(4, 0, ns["g"]), op.mult, op.max)
+        for s in segs["g"]:
+            ts(offs_of("offs", s), ends("Zs", s), 8192.0, op.mult, col(6 if s[3] else 0), op.max)
+        k = 16 * nb["g"]
+        for a in range(M // k - 1, -1, -1):
+            cp(IN(XW, off("offs", a, "g")), R("new", k * a, k * a + k))
         if lastr:
-            store("S", T.yx[:], R("x", 0, V), "o_x", 6.5)
+            store("S", T.yx[:], XG, "o_x", 6.5)
         else:
             xo = R("xo%d" % ((r + 1) % 2))
             add("S", lambda xo=xo: g.sync.dma_start(ap(xo), ap(XA)), [xo], [XA], 0.05, ("d_xo%d" % (r + 1), 16), after=4.0)
+        pr("cj")
+        scan(R("Pj", 8, M + 8), R("rbig"), B(3), op.add, op.min)
+        cp(R("Pmj", 0, 16), R("Pj", 23, M + 8, 16))
+        tt(R("stepj", 0, M), IN(R("Pmj"), R("exps")), R("Pj", 7, M + 7), op.is_equal)
+        mm(B(1, M, 2 * M), R("nbig"), R("stepj", 0, M), False, True)
+        scan(R("selo"), R("stepj", 0, M), B(1, M, 2 * M), op.mult, op.max)
+        mm(B(3, M, 2 * M), row("e15", 128), row("ones"), True, False)
+        for h in HH:
+            mm(B(3, M + 128 * h, M + 128 * h + 128), H("stepj", h, 1), R("idb"), False, False)
+            mm(B(3, M + 128 * h, M + 128 * h + 128), H("stepj", h), R("nidb"), False, h == 1)
+        lin("OH", R(OH, M, 2 * M), B(3, M, 2 * M))
+        ts(R("valj", 0, M, 16), R("selo", 15, M, 16), -2048.0, op.add)
+        pairs("j", not lastr)
+        for s in segs["j"]:
+            ts(blocks("ljo", s), ends("Uj", s), 8192.0, op.mult)
+        act(R(rX, x0 + M, x0 + 2 * M), IN(R("xo%d" % (r % 2)), R("ljo")))
+        if not lastr:
             pr("fill")
-            act(R("XfJ"), IN(R("selo"), R("last")))
+            for s in segs["j"]:
+                tt(blocks("dl", s), ends("Uj", s), blocks("lbs", s), op.subtract)
             act(R("Tj"), IN(TW, R("ljo")))
-            pairs("XmJ", "XfJ")
-            tt(R("Zw", E, E + M), B(6), R("trio"), op.is_equal)
+            tt(N_("Zw", "j"), N_("Uj", "j"), B(5, 0, ns["j"]), op.is_equal)
             if C["dnv"]:
                 tt(R("Dn"), IN(TW, R("lbo")), R("Tj"), op.subtract)
             else:
                 act(R("So"), IN(TW, R("lbo")))
-                mm(B(7), R("id32"), R("So"), True, False)
-                mm(B(7), R("nid32"), R("Tj"), False, True)
-                act(R("Dn"), B(7))
+                mm(B(5), R("id32"), R("So"), True, False)
+                mm(B(5), R("nid32"), R("Tj"), False, True)
+                act(R("Dn"), B(5))
         pr("f")
-        raw("rawg", XW, rS, C["v4"], C["ch"])
+        raw("rawg", XG, rS, C["v4"], C["ch"])
+        pr("fs")
         for a in range(0, V, 16 * C["chq"]):
             scan(R("fsc", a, a + 16 * C["chq"]), R("r01", 0, 16 * C["chq"]), R("rawg", a, a + 16 * C["chq"]), op.mult, op.max)
-        cp(R("sF%d" % r), R("fsc", 15, V, 16))
+        cp(R("sF%d" % r, 0, M), R("fsc", 15, V, 16))
+        keep = list(cur)
+        pr("xs")
+        act(R(sX, M, 2 * M), IN(XW, R("offg")))
+        if C["xin"] == "X":
+            send("X", r, frm)
+        cur[:] = keep
         send("F", r, frm)
         pr("s4")
-        act(R(sX, 0, M), IN(XW, R("offg")))
-        mm(B(2), P8("ones32", 0, 128), P8("throw", 0, M), True, False)
-        score(2, "rawg", "ming", 0, "bm16", rY, False, C["abs4"], C["w4"])
-        count(rY)
-        tt(R("lt"), R("cn", 15, M, 16), R(rY, M, E), op.is_lt)
-        tt(R(sX, M, E), R("lt"), R("noc"), op.max)
-        send("X", r, frm)
+        threshold(2)
+        whole(score(2, "rawg", "ming", 0, "bm16", rY, False, C["a4"], C["w4"]))
+        pr("x4")
+        count("sg4", 2)
+        tt(R("sE%d" % r, 0, M, 16), R("cn", 15, M, 16), R(rY, M, E), op.is_lt)
+        send("E", r, frm)
         pr("raww")
-        raw("raww", XA, "W16", 0, C["ch"])
+        raw("raww", XA, "W16", C["v5"], C["ch"])
         pr("s5")
         arrive("F", r, to)
-        mm(B(1), R("idb"), R("rF%d" % r), True, True)
+        mm(B(1), R("idb"), R("rF%d" % r, 0, M), True, True)
         mm(B(3), row("ones", 128), row("kio"), True, False)
-        score(3, "raww", "minw", 1, "bm32", "rF%d" % r, True, C["abs5"], C["w5"])
-        least("w", 3)
+        mm(B(3), row("ones", 128), row("c128k"), False, False)
+        whole(score(3, "raww", "minw", 1, "bm32", "rF%d" % r, True, C["a5"], C["w5"]))
+        scan(R("Pw", 8, M + 8), R("rbig"), B(3), op.add, op.min)
         pr("ex")
-        arrive("X", r, to)
-        eT = R(rX, M, E)
-        tt(R("XE"), IN(eT, R("exp")), R("diage"), op.mult)
-        mm(B(4, 0, 16), R("idb"), R("ncon"), True, False)
+        if C["xin"] == "X":
+            arrive("X", r, to)
+        arrive("E", r, to)
+        rE = "rE%d" % r
+        eT = R(rE, 16, E, 16)
+        scan(R("XE"), R("r01", 0, M), R(rE, 16, E), op.mult, op.add)
+        if not lastr:
+            mm(B(2, 0, ns["j"]), R("idb"), N_("M3", "j"), True, False)
+            mm(B(2, 0, ns["j"]), R("id6"), N_("Zw", "j"), False, False)
+            spread(2, "Xj", "R1", "j", False)
+            spread(2, "XE", "R2", "j", True)
+        mm(B(4), R("idb"), R("M4"), True, False)
         for h in HH:
-            mm(B(4, 8 * h, 8 * h + 8), H("XE", h), R("b8b"), False, h == 1)
-        cp(R("pick"), B(4, 0, 16))
-        act(R("Ge"), IN(R("DW"), R("pick")))
+            mm(B(4, 128 * h, 128 * h + 128), H("XE", h), R("idE"), False, h == 1)
         if not lastr:
-            act(R("Ze"), IN(R("Zw"), R("pick")))
-            for h in HH:
-                mm(B(4, 16 + 8 * h, 24 + 8 * h), R("two"), R(rX, M, M + 8), True, False)
-                mm(B(4, 16 + 8 * h, 24 + 8 * h), R("two"), R(rX, M + 8, E), False, True)
-            cp(R("c2"), B(4, 16, 32))
-            ts(R("c3"), R("c2"), 2, op.bitwise_and)
-            ts(R("sY%d" % (r + 1), M, E), R("c3"), -10.0, op.add)
-            tt(R("mT"), eT, R("dT"), op.mult)
-            tt(R("lbT"), R("lbT"), R("mT"), op.add)
+            scan(N_("sB", "j"), N_("rseg", "j"), B(2, 0, ns["j"]), op.mult, op.max)
+            for s in segs["j"]:
+                ts(offs_of("offt", s), ends("sB", s), col(6 if s[3] else 0), op.max, col(7 if s[3] else 4), op.min)
+        pr("lb")
+        scan(R("sA"), R("hold4"), B(4), op.add, op.max)
+        cp(R("pick"), R("sA", 15, M, 16))
+        if not lastr:
+            ts(R("el"), R("sA", 15, M, 16), float(M), op.is_ge)
+            tt(R("ml"), R("el"), R("dl"), op.mult)
+            tt(R("lbs"), R("lbs"), R("ml"), op.add)
+            for l, rr in ((row("ones", 128), row("zero", 16)), (R("idm4"), R("par"))):
+                mm(B(0, 0, 16), l, rr, True, False)
+                for h in HH:
+                    mm(B(0, 8 * h, 8 * h + 8), R("two"), R(rE, 16, 144, 16), False, False)
+                    mm(B(0, 8 * h, 8 * h + 8), R("two"), R(rE, 144, E, 16), False, h == 1)
+                if rr[1] == "zero":
+                    lin("par", R("par"), B(0, 0, 16), 0.25, 127.875)
+            lin("par", R("sY%d" % (r + 1), M, E), B(0, 0, 16), 1.0, 512.0 + need)
             bound(r + 1)
-            scan(R("Zt"), R("rown"), R("Ze"), op.mult, op.add)
-            tt(R("ut"), R("ljs"), R("Zt", 15, M, 16), op.subtract)
-            ts(R("offt", 0, 32, 2), R("ut"), 8192.0, op.mult, col(4), op.min)
-        onehot("w", 5, 0)
+        pr("tile")
+        tt(R("Pmw", 0, 16), R("Pw", 23, M + 8, 16), eT, op.mult)
+        tt(R("stepw", 16, E), IN(R("Pmw", 0, 16), R("exp")), R("Pw", 8, M + 8), op.is_equal)
+        mm(B(5), row("ones", 128), row("zero"), True, False)
+        for h in HH:
+            mm(B(5, 128 * h, 128 * h + 128), H(rE, h), R("idb"), False, False)
+        for h in HH:
+            mm(B(5, 128 * h, 128 * h + 128), H("stepw", h, 16), R("idb"), False, False)
+            mm(B(5, 128 * h, 128 * h + 128), H("stepw", h, 15), R("nidb"), False, h == 1)
         if not lastr:
-            pr("pre")
-            raw("rawy", XA, "L16", 0, C["ch"])
-            slot("offb", OH, 288)
-            pr("patch")
-            onehot("w", 6, 0)
-            act(R("ohw"), B(6))
-            slot("offw", "ohw", 304)
-            act(R("vw"), IN(R("raww"), R("offw")))
-            cp(IN(R("rawy"), R("offb")), R("vw"))
-            pr("tile")
             tt(R("nc"), B(5), R("Dn"), op.mult)
-            for a in range(15, -1, -1):
-                tt(IN(TW, R("offt", 2 * a, 2 * a + 1)), R("nc", 16 * a, 16 * a + 16), R("Tj", 16 * a, 16 * a + 16), op.add)
-            cp(R("sS%d" % (r + 1)), IN(TW, R("lbo")))
-            send("S", r + 1, (rank + HOPS[r + 1]) % n)
+            k = 16 * nb["j"]
+            for a in range(M // k - 1, -1, -1):
+                tt(IN(R("tile"), off("offt", a, "j")), R("nc", k * a, k * a + k), R("Tj", k * a, k * a + k), op.add)
+            tiles(r + 1, TW)
         pr("L")
-        tt(R("t"), B(5), R("Ge"), op.mult)
+        tt(R("t"), B(5), R("DW"), op.mult)
         mm(B(2), R("blk"), R("t"), True, True)
         tt(B(2), B(2), R(OH, 0, M), op.mult)
-        tt(R("L"), R("L"), B(2), op.subtract)
-        if r < RO - 2:
+        tt(R("Lo" if lastr else "L"), R("L"), B(2), op.subtract)
+        if not lastr:
             cp(R("L16"), R("L"))
         pr("z")
-        act(R("zm"), IN(R(rX), R("pick")))
+        act(R("zm"), IN(R(rX, x0, x0 + 2 * M), R("pick")))
         act(R(OHn, 0, M), IN(R(OH), R("pick")))
         mm(B(1), row("ones", 128), row("quart"), True, False)
         mm(B(1), R("hidb"), R("z"), False, False)
         mm(B(1), R("hidb"), R("zm"), False, True)
-        act(R("zr"), B(1), AF.Identity, 12582912.0, 1.0)
-        act(R("z"), R("zr"), AF.Identity, -12582912.0, 1.0)
+        if "zr" in C["ona"]:
+            act(R("zr"), B(1), AF.Identity, 12582912.0, 1.0)
+            lin("z", R("z"), R("zr"), 1.0, -12582912.0)
+        else:
+            ts(R("zh"), B(1), 1024.0, op.add)
+            ts(R("z"), R("zh"), -1024.0, op.add)
         pr("W")
+        mm(B(4), R("id32"), R("W"), True, False)
+        mm(B(4), R("idb"), R("t"), False, True)
+        if not lastr:
+            cp(R("W16"), B(4))
+        lin("W", R("W"), B(4))
         if lastr:
-            tt(R("W"), R("W"), R("t"), op.add)
             mm(B(3, 0, M, None, 8), R("kb8"), R(OHn, 0, M), True, True)
             cp(P8("ybo", 0, M), B(3, 0, M, None, 8))
             store("S", T.yz[:], R("z"), "o_z")
             store("A", T.yb[:], P8("ybo", 0, M), "o_b")
             store("S", T.yw[:], R("W"), "o_w")
-            store("A", T.yl[:], R("L"), "o_l")
+            store("A", T.yl[:], R("Lo"), "o_l")
         else:
-            mm(B(5), R("id32"), R("W"), True, False)
-            mm(B(5), R("id32"), R("t"), False, True)
-            cp(R("W16"), B(5))
-            act(R("W"), B(5))
             waiting()
+
+    if C.get("only"):
+        return [(o["cost"], o["after"]) for o in ops]
 
     def meet(a, b):
         return a[2] < b[3] and b[2] < a[3]
@@ -559,8 +781,7 @@ def rank_program(g, core, T, topo):
                         if not (o["free"] and p["free"]):
                             pre.setdefault(j, False)
                     elif meet(x, y) and (kind == "w" or k2 == "w"):
-                        same = p["q"] == q and not p["done"] and not o["done"]
-                        pre[j] = pre.get(j, False) or not same or kind == "r" or C["sameq"]
+                        pre[j] = True
         o["pre"] = pre
         for kind, rs in (("r", o["r"]), ("w", o["w"])):
             for x in rs:
@@ -577,12 +798,9 @@ def rank_program(g, core, T, topo):
     def lag(j, i):
         p = ops[j]
         if ops[i]["pre"][j]:
-            return p["cost"] + p["after"] + C["hop"]
+            return p["cost"] + p["after"] + C["own" if p["q"] == ops[i]["q"] else "hop"]
         return p["cost"] + (p["after"] if ops[i]["q"] is None else 0.0)
 
-    for i in range(len(ops) - 1, -1, -1):
-        o = ops[i]
-        o["rest"] = max([lag(i, k) + ops[k]["rest"] for k in o["post"]] + [o["cost"] + o["after"]])
     N = len(ops)
     true = [[(j, lag(j, i)) for j in ops[i]["pre"]] for i in range(N)]
     room = lambda j, i: C["gap"] if ops[i].get("sc") and ops[j].get("sc") else 0.0
@@ -600,7 +818,15 @@ def rank_program(g, core, T, topo):
             q, c = ops[i]["q"], ops[i]["cost"]
             if q is not None:
                 st, en = line[q]
-                p = int(np.searchsorted(en, t, side="right")) if en and en[-1] > t else len(en)
+                p = len(en)
+                if p and en[-1] > t:
+                    lo = 0
+                    while lo < p:
+                        mid = (lo + p) // 2
+                        if en[mid] > t:
+                            p = mid
+                        else:
+                            lo = mid + 1
                 while p < len(st) and st[p] < t + c - 1e-9:
                     t = max(t, en[p]); p += 1
                 st.insert(p, t); en.insert(p, t + c)
@@ -609,26 +835,136 @@ def rank_program(g, core, T, topo):
 
     for i in range(N - 1, -1, -1):
         ops[i]["pr"] = min([ops[i]["pr"]] + [ops[k]["pr"] for k in ops[i]["post"]])
-    seq = sorted(range(N), key=lambda i: (ops[i]["pr"], i))
-    best = None
-    for it in range(C["iters"]):
+    rest = [0.0] * N
+    for i in range(N - 1, -1, -1):
+        rest[i] = max([lag(i, k) + rest[k] for k in ops[i]["post"]] + [ops[i]["cost"] + ops[i]["after"]])
+    if "dbg" in C:
+        C["dbg"].update(ops=ops, rest=rest, lag=lag)
+    seq = sorted(range(N), key=lambda i: (ops[i]["pr"] * (1 - C["mix"]) - rest[i] * C["mix"] * 3, i))
+    qs = [o["q"] for o in ops]
+    cases = []
+    for case in CASES[:C["cases"]]:
+        D = dict(C, only=True, **case)
+        ca = program(g, core, T, topo, D)
+        edges = [[(j, ca[j][0] + (ca[j][1] + D["own" if qs[j] == qs[i] else "hop"] if w else ca[j][1] if qs[i] is None else 0.0)) for j, w in ops[i]["pre"].items()] for i in range(N)]
+        cases.append((ca, edges, D["weight"]))
+
+    def length(order):
+        total = 0.0
+        for ca, edges, weight in cases:
+            real, free, end = [0.0] * N, dict.fromkeys(list(Q) + [None], 0.0), 0.0
+            for i in order:
+                t = free[qs[i]]
+                for j, d in edges[i]:
+                    if real[j] + d > t:
+                        t = real[j] + d
+                real[i] = t
+                t += ca[i][0]
+                if qs[i]:
+                    free[qs[i]] = t
+                if t + ca[i][1] > end:
+                    end = t + ca[i][1]
+            total += end * weight
+        return total
+
+    def waiting_pairs(order):
+        found = []
+        for ca, edges, weight in cases:
+            real, ready, last, why, end = [0.0] * N, [0.0] * N, {}, [None] * N, (0.0, 0)
+            prev = [None] * N
+            for i in order:
+                t = 0.0
+                for j, d in edges[i]:
+                    if real[j] + d > t:
+                        t, why[i] = real[j] + d, j
+                ready[i], p = t, last.get(qs[i])
+                prev[i] = p
+                if p is not None and real[p] + ca[p][0] > t:
+                    t, why[i] = real[p] + ca[p][0], p
+                real[i] = t
+                if qs[i]:
+                    last[qs[i]] = i
+                end = max(end, (t + ca[i][0] + ca[i][1], i))
+            i = end[1]
+            while why[i] is not None:
+                p = prev[i]
+                while p is not None and real[p] + ca[p][0] > ready[i] + 1e-9:
+                    if p not in ops[i]["pre"]:
+                        found.append((p, i))
+                    p = prev[p]
+                    if len(found) % 6 == 0:
+                        break
+                i = why[i]
+        return found
+
+    def settle(order):
+        ca, edges, weight = cases[0]
+        head, free, end, prev = [0.0] * N, {}, 0.0, [None] * N
+        for i in order:
+            t, p = 0.0, free.get(qs[i])
+            if p is not None:
+                t, prev[i] = head[p] + ca[p][0], p
+            for j, d in edges[i]:
+                if head[j] + d > t:
+                    t = head[j] + d
+            head[i] = t
+            if qs[i] in ("V", "A", "G", "S"):
+                free[qs[i]] = i
+            end = max(end, t + ca[i][0] + ca[i][1])
+        late = [end - ca[i][0] - ca[i][1] for i in range(N)]
+        for i in reversed(order):
+            for j, d in edges[i]:
+                if late[i] - d < late[j]:
+                    late[j] = late[i] - d
+            p = prev[i]
+            if p is not None and late[i] - ca[p][0] < late[p]:
+                late[p] = late[i] - ca[p][0]
+        pos = {i: p for p, i in enumerate(order)}
+        return sorted(order, key=lambda i: (round(head[i] + C["alpha"] * (late[i] - head[i]), 6), pos[i]))
+
+    def tried(seq, best):
         at = place(seq, fwd, [0.0] * N)
         order = sorted(range(N), key=lambda i: (at[i], i))
-        real, free = [0.0] * N, {q: 0.0 for q in Q}
-        for i in order:
-            q = ops[i]["q"]
-            real[i] = max([real[j] + d for j, d in true[i]] + [free.get(q, 0.0)])
-            if q is not None:
-                free[q] = real[i] + ops[i]["cost"]
-        span = max(real[i] + ops[i]["cost"] + ops[i]["after"] for i in range(N))
-        if best is None or span < best[0]:
-            best = (span, order)
-        back = place(sorted(range(N), key=lambda i: (-at[i], -i)), bwd, [o["after"] for o in ops])
-        seq = sorted(range(N), key=lambda i: (-back[i] - ops[i]["cost"], i))
-    order = best[1]
-    C["span"] = best[0]
-    if C.get("dry"):
-        return
+        if C["alpha"]:
+            order = settle(order)
+        span = length(order)
+        return (span, order, at) if best is None or span <= best[0] else best
+
+    name = repr((sorted((k, v) for k, v in C.items() if k not in ("span", "dbg")), sorted(PR.items())))
+    if name not in KEPT:
+        best = tried(seq, None)
+        at = best[2]
+        for it in range(1, C["iters"]):
+            back = place(sorted(range(N), key=lambda i: (-at[i], -i)), bwd, [o["after"] for o in ops])
+            best = tried(sorted(range(N), key=lambda i: (-back[i] - ops[i]["cost"], i)), best)
+        find = {(o["tag"], o["round"]): i for i, o in enumerate(ops)}
+        u, seen, now = C["seed"], None, best
+        for it in range(C["polish"]):
+            if seen is not now:
+                seen, held = now, waiting_pairs(now[1])
+            u = (u * 1103515245 + 12345) % 2 ** 31
+            p0, i0 = held[(u >> 12) % len(held)]
+            order, up = list(now[1]), (u >> 8) % 2
+            for s in (range(-RO, RO) if (u >> 9) % 4 else (0,)):
+                p, i = find.get((ops[p0]["tag"], ops[p0]["round"] + s)), find.get((ops[i0]["tag"], ops[i0]["round"] + s))
+                if p is None or i is None:
+                    continue
+                a, b = order.index(p), order.index(i)
+                if a > b:
+                    continue
+                seg, need = order[a:b + 1], {i if up else p}
+                for x in (reversed(seg) if up else seg):
+                    if not need.isdisjoint(ops[x]["post"] if up else ops[x]["pre"]):
+                        need.add(x)
+                if p not in need or i not in need:
+                    order[a:b + 1] = [x for x in seg if (x in need) == up] + [x for x in seg if (x in need) != up]
+            span = length(order)
+            if span <= now[0] + C["heat"] * (1 - it / C["polish"]) * ((u >> 4) % 16) / 16:
+                now = (span, order)
+                if span < best[0]:
+                    best = now
+        KEPT[name] = best
+    C["span"], order = KEPT[name][:2]
     known = {q: {} for q in Q}
     pos = {i: p for p, i in enumerate(order)}
     for i in order:

import numpy as np
from concourse.mybir import AluOpType, ActivationFunctionType

F32, BF, I32, U16, F16 = "float32", "bfloat16", "int32", "uint16", "float16"
V, A, M, RO = 4096, 2048, 256, 4
HOPS = [1, 2, 3, 1]
E = M + 16
SP = 32
CFG = {"blk": 32, "a1": (16, 4), "a2": (0, 4), "a4": (0, 0), "a5": (0, 4), "early1": 0, "v1": 0, "v2": 64, "v4": 64, "v5": 0, "w1": 0, "w2": 0, "w4": 12, "w5": 4,
       "ch": 32, "chq": 64, "dwv": True, "dnv": True, "gap": 0.1, "iters": 2, "mix": 0.0, "round": 30, "slope": 1.0,
       "cyc": 0.95e-3, "pe": 0.48e-3, "g": 1.56, "sc": 3.8, "hop": 0.08, "fix": 0.0, "lat": 4.2}
PR = {"rawy": -3, "s1": 0, "s1b": 5, "s2": -6, "m2": -5, "cx": -4, "f": 5, "fs": 7, "s4": 9, "x4": 10, "cj": 14, "fill": 16, "raww": 13, "s5": 15,
      "ex": 16, "tile": 16, "lb": 18, "L": 19, "z": 24, "W": 30}
CFG.update({'blk': 32, 'a1': (8, 8), 'a2': (0, 5), 'a4': (0, 4), 'a5': (1, 6), 'early1': 0, 'v1': 96, 'v2': 80, 'v4': 80, 'v5': 0, 'w1': 0, 'w2': 0, 'w4': 0, 'w5': 0, 'ch': 48, 'chq': 32, 'dwv': True, 'dnv': True, 'gap': 0.0, 'cyc': 0.00095, 'hop': 0.1, 'lat': 4.2})
CFG.update(blkg=32, blkj=32, fix=0.05, afix=0.25, gfix=0.015, ona=())
PR.update({'xs': 12, 'rawy': 9, 's1': 0, 's1b': 4, 's2': -6, 'm2': -5, 'cx': -4, 'f': 1, 'fs': 6, 's4': 9, 'x4': 10, 'cj': 25, 'fill': 20, 'raww': 36, 's5': 27, 'ex': 18, 'tile': 18, 'lb': 21, 'L': 27, 'z': 29, 'W': 30})
CFG.update({'a1': (16, 16), 'a2': (4, 8), 'a4': (4, 3), 'a5': (0, 8), 'early1': 0, 'v1': 128, 'v2': 96, 'v4': 80, 'v5': 0, 'w1': 4, 'w2': 4, 'w4': 16, 'w5': 16, 'ch': 64, 'chq': 64, 'dwv': True, 'dnv': True, 'gap': 0.05, 'slope': 0.5, 'cyc': 0.00085, 'hop': 0.06, 'fix': 0.05, 'lat': 4.2, 'blkg': 32, 'blkj': 32, 'noca': False})
PR.update({'rawy': 3, 's1': 21, 's1b': -1, 's2': -8, 'm2': 5, 'cx': -5, 'f': 8, 'fs': 3, 's4': 47, 'x4': 8, 'cj': 12, 'fill': 15, 'raww': 9, 's5': 16, 'ex': 32, 'tile': 19, 'lb': 17, 'L': 14, 'z': 23, 'W': 14, 'xs': 12})
CFG.update({'a1': (12, 12), 'a2': (4, 8), 'a4': (4, 3), 'a5': (1, 8), 'early1': 0, 'v1': 32, 'v2': 112, 'v4': 32, 'v5': 0, 'w1': 4, 'w2': 4, 'w4': 16, 'w5': 16, 'ch': 64, 'chq': 32, 'dwv': True, 'dnv': True, 'gap': 0.1, 'slope': 0, 'cyc': 0.00085, 'hop': 0.07, 'fix': 0.05, 'lat': 3.5, 'blkg': 32, 'blkj': 32, 'ona': ('par',)})
PR.update({'rawy': -9, 's1': 31, 's1b': -2, 's2': -7, 'm2': -2, 'cx': -5, 'f': -4, 'fs': 7, 's4': 39, 'x4': 8, 'cj': 10, 'fill': 15, 'raww': 15, 's5': 13, 'ex': 62, 'tile': 31, 'lb': 16, 'L': 11, 'z': 33, 'W': 27, 'xs': 12})
CFG.update(t2=12, u2=0, ch2=4, s32a=False)
PR.update(sh=-2)
CFG.update(polish=0, seed=1, cases=1, alpha=0.0)
CASES = [{"weight": 1.0},
         {"weight": 1.0, "cyc": 0.83e-3, "pe": 0.40e-3, "g": 1.65, "fix": 0.06, "afix": 0.22, "hop": 0.09, "lat": 4.0},
         {"weight": 0.65, "cyc": 1.3e-3, "pe": 0.65e-3, "g": 1.95, "sc": 5.5, "fix": 0.07, "afix": 0.18, "hop": 0.07, "lat": 4.8}]
CFG.update({'a1': (16, 16), 'a2': (11, 1), 'a4': (4, 4), 'a5': (3, 4), 'early1': 2, 'v1': 64, 'v2': 96, 'v4': 64, 'v5': 0, 'w1': 8, 'w2': 0, 'w4': 16, 'w5': 12, 'ch': 96, 'chq': 64, 'dwv': True, 'dnv': False, 'gap': 0.05, 'slope': 0.5, 'cyc': 0.00095, 'hop': 0.07, 'fix': 0.04, 'lat': 3.5, 'blkg': 32, 'blkj': 32, 'afix': 0.15, 'ona': ('W', 'par', 'q0'), 't2': 12, 'u2': 0, 'ch2': 2, 's32a': True})
PR.update({'rawy': -5, 's1': 22, 's1b': -3, 's2': -3, 'm2': -5, 'cx': -3, 'f': 6, 'fs': 6, 's4': 9, 'x4': 11, 'cj': 19, 'fill': 19, 'raww': 24, 's5': 15, 'ex': 29, 'tile': 23, 'lb': 18, 'L': 16, 'z': 24, 'W': 33, 'xs': 12, 'sh': -11})
CFG.update(ttg=2.0, issue=0.9, t2=0, heat=0.5, two=0, load=3.6, v10=0, early=5, mid=5)
CFG.update({'a1': (15, 12), 'a2': (4, 4), 'a4': (7, 4), 'a5': (2, 6), 'early1': 0, 'v1': 96, 'v2': 96, 'v4': 64, 'v5': 32, 'w1': 16, 'w2': 16, 'w4': 16, 'w5': 8, 'ch': 64, 'chq': 64, 'dwv': True, 'dnv': False, 'gap': 0.0, 'slope': 0, 'cyc': 0.0009, 'hop': 0.07, 'fix': 0.04, 'lat': 5.0, 'blkg': 32, 'blkj': 32, 'afix': 0.16, 'ona': ('W', 'new', 'q0', 't1'), 'two': 0, 'load': 4.2, 'v10': 0})
PR.update({'rawy': -5, 's1': 25, 's1b': 1, 's2': -2, 'm2': -11, 'cx': -6, 'f': 4, 'fs': 3, 's4': 27, 'x4': 7, 'cj': 29, 'fill': 17, 'raww': 18, 's5': 18, 'ex': 28, 'tile': 12, 'lb': 15, 'L': 33, 'z': 12, 'W': 32, 'xs': 13, 'sh': -12})
CFG.update({'a1': (10, 12), 'a2': (4, 8), 'a4': (4, 3), 'a5': (1, 8), 'early1': 0, 'v1': 32, 'v2': 112, 'v4': 32, 'v5': 0, 'w1': 4, 'w2': 16, 'w4': 12, 'w5': 12, 'ch': 64, 'chq': 32, 'dwv': True, 'dnv': True, 'gap': 0.05, 'slope': 0, 'cyc': 0.00085, 'hop': 0.09, 'fix': 0.05, 'lat': 4.2, 'blkg': 32, 'blkj': 32, 'afix': 0.25, 'ona': ('par',), 'ttg': 0, 'issue': 0.6, 'two': 0, 'load': 5.2, 'v10': 0})
PR.update({'rawy': -2, 's1': 31, 's1b': 6, 's2': -15, 'm2': -10, 'cx': -1, 'f': -3, 'fs': 6, 's4': 43, 'x4': 8, 'cj': 10, 'fill': 19, 'raww': 20, 's5': 21, 'ex': 62, 'tile': 38, 'lb': 14, 'L': 10, 'z': 28, 'W': 38, 'xs': 12, 'sh': 0})
CFG.update(own=0.09, scan=1.0, pfix=0.0)
CFG.update({'a1': (16, 16), 'a2': (4, 6), 'a4': (4, 3), 'a5': (0, 8), 'early1': 0, 'v1': 64, 'v2': 128, 'v4': 80, 'v5': 0, 'w1': 16, 'w2': 8, 'w4': 16, 'w5': 8, 'ch': 128, 'chq': 32, 'dwv': True, 'dnv': True, 'gap': 0.1, 'slope': 0, 'cyc': 0.00085, 'pe': 0.00048, 'hop': 0.14, 'fix': 0.04, 'lat': 4.2, 'blkg': 16, 'blkj': 16, 'afix': 0.2, 'gfix': 0.08, 'ona': ('OH', 'W', 'par', 'z', 'zr'), 'ttg': 0, 'issue': 0.9, 'two': 1, 'load': 5.0, 'v10': 32, 'own': 0.08, 'scan': 1.0, 'pfix': 0.02})
PR.update({'rawy': 8, 's1': 27, 's1b': 11, 's2': -1, 'm2': -21, 'cx': 23, 'f': -3, 'fs': 13, 's4': 47, 'x4': -1, 'cj': 31, 'fill': 15, 'raww': 5, 's5': 28, 'ex': 53, 'tile': 31, 'lb': 21, 'L': -1, 'z': 22, 'W': 41, 'xs': 22, 'sh': 8})
CFG.update(xin="F", two=0)
CFG.update({'a1': (12, 9), 'a2': (4, 9), 'a4': (4, 3), 'a5': (1, 8), 'early1': 0, 'v1': 32, 'v2': 112, 'v4': 32, 'v5': 0, 'w1': 0, 'w2': 16, 'w4': 16, 'w5': 12, 'ch': 96, 'chq': 64, 'dwv': True, 'dnv': True, 'gap': 0.0, 'slope': 0, 'cyc': 0.00085, 'pe': 0.00048, 'hop': 0.14, 'fix': 0.04, 'lat': 4.2, 'blkg': 32, 'blkj': 32, 'afix': 0.15, 'gfix': 0.015, 'ona': ('W', 'z'), 'ttg': 0, 'issue': 2.0, 'load': 4.2, 'v10': 0, 'own': 0.03, 'scan': 1.0, 'pfix': 0.0, 'xin': 'E'})
PR.update({'rawy': 1, 's1': 6, 's1b': 12, 's2': 3, 'm2': 9, 'cx': 11, 'f': -13, 'fs': 5, 's4': 54, 'x4': 8, 'cj': 10, 'fill': 15, 'raww': 13, 's5': 12, 'ex': 14, 'tile': 18, 'lb': 16, 'L': 10, 'z': 47, 'W': 42, 'xs': 16, 'sh': 4})
CFG.update(ylag=3.0)
CFG.update({'a1': (12, 12), 'a2': (4, 8), 'a4': (4, 3), 'a5': (1, 8), 'early1': 0, 'v1': 64, 'v2': 112, 'v4': 32, 'v5': 0, 'w1': 4, 'w2': 16, 'w4': 12, 'w5': 16, 'ch': 48, 'chq': 32, 'dwv': True, 'dnv': True, 'gap': 0.0, 'slope': 0, 'cyc': 0.00085, 'pe': 0.0006, 'hop': 0.1, 'fix': 0.06, 'lat': 5.0, 'blkg': 32, 'blkj': 32, 'afix': 0.25, 'gfix': 0.015, 'ona': ('par',), 'ttg': 0, 'issue': 3.0, 'load': 5.0, 'v10': 0, 'own': 0.03, 'scan': 1.0, 'pfix': 0.0, 'xin': 'X', 'ylag': 3.0})
PR.update({'rawy': -5, 's1': 25, 's1b': 4, 's2': -11, 'm2': 8, 'cx': -7, 'f': -4, 'fs': 7, 's4': 45, 'x4': 9, 'cj': 10, 'fill': 7, 'raww': 21, 's5': 0, 'ex': 12, 'tile': 28, 'lb': 8, 'L': 9, 'z': 56, 'W': 26, 'xs': 0, 'sh': -7})
CFG.update({'a1': (8, 8), 'a2': (3, 4), 'a4': (2, 0), 'a5': (2, 8), 'early1': 0, 'v1': 128, 'v2': 96, 'v4': 64, 'v5': 0, 'w1': 0, 'w2': 0, 'w4': 0, 'w5': 4, 'ch': 64, 'chq': 64, 'dwv': True, 'dnv': True, 'gap': 0.0, 'slope': 0, 'cyc': 0.00085, 'pe': 0.00042, 'hop': 0.18, 'fix': 0.0, 'lat': 2.6, 'blkg': 32, 'blkj': 32, 'afix': 0.05, 'gfix': 0.015, 'ona': ('OH', 'W', 'new', 'q0', 'sg', 'z', 'zr'), 'ttg': 0, 'issue': 0.6, 'load': 3.0, 'v10': 32, 'own': 0.24, 'scan': 1.0, 'pfix': 0.0, 'xin': 'X', 'ylag': 0})
PR.update({'rawy': -14, 's1': 29, 's1b': 2, 's2': -5, 'm2': -1, 'cx': 3, 'f': 1, 'fs': 7, 's4': 31, 'x4': 18, 'cj': 28, 'fill': 26, 'raww': 10, 's5': 7, 'ex': 15, 'tile': 11, 'lb': 19, 'L': 30, 'z': 51, 'W': 44, 'xs': 11, 'sh': -7})
KEPT = {}
SEGS = {16: [(0, 16, 8, 0, 1)], 32: [(0, 16, 4, 0, 2), (128, 32, 4, 1, 2)]}
NS = 384


def sb_(w, d):
    return ("sbuf", [128, w], d)


SCRATCH = {
    "x": sb_(V + 32, BF), "xo0": sb_(A, BF), "xo1": sb_(A, BF), "sbi": sb_(A, I32), "tile": sb_(A + 2 * SP, F32), "zh": sb_(M, F16), "r16": sb_(M, BF), "S32": sb_(E, F32), "TT": sb_(2 * M, F32), "perm": sb_(16, U16), "R1": sb_(192, BF), "num": sb_(A, F32),
    "lai": sb_(M, I32), "lwi": sb_(M, I32), "b0i": sb_(M, I32), "thi": sb_(8, I32),
    "L": sb_(M, F16), "Lo": sb_(M, F32), "W": sb_(M, F32), "L16": sb_(M, U16), "W16": sb_(M, U16), "z": sb_(M, BF),
    "rawy": sb_(V, BF), "raww": sb_(V, BF), "rawg": sb_(V, BF), "miny": sb_(2 * V, BF), "minw": sb_(2 * V, BF), "ming": sb_(2 * V, BF), "So": sb_(M, F32), "fsc": sb_(V, BF),
    "ci2": sb_(16, I32), "ci3": sb_(16, I32), "kc": sb_(16, F32), "kio": sb_(M, BF), "ones": sb_(M, BF), "ones32": sb_(128, F32),
    "zero": sb_(M, BF), "e15": sb_(128, BF), "idb": sb_(128, BF), "nidb": sb_(128, BF), "hidb": sb_(128, BF), "id6": sb_(128, BF), "idE": sb_(128, BF),
    "penb": sb_(128, BF), "nbig": sb_(128, BF), "id32": sb_(128, F32), "nid32": sb_(128, F32), "blk": sb_(128, BF),
    "b8": sb_(8, F32), "bo16": sb_(8, BF), "bm32": sb_(8, BF), "bm16": sb_(8, BF), "kb8": sb_(8, BF), "two": sb_(128, BF),
    "b8t": sb_(128, BF), "quart": sb_(M, BF), "c2k": sb_(M, BF), "c128k": sb_(M, BF), "tmpa": sb_(128, F32), "tmpb": sb_(128, F32), "tmpc": sb_(M, F32), "thf": sb_(8, F32), "throw": sb_(128, F16), "c16": sb_(128, BF), "tmpt": sb_(128, BF),
    "diag": sb_(M, BF), "lane": sb_(M, BF), "rbig": sb_(M, F32), "r01": sb_(1024, BF), "exps": sb_(16, U16), "exp": sb_(16, U16),
    "R2": sb_(192, BF), "M3": sb_(NS, BF), "rseg": sb_(NS, BF), "M4": sb_(M, BF), "M5": sb_(M, BF), "hold4": sb_(M, BF), "idm4": sb_(128, BF),
    "selo": sb_(M, F32), "selg": sb_(M, F32), "valg": sb_(M, F16), "valj": sb_(M, F16), "Xg": sb_(M, F16), "Xj": sb_(M, F16), "Ug": sb_(NS, F32), "Uj": sb_(NS, F32),
    "Z": sb_(NS, BF), "Zs": sb_(NS, F32), "Zw": sb_(NS, BF), "sA": sb_(M, F32), "sB": sb_(NS, F32), "XE": sb_(M, BF),
    "sg": sb_(M, BF), "cn": sb_(M, BF), "noc": sb_(16, BF), "nocB": sb_(16, F32), "par": sb_(16, BF), "v": sb_(M, F16), "L32": sb_(M, F32),
    "Sh": sb_(M, F16), "q0": sb_(M, BF), "t1": sb_(M, BF), "new": sb_(M, BF),
    "uf": sb_(16, F32), "ut": sb_(16, F32), "nw": sb_(16, F32), "offg": sb_(16, U16), "offs": sb_(32, U16), "ljo": sb_(16, U16), "ljs": sb_(16, F32), "lbo": sb_(16, U16),
    "offt": sb_(32, U16), "pick": sb_(16, U16), "lbs": sb_(16, F32), "dl": sb_(16, F32), "el": sb_(16, F32), "ml": sb_(16, F32), "Tj": sb_(M, F32), "Dn": sb_(M, F32), "nc": sb_(M, F32),
    "OH0": sb_(2 * M, BF), "OH1": sb_(2 * M, BF), "DW": sb_(M, F32), "lbF": sb_(M, F32), "t": sb_(M, F16), "u": sb_(M, F16), "zm": sb_(M, BF),
    "zr": sb_(M, F32), "c2": sb_(16, I32), "c3": sb_(16, I32), "bb": sb_(M, BF), "ybo": sb_(M, F32),
}
for _c in "jgw":
    SCRATCH["P" + _c] = sb_(M + 8, F32); SCRATCH["Pm" + _c] = sb_(24, F32); SCRATCH["step" + _c] = sb_(M + 16, BF)
for _r in range(RO):
    SCRATCH["sS%d" % _r] = sb_(2 * M, U16); SCRATCH["rS%d" % _r] = sb_(2 * M, U16)
    SCRATCH["sY%d" % _r] = sb_(E, BF); SCRATCH["rY%d" % _r] = sb_(E, BF)
    SCRATCH["sF%d" % _r] = sb_(2 * M, BF); SCRATCH["rF%d" % _r] = sb_(3 * M, BF)
    SCRATCH["sE%d" % _r] = sb_(2 * M, BF); SCRATCH["rE%d" % _r] = sb_(E + 2 * M, BF)
SCRATCH.update({"top%d" % _k: sb_(128, BF) for _k in range(1, 17)})
for _c in "gj":
    SCRATCH.update({"src" + _c: sb_(192, BF), "Rs" + _c: sb_(192, BF)})
    SCRATCH.update({_n + _c: sb_(NS, BF) for _n in ("J", "Ja", "M1", "M2", "hold")})
for _b in range(8):
    SCRATCH["B%d" % _b] = ("psum", [128, 512], F32)
BUF, PLACE = dict(SCRATCH), {}
for _d in (F32, BF, I32, U16, F16):
    _w = 0
    for _n, (_where, _s, _t) in BUF.items():
        if _where == "sbuf" and _t == _d and _s[1] <= 1024 and _n[1:].rstrip("0123") not in ("S", "Y", "F", "X", "E", "T") and _n not in ("lai", "lwi", "b0i", "thi", "z"):
            PLACE[_n] = ("pk_" + _d, _w); _w += (_s[1] + 15) // 16 * 16
            del SCRATCH[_n]
    SCRATCH["pk_" + _d] = sb_(_w, _d)
DMAS = ["d_xo0", "d_xo1", "d_xo2", "d_xo3", "d_la", "d_b0", "d_lw", "d_z", "d_th", "d_sb", "d_x0", "d_x1", "o_x", "o_l", "o_w", "o_z", "o_b"]
SEMAPHORES = ["cV", "cA", "cP", "cG", "sent"] + DMAS + ["a%s%d" % (k, r) for k in "SYFXETU" for r in range(RO)]
SIZE = {F32: 4, I32: 4, BF: 2, U16: 2, F16: 2}


def R(name, a=None, b=None, step=None, parts=None):
    if a is None:
        a, b = 0, BUF[name][1][1]
    return ("r", name, a, b, step, parts)


def IN(win, off):
    return ("i", win, off)


def width(r):
    return 16 * width(r[2]) if r[0] == "i" else len(range(r[2], r[3], r[4] or 1))


def rank_program(g, core, T, topo):
    if T.rank_of(core) is not None:
        program(g, core, T, topo, CFG)


def program(g, core, T, topo, C):
    rank = T.rank_of(core)
    op = AluOpType
    AF = ActivationFunctionType
    n = len(T.cores)
    Q = {"V": g.vector, "A": g.scalar, "P": g.tensor, "G": g, "S": g.sync}
    ops, cur = [], [0.0, {}, 0.0, "start", 0]

    def ap(r):
        if r[0] == "i":
            return ap(r[1]).indirect(ap(r[2]))
        ps = slice(0, r[5]) if r[5] else slice(None)
        nm, o = PLACE.get(r[1], (r[1], 0))
        return T[nm][ps, o + r[2]:o + r[3]:r[4]] if r[4] else T[nm][ps, o + r[2]:o + r[3]]

    def add(q, fn, outs, ins, cost, done=None, free=False, after=0.0):
        w, rd = [], []
        for x in ins:
            if isinstance(x, tuple):
                rd += [x[1], x[2]] if x[0] == "i" else [x]
        for o in outs:
            if o[0] == "i":
                w.append(o[1]); rd.append(o[2])
            else:
                w.append(o)
        ops.append({"q": q, "fn": fn, "w": w, "r": rd, "done": done, "cost": cost, "free": free, "after": after, "also": [], "pr": cur[0] + cur[1].get(q, 0.0),
                    "sc": any(o[0] == "i" for o in outs), "tag": (cur[3], q, cur[1].get((q, 0), 0)), "round": cur[4]})
        cur[1][q] = cur[1].get(q, 0.0) + cost * cur[2]
        cur[1][q, 0] = cur[1].get((q, 0), 0) + 1

    def cost(o, a, per):
        if a[0] == "i" or o[0] == "i":
            return 0.05 + width(o) * C["cyc"] * (C["g"] if a[0] == "i" else C["sc"])
        return C["fix"] + max(64, width(a) * per) * C["cyc"]

    def half(*rs):
        return 0.5 if all(x[0] == "r" and SIZE[BUF[x[1]][2]] == 2 for x in rs) else 1

    def val(s):
        return ap(s) if isinstance(s, tuple) else s

    def cp(o, i):
        add("V", lambda: g.vector.tensor_copy(ap(o), ap(i)), [o], [i], cost(o, i, half(o, i)))

    def tt(o, a, b, f):
        ps = BUF[b[1]][0] == "psum" or (a[0] == "r" and BUF[a[1]][0] == "psum")
        c = cost(o, a, 1 if ps else 2)
        if a[0] == "i":
            c = max(c, 0.05 + width(o) * C["ttg"] * C["cyc"])
        add("V", lambda: g.vector.tensor_tensor(ap(o), ap(a), ap(b), f), [o], [a, b], c)

    def ts(o, a, s1, f1, s2=None, f2=None):
        if f2 is None:
            add("V", lambda: g.vector.tensor_scalar(ap(o), ap(a), val(s1), None, f1), [o], [a, s1], cost(o, a, half(o, a)))
        else:
            add("V", lambda: g.vector.tensor_scalar(ap(o), ap(a), val(s1), val(s2), f1, f2), [o], [a, s1, s2], cost(o, a, half(o, a)))

    def scan(o, d0, d1, f0, f1):
        add("V", lambda: g.vector.tensor_tensor_scan(ap(o), ap(d0), ap(d1), 0.0, f0, f1), [o], [d0, d1], cost(o, d0, 0.5 if half(o, d0, d1) < 1 else C["scan"]))

    def ms(o, c):
        add("V", lambda: g.vector.memset(ap(o), c), [o], [], cost(o, o, 0.5))

    def act(o, i, f=None, bias=0.0, scale=1.0):
        c = cost(o, i, 1) + (C["afix"] - C["fix"] if i[0] == "r" else C["gfix"])
        if f is None:
            add("A", lambda: g.scalar.activation(ap(o), ap(i), AF.Copy), [o], [i], c)
        else:
            add("A", lambda: g.scalar.activation(ap(o), ap(i), f, bias=bias, scale=scale), [o], [i], c)

    def lin(k, o, i, scale=1.0, bias=0.0, relu=False):
        if k in C["ona"]:
            act(o, i, AF.Relu if relu else AF.Identity, bias, scale)
        elif relu:
            ts(o, i, bias, op.add, 0.0, op.max)
        else:
            ts(o, i, scale, op.mult, bias, op.add)

    def mm(o, l, r, st, sp):
        c = C["pfix"] + max(min(64, width(l)), width(r)) * (4 if BUF[l[1]][2] == F32 else 1) * C["pe"]
        add("P", lambda: g.tensor.matmul(ap(o), ap(l), ap(r), st, sp), [o], [l, r], c, free=not (st or sp))

    def iota(o, pat, base, cm):
        if BUF[o[1]][2] == I32:
            add("G", lambda: g.iota(ap(o), pat, base, cm), [o], [], 0.13 + 2 * width(o) * C["cyc"])
        else:
            add("G", lambda: g.iota(ap(o), pat, base, cm, allow_small_or_imprecise_dtypes=True), [o], [], 0.13 + 2 * width(o) * C["cyc"])

    def load(q, o, src, sem, after):
        add(q, lambda: Q[q].dma_start(ap(o), src), [o], [], 0.05, (sem, 16), after=after)

    def store(q, dst, i, sem, after=2.5):
        add(q, lambda: Q[q].dma_start(dst, ap(i)), [], [i], 0.05, (sem, 16), after=after)

    nsent, sends = [0], {}

    def part(kind, r):
        if kind in "SU" and C["two"]:
            return "S%d" % r, 128 * (kind == "U"), 128 * (kind == "U") + 128
        if kind == "X":
            return "F%d" % r, M, 2 * M
        return "%s%d" % (kind, r), 0, E if kind == "Y" else 2 * M if kind == C["xin"] or (kind == "S" and C["t2"]) else M

    def landing(kind, r):
        nm, a, b = part(kind, r)
        o = 16 if kind == "E" else 0
        return R("r" + nm, o + a, o + b)

    def send(kind, r, to):
        dst = T.cores[to]
        rid, pid = topo.addr(dst)[:2]
        mask, ne = topo.mask(core, dst), len(topo.engines(core, dst))
        src, sem = R("s" + part(kind, r)[0], *part(kind, r)[1:]), "a%s%d" % (kind, r)
        land = landing(kind, r)
        first = 2.0 if not sends else 0.0
        nsent[0] += ne
        sends[kind, r] = len(ops)
        add("G", lambda: g.remote_dma(ap(land), ap(src), T.sem[sem], T.sem.sent, pid, rid, mask), [], [src], C["issue"] + first, ("sent", 0), after=C["lat"] - C["issue"] + (C["ylag"] if kind == "Y" else 0.0))
        if kind == "S" and C["ylag"]:
            ops[-1]["also"].append(sends["Y", r])

    def arrive(kind, r, frm):
        ne = len(topo.engines(T.cores[frm], core))
        add(None, None, [landing(kind, r)], [], 0.0, ("a%s%d" % (kind, r), ne))
        ops[-1]["also"].append(sends[kind, r])

    col = lambda j: R("kc", j, j + 1)
    B = lambda b, a=0, e=M, st=None, parts=None: R("B%d" % b, a, e, st, parts)
    row = lambda nm, w=M: R(nm, 0, w, None, 1)
    H = lambda nm, h, o=0: R(nm, 128 * h + o, 128 * h + 128 + o)
    P8 = lambda nm, a, b: R(nm, a, b, None, 8)
    XA, XG, XW, TW = R("x", SP, SP + A), R("x", SP, SP + V), R("x"), R("tile", SP, SP + A)
    HH = (0, 1)
    segs = {c: SEGS[C["blk" + c]] for c in "gj"}
    ns = {c: sum(2 * w * k for c0, w, k, b0, bs in segs[c]) for c in "gj"}
    nb = {c: C["blk" + c] // 16 for c in "gj"}
    ends = lambda nm, s: R(nm, s[0] + s[1] - 1, s[0] + 2 * s[1] * s[2], s[1])
    blocks = lambda nm, s: R(nm, s[3], 16, s[4])
    off = lambda nm, a, c: R(nm, 2 * a, 2 * a + nb[c])
    offs_of = lambda nm, s: R(nm, s[3], 16, 2) if s[4] == 2 else R(nm, 0, 32, 2)
    N_ = lambda nm, c: R(nm, 0, ns[c])

    load("S", R("lai"), T.la[:], "d_la", 2.5)
    load("A", P8("b0i", 0, M), T.b0[:], "d_b0", 2.5)
    load("A", P8("thi", 0, 1), T.th[:], "d_th", 2.5)
    mb = C["load"]
    load("S", XA, T.xs[:, 0:A], "d_x0", 2 + 0.63 * mb)
    load("S", R("z"), T.z0[:], "d_z", 2 + 0.69 * mb)
    load("S", R("sbi"), T.sb[:], "d_sb", 2 + 1.69 * mb)
    load("S", R("x", SP + A, SP + V), T.xs[:, A:V], "d_x1", 2 + 2.19 * mb)
    load("S", R("lwi"), T.lw[:], "d_lw", 2 + 2.32 * mb)
    load("S", R("xo0"), T.xs[:, 0:A], "d_xo0", 2 + 2.82 * mb)
    nload = len(ops)

    cur[0] = 1
    iota(R("ci2", 0, 2), [[0, 2]], 0, 1)
    iota(R("kio"), [[0, 16], [1, 16]], 0, 0)
    iota(R("tmpa"), [[1, 8], [0, 16]], 0, 0)
    iota(R("tmpb"), [[1, 128]], 0, -1)
    iota(R("ci3"), [[1, 16]], 0, 0)
    cur[0] = 5
    iota(R("lane"), [[1, M]], 0, 0)
    for c in "gj":
        c1 = 0
        for c0, w, k, b0, bs in segs[c]:
            iota(R("src" + c, c1, c1 + w * k), [[16 * bs, k], [-1, w]], 16 * b0 + 15, -1)
            iota(R("J" + c, c0, c0 + 2 * w * k), [[0, 2 * k], [1, w]], 0, 0)
            c1 += w * k
    cur[0] = 40
    iota(R("num"), [[1, A]], 0, 0)
    cur[0] = 2
    ts(R("ci2", 4, 5), R("ci2", 0, 1), 15, op.bitwise_and)
    ts(R("ci2", 5, 6), R("ci2", 0, 1), 4, op.arith_shift_right)
    ts(R("ci2", 6, 7), R("ci2", 0, 1), 0, op.arith_shift_right)
    cp(R("kc", 0, 3), R("ci2", 4, 7))
    ts(R("b8t"), R("tmpa"), col(2), op.is_equal)
    ts(R("blk"), R("tmpa"), col(1), op.is_equal)
    ts(R("diag"), R("kio"), col(0), op.is_equal)
    ts(R("id32"), R("tmpb"), 0.0, op.is_equal)
    act(R("idb"), R("id32"))
    act(R("M5"), R("diag"), AF.Identity, -4096.0, 4096.0)
    act(R("hold4"), R("diag"), AF.Identity, 0.0, -8192.0)
    if C["t2"]:
        tt(R("ci2", 8, 9), R("ci2", 0, 1), R("ci2", 5, 6), op.add)
        ts(R("ci2", 9, 10), R("ci2", 0, 1), 15.0, op.add)
        ts(R("ci2", 10, 11), R("ci2", 8, 9), 1, op.bitwise_and)
        ts(R("ci2", 11, 12), R("ci2", 9, 10), 15, op.bitwise_and)
        cp(R("kc", 8, 10), R("ci2", 10, 12))
        ts(R("kc", 10, 11), col(9), col(0), op.subtract, 16.0, op.add)
        ts(R("kc", 11, 12), col(10), col(8), op.mult, col(0), op.add)
        ts(R("kc", 12, 13), col(11), 16.0, op.mult)
        ts(R("perm"), R("ci3"), col(12), op.add)
    cur[0] = 5
    for j, c in ((4, SP + A), (6, 16), (7, SP + A + 16)):
        ts(R("kc", j, j + 1), col(0), float(c), op.add)
    ts(R("kc", 5, 6), col(0), 0.0, op.is_equal, 1000.0, op.mult)
    ts(R("b8"), R("kio", 0, 8), col(1), op.is_equal)
    for nm, c in (("penb", 2.0 ** 18), ("nidb", -1.0), ("hidb", 0.5), ("nbig", -8192.0), ("nid32", -1.0), ("id6", 24576.0), ("idE", float(M)), ("idm4", -4.0)):
        act(R(nm), R("id32"), AF.Identity, 0.0, c)
    for nm, c in (("bo16", 16.0), ("bm32", -32.0), ("bm16", -16.0), ("kb8", col(0))):
        ts(R(nm), R("b8"), c, op.mult)
    cp(R("exp"), R("ci3"))
    ts(R("exps"), R("ci3"), col(5), op.add, 16.0, op.min)
    for nm, c in (("ones", 1.0), ("zero", 0.0), ("ones32", 1.0), ("two", 2.0), ("quart", -0.25), ("c2k", 2048.0), ("c128k", 131072.0),
                  ("valg", 0.0), ("valj", 0.0)):
        if BUF[nm][2] == F16:
            ts(R(nm), R("kio"), 0.0, op.mult)
        else:
            ms(R(nm), c)
    ms(R("x", 0, SP), 0.0); ms(R("tile", 0, SP), 0.0); ms(R("tile", SP + A, 2 * SP + A), 0.0)
    ms(R("Pj", 0, 8), -1.0e9); ms(R("Pmj", 16, 24), 1.0e9); ms(R("stepj", M, M + 16), 0.0); ms(R("stepw", 0, 16), 0.0)
    for r in range(RO):
        ms(R("sE%d" % r, 0, M), 0.0); ms(R("rE%d" % r, 0, 16), 0.0)
    need = -10.0
    ms(R("sY0", M, E), need)
    ts(R("e15"), R("kio", 0, 128), 15.0, op.is_equal)
    for j in range(4):
        act(R("r01", M * j, M * j + M), R("kio"), AF.Sign)
    act(R("rbig"), R("r01", 0, M), AF.Identity, 2.0 ** 22, -2.0 ** 22)
    act(R("r16"), R("r01", 0, M), AF.Identity, 16.0, -528.0)
    for c, sh, never in (("g", (2048 + SP) / 8192, op.is_lt), ("j", 0.25, op.is_le)):
        ts(R("Rs" + c, 0, ns[c] // 2), R("src" + c, 0, ns[c] // 2), 0.0, op.is_equal, 2.0 ** -13, op.mult)
        ts(N_("Ja" + c, c), N_("J" + c, c), col(0), op.add, 15.0, op.subtract)
        ts(N_("hold" + c, c), N_("Ja" + c, c), 0.0, op.is_equal, -4.0, op.mult)
        act(N_("M1" + c, c), N_("hold" + c, c), AF.Identity, -2.0, -(2 + sh) / 4)
        ts(N_("M2" + c, c), N_("Ja" + c, c), 0.0, never, 128.0, op.mult)
        ts(N_("M2" + c, c), N_("M2" + c, c), sh, op.max)
    ts(R("R1", 0, ns["j"] // 2), R("srcj", 0, ns["j"] // 2), 0.0, op.is_equal)
    ts(R("R2", 0, ns["j"] // 2), R("srcj", 0, ns["j"] // 2), 0.0, op.is_equal, 8192.0, op.mult)
    act(N_("M3", "j"), N_("holdj", "j"), AF.Identity, -26624.0, (2048 + SP - 8192 + 26624) / -4)
    act(N_("rseg", "j"), N_("Jj", "j"), AF.Sign)
    tt(R("M4"), R("diag"), R("lane"), op.mult)
    tt(R("M4"), R("M4"), R("M5"), op.add)
    ts(P8("thf", 0, 1), P8("thi", 0, 1), -2048.0, op.add)
    ts(P8("throw", 0, 128), P8("b8t", 0, 128), P8("thf", 0, 1), op.mult)
    ms(P8("c16", 0, 128), 16.0)
    for na in sorted(set(C["a1"] + C["a2"] + C["a4"] + C["a5"]) - {0}):
        ts(R("tmpt"), R("kio", 0, 128), 15.5 - na, op.is_ge, -16.0, op.mult)
        tt(R("top%d" % na), R("tmpt"), R("blk"), op.mult)

    def threshold(bank):
        mm(B(bank), row("ones", 128), row("kio"), True, False)
        for h in HH:
            mm(B(bank, 128 * h, 128 * h + 128), P8("c16", 0, 128), P8("throw", 0, 128), False, False)

    cur[0] = 1
    cp(P8("bb", 0, M), P8("b0i", 0, M))
    mm(B(7), P8("b8t", 0, 128), P8("bb", 0, M), True, True)
    cp(R("L"), R("lai")); cp(R("L16"), R("L"))
    ts(R("OH0", 0, M), B(7), col(0), op.is_equal)
    tt(R("u"), R("OH0", 0, M), R("L"), op.mult)
    mm(B(4), R("idb"), R("M5"), True, False)
    mm(B(4), R("blk"), R("u"), False, True)
    scan(R("sA"), R("hold4"), B(4), op.add, op.max)
    ts(R("lbs"), R("sA", 15, M, 16), 2.0 ** -13, op.mult)
    cur[0] = 30
    cp(R("W"), R("lwi")); cp(R("W16"), R("lwi"))

    def bound(r):
        ts(R("lbo"), R("lbs"), 8192.0, op.mult)
        act(R("sY%d" % r, 0, M), IN(XA, R("lbo")))
        send("Y", r, (rank + HOPS[r]) % n)

    def tiles(r, win):
        to = (rank + HOPS[r]) % n
        if not C["t2"]:
            for kind in "SU"[:1 + C["two"]]:
                nm, a, b = part(kind, r)
                cp(R("s" + nm, a, b), IN(win, R("lbo", a // 16, b // 16)))
                send(kind, r, to)
            return
        get = act if r and C["s32a"] else cp
        get(R("S32", 0, M), IN(win, R("lbo")))
        get(R("S32", M, E), IN(win, R("lbo", 0, 1)))
        for j in HH:
            o, i = R("TT", M * j, M * j + M), R("S32", 16 * j, 16 * j + M)
            add("V", lambda o=o, i=i: g.vector.transpose(ap(o), ap(i)), [o], [i], cost(o, i, 1))
        cp(R("sS%d" % r, M, 2 * M), IN(R("TT"), R("perm")))
        cp(R("sS%d" % r, 0, M), R("S32", 0, M))
        send("S", r, to)

    def waiting():
        if C["dwv"]:
            tt(R("DW"), IN(R("num"), R("lbo")), R("W"), op.subtract)
        else:
            act(R("lbF"), IN(R("num"), R("lbo")))
            mm(B(7), R("nid32"), R("W"), True, False)
            mm(B(7), R("id32"), R("lbF"), False, True)
            act(R("DW"), B(7))

    cur[0] = 0
    bound(0)
    tiles(0, R("sbi"))
    cur[0] = 50
    for j in range(4):
        cp(R("tile", SP + 512 * j, SP + 512 * j + 512), R("sbi", 512 * j, 512 * j + 512))
    waiting()

    def raw(buf, win, off, nv, ch):
        cuts = list(range(0, nv, ch)) + list(range(nv, M, ch)) + [M]
        for a, b in zip(cuts, cuts[1:]):
            (cp if a < nv else act)(R(buf, 16 * a, 16 * b), IN(win, R(off, a, b)))

    turnb = [0]

    def score(bank, rawb, minb, yb, wt, other, dist, na, wide, twice=False):
        top = 16 - max(na)
        wide = range(top - min(wide, top), top)
        held = []

        def flush(stop):
            o, l, w = held.pop()
            mm(o, l, w, False, stop)
            if twice:
                mm(("r", "B5") + o[2:], l, w, False, stop)

        def emit(o, l, w):
            if held:
                flush(False)
            held.append((o, l, R(w)))

        def onv(h):
            for k in range(16 - na[h]):
                src, dst = R(rawb, 2048 * h + k, 2048 * h + 2048, 16), R(minb, M * k + 128 * h, M * k + 128 * h + 128)
                key = B(bank, 128 * h + k, 128 * h + 128, 16)
                if dist:
                    emit(key, src, "bo16")
                if k not in wide:
                    tt(dst, src, B(yb, 128 * h, 128 * h + 128), op.min)
                elif h == 1:
                    tt(R(minb, M * k, M * k + M), R(rawb, k, V, 16), B(yb), op.min)
                    emit(B(bank, k, 128, 16), R(minb, M * k, M * k + 128), wt)
                if k not in wide or h == 1:
                    emit(key, dst, wt)

        def ona(h, k0):
            ks = range(k0, min(k0 + 4, 16))
            db = 6 + turnb[0] % 2
            turnb[0] += 1
            far = lambda k, w=1: R(minb, V + 2048 * h + 128 * k, V + 2048 * h + 128 * (k + w))
            for j, k in enumerate(ks):
                mm(B(db, 128 * j, 128 * j + 128), R("nidb"), R(rawb, 2048 * h + k, 2048 * h + 2048, 16), True, False)
                mm(B(db, 128 * j, 128 * j + 128), R("idb"), H(other, h), False, True)
            act(far(k0, len(ks)), B(db, 0, 128 * len(ks)), AF.Abs if dist else AF.Relu)
            if k0 == 16 - na[h] and (na[h] < 16 or not dist):
                emit(B(bank, 128 * h, 128 * h + 128), H(other, h), "top%d" % na[h])
            for k in ks:
                emit(B(bank, 128 * h + k, 128 * h + 128, 16), far(k), "bo16")

        parts = [lambda h=h: onv(h) for h in HH] + [lambda h=h, k0=k0: ona(h, k0) for h in HH for k0 in range(16 - na[h], 16, 4)]
        return parts, lambda: flush(True)

    def fused(r, nv, nu):
        y, offs = R("rY%d" % r, 0, M), lambda a, b: R("rS%d" % r, M + 16 * a, M + 16 * b)
        keys = []
        for a in range(nv, 16, C["ch2"]):
            b = min(a + C["ch2"], 16)
            act(R("rawg", M * a, M * b), IN(XG, offs(a, b)))
        for k0 in range(nv + nu, 16, 2):
            ks = range(k0, min(k0 + 2, 16))
            db = 6 + turnb[0] % 2
            turnb[0] += 1
            mm(B(db, 0, M * len(ks)), R("nidb"), R("rawg", M * k0, M * (k0 + len(ks))), True, False)
            for j, k in enumerate(ks):
                mm(B(db, M * j, M * j + M), R("idb"), y, False, k == ks[-1])
            act(R("ming", M * k0, M * (k0 + len(ks))), B(db, 0, M * len(ks)), AF.Relu)
        for k in range(16):
            if k < nv:
                tt(R("ming", M * k, M * k + M), IN(XG, offs(k, k + 1)), y, op.min)
            elif k < nv + nu:
                tt(R("ming", M * k, M * k + M), R("rawg", M * k, M * k + M), B(0), op.min)
            for h in HH:
                key = B(2, 128 * h + k, 128 * h + 128, 16)
                if k >= nv + nu:
                    keys.insert(0, (key, H(y[1], h), R("bm16")))
                keys.append((key, H("ming", h, M * k), R("bm16" if k < nv + nu else "bo16")))
        if "sg" in C["ona"]:
            threshold(5)
        for i, (o, l, w) in enumerate(keys):
            mm(o, l, w, False, i == len(keys) - 1)
            if "sg" in C["ona"]:
                mm(("r", "B5") + o[2:], l, w, False, i == len(keys) - 1)

    def whole(sc):
        for p in sc[0]:
            p()
        sc[1]()

    def pairs(c, both):
        scan(R("X" + c), R("r01", 0, M), R("val" + c), op.mult, op.add)
        for bank, m in ((4, "M1"), (5, "M2"))[:1 + both]:
            mm(B(bank, 0, ns[c]), R("idb"), N_(m + c, c), True, False)
            spread(bank, "X" + c, "Rs" + c, c, True)
        scan(N_("U" + c, c), N_("hold" + c, c), B(4, 0, ns[c]), op.add, op.max)

    def spread(bank, src, by, c, stop):
        c1 = 0
        for s in segs[c]:
            w = s[1] * s[2]
            for h in HH:
                mm(B(bank, s[0] + w * h, s[0] + w * h + w), H(src, h), R(by, c1, c1 + w), False, stop and h == 1 and s is segs[c][-1])
            c1 += w

    def count(k, bank):
        if k in C["ona"]:
            act(R("sg"), B(bank), AF.Sign, 15.5 - 32768, -1.0)
            scan(R("cn"), R("r01", 0, M), R("sg"), op.mult, op.add)
        else:
            ts(R("sg"), B(2), 15.5 - 32768, op.is_ge, -2.0, op.mult)
            scan(R("cn"), R("r16"), R("sg"), op.max, op.add)

    for r in range(RO):
        lastr = r == RO - 1
        to, frm = (rank + HOPS[r]) % n, (rank - HOPS[r]) % n
        x0, xb = (E, "E") if C["xin"] == "E" else (M, "F")
        sX, rX, rY, rS, OH, OHn = "s%s%d" % (xb, r), "r%s%d" % (xb, r), "rY%d" % r, "rS%d" % r, "OH%d" % (r % 2), "OH%d" % ((r + 1) % 2)

        def pr(k):
            cur[:] = [100 + C["round"] * r + PR[k], {}, C["slope"], k, r]
        pr("rawy")
        raw("rawy", XA, "L16", C["v1"] if r else C["v10"], C["ch"])
        pr("s1")
        mm(B(1), R("idb"), R("z"), True, True)
        mm(B(1, M, 2 * M), row("ones", 128), row("zero"), True, False)
        mm(B(3), row("ones", 128), row("kio"), True, False)
        for h in HH:
            mm(B(1, M + 128 * h, M + 128 * h + 128), H("L", h), R("idb"), False, False)
            mm(B(3, 128 * h, 128 * h + 128), H(OH, h), R("penb"), False, False)
        s1 = score(3, "rawy", "miny", 1, "bm32", "z", True, C["a1"], C["w1"])
        early = 99 if r == 0 else 2 + C["early1"]
        for p in s1[0][:early]:
            p()
        pr("s2")
        arrive("Y", r, frm); arrive("S", r, frm)
        if C["two"]:
            arrive("U", r, frm)
        if not C["t2"]:
            raw("rawg", XG, rS, C["v2"], C["ch"])
        mm(B(0), R("idb"), R(rY, 0, M), True, True)
        threshold(2)
        pr("sh")
        ts(R("Sh"), R(rS, 0, M), -2048.0, op.add)
        mm(B(0, M, 2 * M), row("ones", 128), row("c2k"), True, False)
        for h in HH:
            mm(B(0, M + 128 * h, M + 128 * h + 128), H("Sh", h), R("idb"), False, False)
        pr("m2")
        if C["t2"]:
            fused(r, C["t2"], C["u2"])
        else:
            if "sg" in C["ona"]:
                threshold(5)
            whole(score(2, "rawg", "ming", 0, "bm16", rY, False, C["a2"], C["w2"], "sg" in C["ona"]))
        pr("s1b")
        for p in s1[0][early:]:
            p()
        s1[1]()
        pr("cx")
        lin("q0", R("q0"), R(rY, 0, M), 0.25, 191.625)
        scan(R("Pg", 8, M + 8), R("rbig"), B(2), op.add, op.min)
        tt(R("stepg", 0, M), R("Pg", 8, M + 8), B(2), op.not_equal)
        count("sg", 5)
        mm(B(0, M, 2 * M), R("nbig"), R("stepg", 0, M), False, True)
        scan(R("selg"), R("stepg", 0, M), B(0, M, 2 * M), op.mult, op.max)
        tt(R("noc"), R("cn", 15, M, 16), R(rY, M, E), op.is_lt)
        lin("nocB", R("nocB"), R("noc"), -8192.0, -2048.0)
        tt(R("valg", 0, M, 16), R("selg", 15, M, 16), R("nocB"), op.add)
        pairs("g", True)
        for s in segs["g"]:
            ts(blocks("offg", s), ends("Ug", s), 8192.0, op.mult, 0.0, op.max)
        if "t1" in C["ona"]:
            db = 6 + turnb[0] % 2
            turnb[0] += 1
            act(R("t1"), IN(XW, R("offg")))
            mm(B(db), R("nidb"), R("q0"), True, False)
            mm(B(db), R("idb"), R("t1"), False, True)
            lin("new", R("new"), B(db), 1.0, 192.0, True)
        else:
            tt(R("t1"), IN(XW, R("offg")), R("q0"), op.subtract)
            lin("new", R("new"), R("t1"), 1.0, 192.0, True)
        tt(N_("Z", "g"), N_("Ug", "g"), B(5, 0, ns["g"]), op.not_equal)
        scan(N_("Zs", "g"), N_("Z", "g"), B(4, 0, ns["g"]), op.mult, op.max)
        for s in segs["g"]:
            ts(offs_of("offs", s), ends("Zs", s), 8192.0, op.mult, col(6 if s[3] else 0), op.max)
        k = 16 * nb["g"]
        for a in range(M // k - 1, -1, -1):
            cp(IN(XW, off("offs", a, "g")), R("new", k * a, k * a + k))
        if lastr:
            store("S", T.yx[:], XG, "o_x", 6.5)
        else:
            xo = R("xo%d" % ((r + 1) % 2))
            add("S", lambda xo=xo: g.sync.dma_start(ap(xo), ap(XA)), [xo], [XA], 0.05, ("d_xo%d" % (r + 1), 16), after=4.0)
        pr("cj")
        scan(R("Pj", 8, M + 8), R("rbig"), B(3), op.add, op.min)
        cp(R("Pmj", 0, 16), R("Pj", 23, M + 8, 16))
        tt(R("stepj", 0, M), IN(R("Pmj"), R("exps")), R("Pj", 7, M + 7), op.is_equal)
        mm(B(1, M, 2 * M), R("nbig"), R("stepj", 0, M), False, True)
        scan(R("selo"), R("stepj", 0, M), B(1, M, 2 * M), op.mult, op.max)
        mm(B(3, M, 2 * M), row("e15", 128), row("ones"), True, False)
        for h in HH:
            mm(B(3, M + 128 * h, M + 128 * h + 128), H("stepj", h, 1), R("idb"), False, False)
            mm(B(3, M + 128 * h, M + 128 * h + 128), H("stepj", h), R("nidb"), False, h == 1)
        lin("OH", R(OH, M, 2 * M), B(3, M, 2 * M))
        ts(R("valj", 0, M, 16), R("selo", 15, M, 16), -2048.0, op.add)
        pairs("j", not lastr)
        for s in segs["j"]:
            ts(blocks("ljo", s), ends("Uj", s), 8192.0, op.mult)
        act(R(rX, x0 + M, x0 + 2 * M), IN(R("xo%d" % (r % 2)), R("ljo")))
        if not lastr:
            pr("fill")
            for s in segs["j"]:
                tt(blocks("dl", s), ends("Uj", s), blocks("lbs", s), op.subtract)
            act(R("Tj"), IN(TW, R("ljo")))
            tt(N_("Zw", "j"), N_("Uj", "j"), B(5, 0, ns["j"]), op.is_equal)
            if C["dnv"]:
                tt(R("Dn"), IN(TW, R("lbo")), R("Tj"), op.subtract)
            else:
                act(R("So"), IN(TW, R("lbo")))
                mm(B(5), R("id32"), R("So"), True, False)
                mm(B(5), R("nid32"), R("Tj"), False, True)
                act(R("Dn"), B(5))
        pr("f")
        raw("rawg", XG, rS, C["v4"], C["ch"])
        pr("fs")
        for a in range(0, V, 16 * C["chq"]):
            scan(R("fsc", a, a + 16 * C["chq"]), R("r01", 0, 16 * C["chq"]), R("rawg", a, a + 16 * C["chq"]), op.mult, op.max)
        cp(R("sF%d" % r, 0, M), R("fsc", 15, V, 16))
        keep = list(cur)
        pr("xs")
        act(R(sX, M, 2 * M), IN(XW, R("offg")))
        if C["xin"] == "X":
            send("X", r, frm)
        cur[:] = keep
        send("F", r, frm)
        pr("s4")
        threshold(2)
        whole(score(2, "rawg", "ming", 0, "bm16", rY, False, C["a4"], C["w4"]))
        pr("x4")
        count("sg4", 2)
        tt(R("sE%d" % r, 0, M, 16), R("cn", 15, M, 16), R(rY, M, E), op.is_lt)
        send("E", r, frm)
        pr("raww")
        raw("raww", XA, "W16", C["v5"], C["ch"])
        pr("s5")
        arrive("F", r, to)
        mm(B(1), R("idb"), R("rF%d" % r, 0, M), True, True)
        mm(B(3), row("ones", 128), row("kio"), True, False)
        mm(B(3), row("ones", 128), row("c128k"), False, False)
        whole(score(3, "raww", "minw", 1, "bm32", "rF%d" % r, True, C["a5"], C["w5"]))
        scan(R("Pw", 8, M + 8), R("rbig"), B(3), op.add, op.min)
        pr("ex")
        if C["xin"] == "X":
            arrive("X", r, to)
        arrive("E", r, to)
        rE = "rE%d" % r
        eT = R(rE, 16, E, 16)
        scan(R("XE"), R("r01", 0, M), R(rE, 16, E), op.mult, op.add)
        if not lastr:
            mm(B(2, 0, ns["j"]), R("idb"), N_("M3", "j"), True, False)
            mm(B(2, 0, ns["j"]), R("id6"), N_("Zw", "j"), False, False)
            spread(2, "Xj", "R1", "j", False)
            spread(2, "XE", "R2", "j", True)
        mm(B(4), R("idb"), R("M4"), True, False)
        for h in HH:
            mm(B(4, 128 * h, 128 * h + 128), H("XE", h), R("idE"), False, h == 1)
        if not lastr:
            scan(N_("sB", "j"), N_("rseg", "j"), B(2, 0, ns["j"]), op.mult, op.max)
            for s in segs["j"]:
                ts(offs_of("offt", s), ends("sB", s), col(6 if s[3] else 0), op.max, col(7 if s[3] else 4), op.min)
        pr("lb")
        scan(R("sA"), R("hold4"), B(4), op.add, op.max)
        cp(R("pick"), R("sA", 15, M, 16))
        if not lastr:
            ts(R("el"), R("sA", 15, M, 16), float(M), op.is_ge)
            tt(R("ml"), R("el"), R("dl"), op.mult)
            tt(R("lbs"), R("lbs"), R("ml"), op.add)
            for l, rr in ((row("ones", 128), row("zero", 16)), (R("idm4"), R("par"))):
                mm(B(0, 0, 16), l, rr, True, False)
                for h in HH:
                    mm(B(0, 8 * h, 8 * h + 8), R("two"), R(rE, 16, 144, 16), False, False)
                    mm(B(0, 8 * h, 8 * h + 8), R("two"), R(rE, 144, E, 16), False, h == 1)
                if rr[1] == "zero":
                    lin("par", R("par"), B(0, 0, 16), 0.25, 127.875)
            lin("par", R("sY%d" % (r + 1), M, E), B(0, 0, 16), 1.0, 512.0 + need)
            bound(r + 1)
        pr("tile")
        tt(R("Pmw", 0, 16), R("Pw", 23, M + 8, 16), eT, op.mult)
        tt(R("stepw", 16, E), IN(R("Pmw", 0, 16), R("exp")), R("Pw", 8, M + 8), op.is_equal)
        mm(B(5), row("ones", 128), row("zero"), True, False)
        for h in HH:
            mm(B(5, 128 * h, 128 * h + 128), H(rE, h), R("idb"), False, False)
        for h in HH:
            mm(B(5, 128 * h, 128 * h + 128), H("stepw", h, 16), R("idb"), False, False)
            mm(B(5, 128 * h, 128 * h + 128), H("stepw", h, 15), R("nidb"), False, h == 1)
        if not lastr:
            tt(R("nc"), B(5), R("Dn"), op.mult)
            k = 16 * nb["j"]
            for a in range(M // k - 1, -1, -1):
                tt(IN(R("tile"), off("offt", a, "j")), R("nc", k * a, k * a + k), R("Tj", k * a, k * a + k), op.add)
            tiles(r + 1, TW)
        pr("L")
        tt(R("t"), B(5), R("DW"), op.mult)
        mm(B(2), R("blk"), R("t"), True, True)
        tt(B(2), B(2), R(OH, 0, M), op.mult)
        tt(R("Lo" if lastr else "L"), R("L"), B(2), op.subtract)
        if not lastr:
            cp(R("L16"), R("L"))
        pr("z")
        act(R("zm"), IN(R(rX, x0, x0 + 2 * M), R("pick")))
        act(R(OHn, 0, M), IN(R(OH), R("pick")))
        mm(B(1), row("ones", 128), row("quart"), True, False)
        mm(B(1), R("hidb"), R("z"), False, False)
        mm(B(1), R("hidb"), R("zm"), False, True)
        if "zr" in C["ona"]:
            act(R("zr"), B(1), AF.Identity, 12582912.0, 1.0)
            lin("z", R("z"), R("zr"), 1.0, -12582912.0)
        else:
            ts(R("zh"), B(1), 1024.0, op.add)
            ts(R("z"), R("zh"), -1024.0, op.add)
        pr("W")
        mm(B(4), R("id32"), R("W"), True, False)
        mm(B(4), R("idb"), R("t"), False, True)
        if not lastr:
            cp(R("W16"), B(4))
        lin("W", R("W"), B(4))
        if lastr:
            mm(B(3, 0, M, None, 8), R("kb8"), R(OHn, 0, M), True, True)
            cp(P8("ybo", 0, M), B(3, 0, M, None, 8))
            store("S", T.yz[:], R("z"), "o_z")
            store("A", T.yb[:], P8("ybo", 0, M), "o_b")
            store("S", T.yw[:], R("W"), "o_w")
            store("A", T.yl[:], R("Lo"), "o_l")
        else:
            waiting()

    if C.get("only"):
        return [(o["cost"], o["after"]) for o in ops]

    def meet(a, b):
        return a[2] < b[3] and b[2] < a[3]

    acc, era = {}, {}
    for i, o in enumerate(ops):
        q = o["q"]
        o["key"] = o["done"][0] if o["done"] else "c" + q
        pre = {j: False for j in o["also"]}
        if 0 < i < nload:
            pre[i - 1] = False
        for kind, rs in (("r", o["r"]), ("w", o["w"])):
            for x in rs:
                psum = BUF[x[1]][0] == "psum"
                if psum:
                    e = era.setdefault(x[1], [q, []])
                    if e[0] != q:
                        e[0], e[1], acc[x[1]] = q, [j for j, k2, y in acc[x[1]]], []
                    for j in e[1]:
                        pre[j] = True
                for (j, k2, y) in acc.get(x[1], []):
                    p = ops[j]
                    if j == i:
                        continue
                    if psum and q == "P":
                        if not (o["free"] and p["free"]):
                            pre.setdefault(j, False)
                    elif meet(x, y) and (kind == "w" or k2 == "w"):
                        pre[j] = True
        o["pre"] = pre
        for kind, rs in (("r", o["r"]), ("w", o["w"])):
            for x in rs:
                lst = acc.setdefault(x[1], [])
                if kind == "w" and not x[4] and not x[5] and BUF[x[1]][0] != "psum":
                    lst[:] = [e for e in lst if not (x[2] <= e[2][2] and e[2][3] <= x[3])]
                lst.append((i, kind, x))
    for i, o in enumerate(ops):
        o["post"] = []
    for i, o in enumerate(ops):
        for j in o["pre"]:
            ops[j]["post"].append(i)

    def lag(j, i):
        p = ops[j]
        if ops[i]["pre"][j]:
            return p["cost"] + p["after"] + C["own" if p["q"] == ops[i]["q"] else "hop"]
        return p["cost"] + (p["after"] if ops[i]["q"] is None else 0.0)

    N = len(ops)
    true = [[(j, lag(j, i)) for j in ops[i]["pre"]] for i in range(N)]
    room = lambda j, i: C["gap"] if ops[i].get("sc") and ops[j].get("sc") else 0.0
    fwd = [[(j, lag(j, i) + room(j, i)) for j in ops[i]["pre"]] for i in range(N)]
    bwd = [[(k, lag(i, k) + room(i, k) + ops[k]["cost"] - ops[i]["cost"]) for k in ops[i]["post"]] for i in range(N)]

    def place(seq, edges, first):
        at = [0.0] * N
        line = {q: ([], []) for q in Q}
        for i in seq:
            t = first[i]
            for j, d in edges[i]:
                if at[j] + d > t:
                    t = at[j] + d
            q, c = ops[i]["q"], ops[i]["cost"]
            if q is not None:
                st, en = line[q]
                p = len(en)
                if p and en[-1] > t:
                    lo = 0
                    while lo < p:
                        mid = (lo + p) // 2
                        if en[mid] > t:
                            p = mid
                        else:
                            lo = mid + 1
                while p < len(st) and st[p] < t + c - 1e-9:
                    t = max(t, en[p]); p += 1
                st.insert(p, t); en.insert(p, t + c)
            at[i] = t
        return at

    for i in range(N - 1, -1, -1):
        ops[i]["pr"] = min([ops[i]["pr"]] + [ops[k]["pr"] for k in ops[i]["post"]])
    rest = [0.0] * N
    for i in range(N - 1, -1, -1):
        rest[i] = max([lag(i, k) + rest[k] for k in ops[i]["post"]] + [ops[i]["cost"] + ops[i]["after"]])
    if "dbg" in C:
        C["dbg"].update(ops=ops, rest=rest, lag=lag)
    seq = sorted(range(N), key=lambda i: (ops[i]["pr"] * (1 - C["mix"]) - rest[i] * C["mix"] * 3, i))
    qs = [o["q"] for o in ops]
    cases = []
    for case in CASES[:C["cases"]]:
        D = dict(C, only=True, **case)
        ca = program(g, core, T, topo, D)
        edges = [[(j, ca[j][0] + (ca[j][1] + D["own" if qs[j] == qs[i] else "hop"] if w else ca[j][1] if qs[i] is None else 0.0)) for j, w in ops[i]["pre"].items()] for i in range(N)]
        cases.append((ca, edges, D["weight"]))

    def length(order):
        total = 0.0
        for ca, edges, weight in cases:
            real, free, end = [0.0] * N, dict.fromkeys(list(Q) + [None], 0.0), 0.0
            for i in order:
                t = free[qs[i]]
                for j, d in edges[i]:
                    if real[j] + d > t:
                        t = real[j] + d
                real[i] = t
                t += ca[i][0]
                if qs[i]:
                    free[qs[i]] = t
                if t + ca[i][1] > end:
                    end = t + ca[i][1]
            total += end * weight
        return total

    def waiting_pairs(order):
        found = []
        for ca, edges, weight in cases:
            real, ready, last, why, end = [0.0] * N, [0.0] * N, {}, [None] * N, (0.0, 0)
            prev = [None] * N
            for i in order:
                t = 0.0
                for j, d in edges[i]:
                    if real[j] + d > t:
                        t, why[i] = real[j] + d, j
                ready[i], p = t, last.get(qs[i])
                prev[i] = p
                if p is not None and real[p] + ca[p][0] > t:
                    t, why[i] = real[p] + ca[p][0], p
                real[i] = t
                if qs[i]:
                    last[qs[i]] = i
                end = max(end, (t + ca[i][0] + ca[i][1], i))
            i = end[1]
            while why[i] is not None:
                p = prev[i]
                while p is not None and real[p] + ca[p][0] > ready[i] + 1e-9:
                    if p not in ops[i]["pre"]:
                        found.append((p, i))
                    p = prev[p]
                    if len(found) % 6 == 0:
                        break
                i = why[i]
        return found

    def settle(order):
        ca, edges, weight = cases[0]
        head, free, end, prev = [0.0] * N, {}, 0.0, [None] * N
        for i in order:
            t, p = 0.0, free.get(qs[i])
            if p is not None:
                t, prev[i] = head[p] + ca[p][0], p
            for j, d in edges[i]:
                if head[j] + d > t:
                    t = head[j] + d
            head[i] = t
            if qs[i] in ("V", "A", "G", "S"):
                free[qs[i]] = i
            end = max(end, t + ca[i][0] + ca[i][1])
        late = [end - ca[i][0] - ca[i][1] for i in range(N)]
        for i in reversed(order):
            for j, d in edges[i]:
                if late[i] - d < late[j]:
                    late[j] = late[i] - d
            p = prev[i]
            if p is not None and late[i] - ca[p][0] < late[p]:
                late[p] = late[i] - ca[p][0]
        pos = {i: p for p, i in enumerate(order)}
        return sorted(order, key=lambda i: (round(head[i] + C["alpha"] * (late[i] - head[i]), 6), pos[i]))

    def tried(seq, best):
        at = place(seq, fwd, [0.0] * N)
        order = sorted(range(N), key=lambda i: (at[i], i))
        if C["alpha"]:
            order = settle(order)
        span = length(order)
        return (span, order, at) if best is None or span <= best[0] else best

    name = repr((sorted((k, v) for k, v in C.items() if k not in ("span", "dbg")), sorted(PR.items())))
    if name not in KEPT:
        best = tried(seq, None)
        at = best[2]
        for it in range(1, C["iters"]):
            back = place(sorted(range(N), key=lambda i: (-at[i], -i)), bwd, [o["after"] for o in ops])
            best = tried(sorted(range(N), key=lambda i: (-back[i] - ops[i]["cost"], i)), best)
        find = {(o["tag"], o["round"]): i for i, o in enumerate(ops)}
        u, seen, now = C["seed"], None, best
        for it in range(C["polish"]):
            if seen is not now:
                seen, held = now, waiting_pairs(now[1])
            u = (u * 1103515245 + 12345) % 2 ** 31
            p0, i0 = held[(u >> 12) % len(held)]
            order, up = list(now[1]), (u >> 8) % 2
            for s in (range(-RO, RO) if (u >> 9) % 4 else (0,)):
                p, i = find.get((ops[p0]["tag"], ops[p0]["round"] + s)), find.get((ops[i0]["tag"], ops[i0]["round"] + s))
                if p is None or i is None:
                    continue
                a, b = order.index(p), order.index(i)
                if a > b:
                    continue
                seg, need = order[a:b + 1], {i if up else p}
                for x in (reversed(seg) if up else seg):
                    if not need.isdisjoint(ops[x]["post"] if up else ops[x]["pre"]):
                        need.add(x)
                if p not in need or i not in need:
                    order[a:b + 1] = [x for x in seg if (x in need) == up] + [x for x in seg if (x in need) != up]
            span = length(order)
            if span <= now[0] + C["heat"] * (1 - it / C["polish"]) * ((u >> 4) % 16) / 16:
                now = (span, order)
                if span < best[0]:
                    best = now
        KEPT[name] = best
    C["span"], order = KEPT[name][:2]
    known = {q: {} for q in Q}
    pos = {i: p for p, i in enumerate(order)}
    for i in order:
        o = ops[i]
        o["waits"], o["clock"] = [], {}
        if o["q"] is not None:
            kn = known[o["q"]]
            for j in sorted((j for j, w in o["pre"].items() if w), key=lambda j: -pos[j]):
                key = ops[j]["key"]
                if kn.get(key, -1) < pos[j]:
                    o["waits"].append(j)
                    ops[j]["sig"] = True
                    kn[key] = pos[j]
                    for k3, j3 in ops[j]["clock"].items():
                        if kn.get(k3, -1) < j3:
                            kn[k3] = j3
            o["clock"] = dict(kn)
    total = {}
    for i in order:
        o = ops[i]
        key = o["key"]
        for j in o["waits"]:
            Q[o["q"]].wait_ge(T.sem[ops[j]["key"]], ops[j]["val"])
        ins = o["fn"]() if o["fn"] else None
        if o["done"]:
            if key != "sent":
                total[key] = o["val"] = o["done"][1]
                if ins is not None:
                    ins.then_inc(T.sem[key], 16)
        elif o.get("sig"):
            total[key] = o["val"] = total.get(key, 0) + 1
            ins.then_inc(T.sem[key], 1)
    total["sent"] = nsent[0]
    for key, c in total.items():
        g.wait_ge(T.sem[key], c)
